import numpy as np
import ml_dtypes


def mxq(x, axis, fmt="e4m3"):
    dtype, down = {"e4m3": (ml_dtypes.float8_e4m3fn, 7), "e5m2": (ml_dtypes.float8_e5m2, 14)}[fmt]
    v = np.moveaxis(np.asarray(x, np.float32).astype(ml_dtypes.bfloat16).astype(np.float64), axis, -1)
    blocks = v.reshape(v.shape[:-1] + (-1, 32))
    amax = np.abs(blocks).max(-1, keepdims=True)
    byte = np.maximum(np.where(amax > 0, np.frexp(amax)[1] - 1 + 127, 0) - down, 1)
    scale = np.exp2(byte - 127.0)
    codes = (blocks / scale).astype(np.float32).astype(dtype).astype(np.float64)
    return np.moveaxis((codes * scale).reshape(v.shape), -1, axis)


WIDE = False


def mx_kscale(k):
    if not WIDE:
        return np.ones(k)
    levels = np.array([10, -10, 5, -5, 0])
    if k % 512:
        return np.exp2(np.random.permutation(np.resize(levels, k // 32))).repeat(32)
    a = np.empty((k // 512, 16))
    for p in range(k // 512):
        a[p, :8] = np.random.permutation(np.resize(levels, 8))
        for g in range(8):
            far = levels[np.abs(levels - a[p, g]) >= 10]
            a[p, g + 8] = far[np.random.randint(len(far))]
    return np.exp2(a.ravel()).repeat(32)


def f64(x):
    return np.asarray(x).astype(np.float64)


def striped(idx):
    return np.tile(idx.reshape(-1, 16).T, (8, 1)).astype(np.uint16)


def unstriped(offs):
    return offs[:16].T.reshape(-1).astype(np.int64)


E2M1 = np.array([0.0, 0.5, 1.0, 1.5, 2.0, 3.0, 4.0, 6.0, -0.0, -0.5, -1.0, -1.5, -2.0, -3.0, -4.0, -6.0])


def pack_weight(w, fmt):
    k, n = w.shape
    w = f64(np.asarray(w, np.float32).astype(ml_dtypes.bfloat16)).reshape(k // 32, 32, n)
    amax = np.abs(w).max(1)
    if fmt == "e4m3":
        byte = np.frexp(amax)[1] - 1 + 127 - 7
    else:
        mant, ex = np.frexp(amax / 6.0)
        byte = np.where(mant > 0.5, ex, ex - 1) + 127
    byte = np.clip(np.where(amax > 0, byte, 1), 1, 254)
    scaled = (w * np.exp2(127.0 - byte)[:, None, :]).reshape(k, n).astype(np.float32)
    by_word = np.ascontiguousarray(scaled.reshape(k // 512, 128, 4, n).transpose(0, 1, 3, 2))
    if fmt == "e4m3":
        words = by_word.astype(ml_dtypes.float8_e4m3fn).view(np.uint8)
    else:
        c = by_word.astype(ml_dtypes.float4_e2m1fn).view(np.uint8) & 0xF
        words = (c[..., 0::2] | (c[..., 1::2] << 4)).reshape(k // 512, 128, 2 * n)
    return np.ascontiguousarray(words), np.ascontiguousarray(byte.astype(np.uint8).reshape(k // 512, 16, n))


def unpack_weight(words, scales, fmt):
    g, _, n = scales.shape
    words = np.ascontiguousarray(words).reshape(g, 128, n, -1)
    if fmt == "e4m3":
        vals = words.view(ml_dtypes.float8_e4m3fn).astype(np.float64)
    else:
        nib = np.empty((g, 128, n, 4), np.uint8)
        nib[..., 0::2] = words & 0xF
        nib[..., 1::2] = words >> 4
        vals = E2M1[nib]
    vals = vals * np.repeat(np.exp2(scales.astype(np.float64) - 127.0), 8, axis=1)[..., None]
    return vals.transpose(0, 1, 3, 2).reshape(g * 512, n)


def gelu(v):
    return 0.5 * v * (1.0 + np.tanh(np.sqrt(2.0 / np.pi) * (v + 0.044715 * v**3)))


K, C, H, N, T, S = 1024, 512, 1024, 512, 2048, 1024

def setup_inputs():
    n = np.random.standard_normal
    sk = mx_kscale(K)[:, None]
    sc = mx_kscale(C)[:, None]
    u = mx_kscale(H)[:, None]
    tab_words, tab_scales = pack_weight(n((K, T)) * sk, "e4m3")
    tab2_words, tab2_scales = pack_weight(n((C, T)) * sc, "e4m3")
    a4_words, a4_scales = pack_weight(n((K, H)) / np.sqrt(K) / sk, "e2m1")
    b = (n((C, H)) / np.sqrt(C) / sc * u.T).astype(np.float32)
    w = (1.5 * n((H, N)) / np.sqrt(H) / u).astype(np.float32)
    gT = np.exp(0.3 * n((N, T))).astype(np.float32)
    offs = striped(np.random.permutation(T)[:S])
    offs2 = striped(np.random.permutation(T)[:S])
    return {"tab_words": tab_words, "tab_scales": tab_scales, "tab2_words": tab2_words, "tab2_scales": tab2_scales,
            "offs": offs, "offs2": offs2, "a4_words": a4_words, "a4_scales": a4_scales, "b": b, "w": w, "gT": gT}

def reference(tab_words, tab_scales, tab2_words, tab2_scales, offs, offs2, a4_words, a4_scales, b, w, gT):
    v = unpack_weight(tab_words, tab_scales, "e4m3")[:, unstriped(offs)]
    v2 = unpack_weight(tab2_words, tab2_scales, "e4m3")[:, unstriped(offs2)]
    a4 = unpack_weight(a4_words, a4_scales, "e2m1")
    p = a4.T @ v
    q = mxq(f64(b), 0, "e4m3").T @ v2
    h = np.log(1.0 + np.abs(p)) * q
    y = mxq(f64(w), 0, "e4m3").T @ mxq(h, 0, "e4m3")
    g = f64(gT)[:, unstriped(offs)]
    return y * g

@@ -1,0 +1,237 @@
+from contextlib import ExitStack
+
+import concourse.mybir as mybir
+
+K, C, H, N, T, S = 1024, 512, 1024, 512, 2048, 1024
+FLOPS = 2 * S * (K * H + C * H + H * N)
+
+F32 = mybir.dt.float32
+BF16 = mybir.dt.bfloat16
+I32 = mybir.dt.int32
+U32 = mybir.dt.uint32
+U16 = mybir.dt.uint16
+U8 = mybir.dt.uint8
+FP8X4 = mybir.dt.float8_e4m3fn_x4
+FP4X4 = mybir.dt.float4_e2m1fn_x4
+ACT = mybir.ActivationFunctionType
+MULT = mybir.AluOpType.mult
+ADD = mybir.AluOpType.add
+
+P = 128
+MOVE = True
+B_ENG = "ssssssss"
+W_ENG = "vvvvssss"
+CHUNKS = [512,256,256]
+SCALE_Q = ["sync","sync","sync"]
+
+
+def tile_list_ad_bid_scores_kernel(tc, tab_words, tab_scales, tab2_words, tab2_scales, offs, offs2, a4_words, a4_scales, b, w, gT, out):
+    nc = tc.nc
+    with ExitStack() as ctx:
+        keep = ctx.enter_context(tc.tile_pool(name="keep", bufs=1))
+        ring = ctx.enter_context(tc.tile_pool(name="ring", bufs=1))
+        psum = ctx.enter_context(tc.psum_pool(name="psum", bufs=1))
+        queues = {"sync": nc.sync, "scalar": nc.scalar, "gpsimd": nc.gpsimd}
+
+        def kt(shape, dtype, name):
+            return keep.tile(shape, dtype, name=name, align_bytes=64)
+
+        def big(shape, dtype, name):
+            return ring.tile(shape, dtype, name=name, tag="big", bufs=5, align_bytes=64)
+
+        idx = keep.tile([P, S // 16], U16, name="idx")
+        idx2 = keep.tile([P, S // 16], U16, name="idx2")
+        tab = [big([P, T], I32, "tab%d" % a) for a in range(2)]
+        braw = [big([P, 4, 512], F32, "braw0")]
+        tab2 = big([P, T], I32, "tab2")
+        braw.append(big([P, 4, 512], F32, "braw1"))
+        wraw = [big([P, 4, N], F32, "wraw%d" % A) for A in range(2)]
+        g = [big([P, T], F32, "g%d" % n) for n in range(4)]
+        if MOVE:
+            tsw = kt([P, T // 4], I32, "tsw")
+        else:
+            tsw = kt([P, 2, T // 4], I32, "tsw")
+        t2sw = kt([P, T // 4], I32, "t2sw")
+        v = [kt([P, S], I32, "v%d" % a) for a in range(2)]
+        vs = [kt([P, S // 4], I32, "vs%d" % a) for a in range(2)]
+        v2 = kt([P, S], I32, "v2")
+        v2s = kt([P, S // 4], I32, "v2s")
+        a4raw = kt([P, 2, H // 2], I32, "a4raw")
+        a4p = kt([P, 2 * H // 2], I32, "a4p")
+        a4sraw = kt([P, 2, H // 4], I32, "a4sraw")
+        a4sp = kt([P, 2 * H // 4], I32, "a4sp")
+        bbf = [kt([P, 2048], BF16, "bbf%d" % A) for A in range(2)]
+        bq = [kt([P, 512], I32, "bq%d" % A) for A in range(2)]
+        bs = [kt([P, 512], U8, "bs%d" % A) for A in range(2)]
+        wbf = [kt([P, 4 * N], BF16, "wbf%d" % A) for A in range(2)]
+        wq = [kt([P, N], I32, "wq%d" % A) for A in range(2)]
+        ws = [kt([P, N], U8, "ws%d" % A) for A in range(2)]
+        hq = [kt([P, S], I32, "hq%d" % A) for A in range(2)]
+        hs = [kt([P, S], U8, "hs%d" % A) for A in range(2)]
+        ysb = kt([P, 4, S], F32, "ysb")
+        osb = kt([P, 4, S], F32, "osb")
+        one = kt([P, 2], F32, "one")
+
+        if MOVE:
+            nc.vector.memset(tsw[:], 0)
+        else:
+            nc.vector.memset(tsw[:].rearrange("p a n -> p (a n)"), 0)
+        nc.gpsimd.memset(a4sraw[:].rearrange("p a n -> p (a n)"), 0)
+        nc.gpsimd.memset(t2sw[:], 0)
+        if MOVE:
+            nc.gpsimd.memset(vs[1][:], 0)
+        nc.vector.memset(one[:, 0:1], 1.0)
+
+        nc.sync.dma_start(idx[:], offs)
+        nc.sync.dma_start(idx2[:], offs2)
+        q0, q1, q2 = queues[SCALE_Q[0]], queues[SCALE_Q[1]], queues[SCALE_Q[2]]
+        for Q in range(4):
+            if MOVE:
+                q0.dma_start(out=tsw[32 * Q : 32 * Q + 8, :], in_=tab_scales[:, 4 * Q : 4 * Q + 4, :].bitcast(I32))
+            else:
+                q0.dma_start(out=tsw[32 * Q : 32 * Q + 4, :, :], in_=tab_scales[:, 4 * Q : 4 * Q + 4, :].rearrange("a r n -> r a n").bitcast(I32))
+        nc.sync.dma_start(out=tab[0][:], in_=tab_words[0].rearrange("p t i -> p (t i)").bitcast(I32))
+        nc.sync.dma_start(out=a4raw[:], in_=a4_words.rearrange("a p n -> p a n").bitcast(I32))
+        for Q in range(4):
+            q1.dma_start(out=a4sraw[32 * Q : 32 * Q + 4, :, :], in_=a4_scales[:, 4 * Q : 4 * Q + 4, :].rearrange("a r n -> r a n").bitcast(I32))
+        nc.sync.dma_start(out=tab[1][:], in_=tab_words[1].rearrange("p t i -> p (t i)").bitcast(I32))
+        nc.sync.dma_start(out=braw[0][:], in_=b[:, 0:512].rearrange("(p j) r -> p j r", j=4))
+        for Q in range(4):
+            q2.dma_start(out=t2sw[32 * Q : 32 * Q + 4, :], in_=tab2_scales[0, 4 * Q : 4 * Q + 4, :].bitcast(I32))
+        nc.scalar.activation(one[:, 1:2], one[:, 0:1], ACT.Ln)
+        nc.sync.dma_start(out=tab2[:], in_=tab2_words[0].rearrange("p t i -> p (t i)").bitcast(I32))
+        nc.sync.dma_start(out=braw[1][:], in_=b[:, 512:1024].rearrange("(p j) r -> p j r", j=4))
+        for A in range(2):
+            rows = w[512 * A : 512 * (A + 1), :].rearrange("(m t e) n -> e m t n", t=4, e=4)
+            for e in range(4):
+                nc.sync.dma_start(out=wraw[A][e:P:4, :, :], in_=rows[e])
+        for n in range(4):
+            nc.sync.dma_start(out=g[n][:], in_=gT[P * n : P * (n + 1), :])
+
+        def gather_words(dst, window, lst, j0, j1):
+            nc.vector.tensor_copy(dst[:, j0:j1].bitcast(U32), window[:].bitcast(U32).indirect(lst[:, j0 // 16 : j1 // 16]))
+
+        def gather_scales(dst, window, lst):
+            nc.vector.tensor_copy(dst[:].bitcast(U8), window.bitcast(U8).indirect(lst[:]))
+
+        def cast(eng, dst, src):
+            if eng == "s":
+                nc.scalar.copy(dst, src)
+            elif eng == "v":
+                nc.vector.tensor_copy(dst, src)
+            else:
+                nc.gpsimd.tensor_scalar(dst, src, 1.0, 0.0, MULT, ADD)
+
+        if MOVE:
+            gather_scales(vs[0], tsw[:], idx)
+            queues["scalar"].dma_start(out=vs[1][0:112, :], in_=vs[0][4:116, :])
+        else:
+            gather_scales(vs[0], tsw[:, 0, :], idx)
+            gather_scales(vs[1], tsw[:, 1, :], idx)
+        gather_words(v[0], tab[0], idx, 0, 1024)
+        nc.vector.tensor_copy(
+            a4p[:].rearrange("p (x t m e) -> p x t m e", x=4, t=4, e=2),
+            a4raw[:].rearrange("p a (x m t e) -> p (a x) t m e", x=2, t=4, e=2),
+        )
+        nc.vector.tensor_copy(
+            a4sp[:].rearrange("p (x t m) -> p x t m", x=4, t=4),
+            a4sraw[:].rearrange("p a (x m t) -> p (a x) t m", x=2, t=4),
+        )
+        for j0, j1 in ((0, 256), (256, 512), (512, 1024)):
+            gather_words(v[1], tab[1], idx, j0, j1)
+
+        def prep_b(A):
+            src = braw[A][:].rearrange("p j (m t e) -> p t m j e", t=4, e=4)
+            dst = bbf[A][:].rearrange("p (t m e j) -> p t m j e", t=4, e=4, j=4)
+            for t in range(4):
+                cast(B_ENG[4 * A + t], dst[:, t], src[:, t])
+            for u in range(2):
+                nc.vector.quantize_mx(out=bq[A][:, 256 * u : 256 * (u + 1)].bitcast(FP8X4), scales=bs[A][:, 256 * u : 256 * (u + 1)], in_=bbf[A][:, 1024 * u : 1024 * (u + 1)])
+
+        def prep_w(A):
+            src = wraw[A][:].rearrange("p t (u c i) -> p u c t i", u=4, i=4)
+            dst = wbf[A][:].rearrange("p (u c i t) -> p u c t i", u=4, i=4, t=4)
+            for u in range(4):
+                cast(W_ENG[4 * A + u], dst[:, u], src[:, u])
+            nc.vector.quantize_mx(out=wq[A][:].bitcast(FP8X4), scales=ws[A][:], in_=wbf[A][:])
+
+        prep_b(0)
+        gather_scales(v2s, t2sw[:], idx2)
+        for j0, j1 in ((0, 256), (256, 512), (512, 1024)):
+            gather_words(v2, tab2, idx2, j0, j1)
+        prep_b(1)
+
+        def unit(A, j0, hb, col):
+            pp = psum.tile([P, 4, P], F32, name="pp", bufs=3)
+            for t in range(4):
+                for a in range(2):
+                    o = (2 * a + A) * 4 + t
+                    nc.tensor.matmul_mx(
+                        out=pp[:, t, :],
+                        lhsT=a4p[:, 64 * o : 64 * (o + 1)].bitcast(FP4X4),
+                        lhsT_scale=a4sp[:, 32 * o : 32 * (o + 1)].bitcast(U8),
+                        rhs=v[a][:, j0 : j0 + P].bitcast(FP8X4),
+                        rhs_scale=vs[a][:, j0 // 4 : (j0 + P) // 4].bitcast(U8),
+                        start=(a == 0),
+                        stop=(a == 1),
+                    )
+            ab = ring.tile([P, P, 4], F32, name="ab", bufs=3)
+            nc.scalar.activation(ab[:], pp[:].rearrange("p t n -> p n t"), ACT.Abs)
+            lg = ring.tile([P, P, 4], F32, name="lg", bufs=10)
+            nc.scalar.activation(lg[:], ab[:], ACT.Ln, bias=1.0)
+            qq = psum.tile([P, 4, P], F32, name="qq", bufs=3)
+            for t in range(4):
+                nc.tensor.matmul_mx(
+                    out=qq[:, t, :],
+                    lhsT=bq[A][:, P * t : P * (t + 1)].bitcast(FP8X4),
+                    lhsT_scale=bs[A][:, P * t : P * (t + 1)],
+                    rhs=v2[:, j0 : j0 + P].bitcast(FP8X4),
+                    rhs_scale=v2s[:, j0 // 4 : (j0 + P) // 4].bitcast(U8),
+                    start=True,
+                    stop=True,
+                )
+            nc.vector.tensor_tensor(hb[:, col : col + P, :], qq[:].rearrange("p t n -> p n t"), lg[:], MULT)
+
+        def h_part(A, j0, width):
+            hb = ring.tile([P, 256, 4], BF16, name="hb", bufs=4, align_bytes=64)
+            for col in range(0, width, P):
+                unit(A, j0 + col, hb, col)
+            nc.vector.quantize_mx(out=hq[A][:, j0 : j0 + width].bitcast(FP8X4), scales=hs[A][:, j0 : j0 + width], in_=hb[:, 0:width, :].rearrange("p n t -> p (n t)"))
+
+        def scores(j0, width):
+            per = 512 // width
+            for n0 in range(0, 4, per):
+                yy = psum.tile([P, 512], F32, name="yy", bufs=2)
+                for i in range(per):
+                    n = n0 + i
+                    for A in range(2):
+                        nc.tensor.matmul_mx(
+                            out=yy[:, width * i : width * (i + 1)],
+                            lhsT=wq[A][:, P * n : P * (n + 1)].bitcast(FP8X4),
+                            lhsT_scale=ws[A][:, P * n : P * (n + 1)],
+                            rhs=hq[A][:, j0 : j0 + width].bitcast(FP8X4),
+                            rhs_scale=hs[A][:, j0 : j0 + width],
+                            start=(A == 0),
+                            stop=(A == 1),
+                        )
+                nc.scalar.copy(ysb[:, n0 : n0 + per, j0 : j0 + width], yy[:].rearrange("p (i n) -> p i n", i=per))
+
+        def bids(j0, width):
+            for n in range(4):
+                nc.vector.tensor_tensor(osb[:, n, j0 : j0 + width], g[n][:].indirect(idx[:, j0 // 16 : (j0 + width) // 16]), ysb[:, n, j0 : j0 + width], MULT)
+                nc.sync.dma_start(out=out[P * n : P * (n + 1), j0 : j0 + width], in_=osb[:, n, j0 : j0 + width])
+
+        j0 = 0
+        prev = None
+        for ci, width in enumerate(CHUNKS):
+            for A in range(2):
+                for s0 in range(0, width, 256):
+                    h_part(A, j0 + s0, min(256, width - s0))
+                if ci == 0:
+                    prep_w(A)
+            scores(j0, width)
+            if prev is not None:
+                bids(*prev)
+            prev = (j0, width)
+            j0 += width
+        bids(*prev)

@@ -19,8 +19,8 @@ ADD = mybir.AluOpType.add
 
 P = 128
 MOVE = True
-B_ENG = "ssssssss"
-W_ENG = "vvvvssss"
+B_ENG = "ssgggggg"
+W_ENG = "gggggggg"
 CHUNKS = [512,256,256]
 SCALE_Q = ["sync","sync","sync"]
 
@@ -37,11 +37,13 @@ def tile_list_ad_bid_scores_kernel(tc, tab_words, tab_scales, tab2_words, tab2_s
             return keep.tile(shape, dtype, name=name, align_bytes=64)
 
         def big(shape, dtype, name):
-            return ring.tile(shape, dtype, name=name, tag="big", bufs=5, align_bytes=64)
+            return ring.tile(shape, dtype, name=name, tag="big", bufs=4, align_bytes=64)
 
         idx = keep.tile([P, S // 16], U16, name="idx")
         idx2 = keep.tile([P, S // 16], U16, name="idx2")
-        tab = [big([P, T], I32, "tab%d" % a) for a in range(2)]
+        tab = [big([P, T], I32, "tab0")]
+        a4raw = big([P, 2, H // 2], I32, "a4raw")
+        tab.append(big([P, T], I32, "tab1"))
         braw = [big([P, 4, 512], F32, "braw0")]
         tab2 = big([P, T], I32, "tab2")
         braw.append(big([P, 4, 512], F32, "braw1"))
@@ -56,7 +58,6 @@ def tile_list_ad_bid_scores_kernel(tc, tab_words, tab_scales, tab2_words, tab2_s
         vs = [kt([P, S // 4], I32, "vs%d" % a) for a in range(2)]
         v2 = kt([P, S], I32, "v2")
         v2s = kt([P, S // 4], I32, "v2s")
-        a4raw = kt([P, 2, H // 2], I32, "a4raw")
         a4p = kt([P, 2 * H // 2], I32, "a4p")
         a4sraw = kt([P, 2, H // 4], I32, "a4sraw")
         a4sp = kt([P, 2 * H // 4], I32, "a4sp")
@@ -72,33 +73,28 @@ def tile_list_ad_bid_scores_kernel(tc, tab_words, tab_scales, tab2_words, tab2_s
         osb = kt([P, 4, S], F32, "osb")
         one = kt([P, 2], F32, "one")
 
-        if MOVE:
-            nc.vector.memset(tsw[:], 0)
-        else:
-            nc.vector.memset(tsw[:].rearrange("p a n -> p (a n)"), 0)
-        nc.gpsimd.memset(a4sraw[:].rearrange("p a n -> p (a n)"), 0)
-        nc.gpsimd.memset(t2sw[:], 0)
-        if MOVE:
-            nc.gpsimd.memset(vs[1][:], 0)
+        gs = kt([P, S // 4], I32, "gs")
+        for Q in range(4):
+            nc.gpsimd.memset(tsw[32 * Q : 32 * Q + 24, :], 0)
         nc.vector.memset(one[:, 0:1], 1.0)
+        nc.gpsimd.memset(t2sw[:], 0)
+        nc.vector.memset(vs[0][96:128, :], 0)
+        nc.vector.memset(vs[1][96:128, :], 0)
+        nc.vector.memset(a4sp[:], 0)
+        nc.scalar.activation(one[:, 1:2], one[:, 0:1], ACT.Ln)
 
         nc.sync.dma_start(idx[:], offs)
-        nc.sync.dma_start(idx2[:], offs2)
-        q0, q1, q2 = queues[SCALE_Q[0]], queues[SCALE_Q[1]], queues[SCALE_Q[2]]
         for Q in range(4):
-            if MOVE:
-                q0.dma_start(out=tsw[32 * Q : 32 * Q + 8, :], in_=tab_scales[:, 4 * Q : 4 * Q + 4, :].bitcast(I32))
-            else:
-                q0.dma_start(out=tsw[32 * Q : 32 * Q + 4, :, :], in_=tab_scales[:, 4 * Q : 4 * Q + 4, :].rearrange("a r n -> r a n").bitcast(I32))
+            nc.sync.dma_start(out=tsw[32 * Q + 24 : 32 * Q + 32, :], in_=tab_scales[:, 4 * Q : 4 * Q + 4, :].bitcast(I32))
         nc.sync.dma_start(out=tab[0][:], in_=tab_words[0].rearrange("p t i -> p (t i)").bitcast(I32))
         nc.sync.dma_start(out=a4raw[:], in_=a4_words.rearrange("a p n -> p a n").bitcast(I32))
+        nc.sync.dma_start(idx2[:], offs2)
         for Q in range(4):
-            q1.dma_start(out=a4sraw[32 * Q : 32 * Q + 4, :, :], in_=a4_scales[:, 4 * Q : 4 * Q + 4, :].rearrange("a r n -> r a n").bitcast(I32))
+            nc.sync.dma_start(out=a4sraw[32 * Q : 32 * Q + 4, :, :], in_=a4_scales[:, 4 * Q : 4 * Q + 4, :].rearrange("a r n -> r a n").bitcast(I32))
         nc.sync.dma_start(out=tab[1][:], in_=tab_words[1].rearrange("p t i -> p (t i)").bitcast(I32))
         nc.sync.dma_start(out=braw[0][:], in_=b[:, 0:512].rearrange("(p j) r -> p j r", j=4))
         for Q in range(4):
-            q2.dma_start(out=t2sw[32 * Q : 32 * Q + 4, :], in_=tab2_scales[0, 4 * Q : 4 * Q + 4, :].bitcast(I32))
-        nc.scalar.activation(one[:, 1:2], one[:, 0:1], ACT.Ln)
+            nc.sync.dma_start(out=t2sw[32 * Q : 32 * Q + 4, :], in_=tab2_scales[0, 4 * Q : 4 * Q + 4, :].bitcast(I32))
         nc.sync.dma_start(out=tab2[:], in_=tab2_words[0].rearrange("p t i -> p (t i)").bitcast(I32))
         nc.sync.dma_start(out=braw[1][:], in_=b[:, 512:1024].rearrange("(p j) r -> p j r", j=4))
         for A in range(2):
@@ -122,37 +118,49 @@ def tile_list_ad_bid_scores_kernel(tc, tab_words, tab_scales, tab2_words, tab2_s
             else:
                 nc.gpsimd.tensor_scalar(dst, src, 1.0, 0.0, MULT, ADD)
 
-        if MOVE:
-            gather_scales(vs[0], tsw[:], idx)
-            queues["scalar"].dma_start(out=vs[1][0:112, :], in_=vs[0][4:116, :])
-        else:
-            gather_scales(vs[0], tsw[:, 0, :], idx)
-            gather_scales(vs[1], tsw[:, 1, :], idx)
-        gather_words(v[0], tab[0], idx, 0, 1024)
+        gather_scales(gs, tsw[:], idx)
+        nc.scalar.dma_start(out=vs[0][0:104, :], in_=gs[24:128, :])
+        nc.scalar.dma_start(out=vs[1][0:100, :], in_=gs[28:128, :])
+        cuts = ((0, 256), (256, 512), (512, 1024))
+        gather_words(v[0], tab[0], idx, *cuts[0])
         nc.vector.tensor_copy(
             a4p[:].rearrange("p (x t m e) -> p x t m e", x=4, t=4, e=2),
             a4raw[:].rearrange("p a (x m t e) -> p (a x) t m e", x=2, t=4, e=2),
         )
-        nc.vector.tensor_copy(
-            a4sp[:].rearrange("p (x t m) -> p x t m", x=4, t=4),
-            a4sraw[:].rearrange("p a (x m t) -> p (a x) t m", x=2, t=4),
-        )
-        for j0, j1 in ((0, 256), (256, 512), (512, 1024)):
-            gather_words(v[1], tab[1], idx, j0, j1)
+        for Q in range(4):
+            nc.vector.tensor_copy(
+                a4sp[32 * Q : 32 * Q + 4, :].rearrange("p (x t m) -> p x m t", x=4, t=4),
+                a4sraw[32 * Q : 32 * Q + 4, :, :].rearrange("p a (x m t) -> p (a x) m t", x=2, t=4),
+            )
+        gather_words(v[1], tab[1], idx, *cuts[0])
+        for cut in cuts[1:]:
+            gather_words(v[0], tab[0], idx, *cut)
+        for cut in cuts[1:]:
+            gather_words(v[1], tab[1], idx, *cut)
 
         def prep_b(A):
             src = braw[A][:].rearrange("p j (m t e) -> p t m j e", t=4, e=4)
             dst = bbf[A][:].rearrange("p (t m e j) -> p t m j e", t=4, e=4, j=4)
+            src_g = braw[A][:].rearrange("p j (m t e) -> p t m e j", t=4, e=4)
+            dst_g = bbf[A][:].rearrange("p (t m e j) -> p t m e j", t=4, e=4, j=4)
             for t in range(4):
-                cast(B_ENG[4 * A + t], dst[:, t], src[:, t])
+                if B_ENG[4 * A + t] == "g":
+                    cast("g", dst_g[:, t], src_g[:, t])
+                else:
+                    cast(B_ENG[4 * A + t], dst[:, t], src[:, t])
             for u in range(2):
                 nc.vector.quantize_mx(out=bq[A][:, 256 * u : 256 * (u + 1)].bitcast(FP8X4), scales=bs[A][:, 256 * u : 256 * (u + 1)], in_=bbf[A][:, 1024 * u : 1024 * (u + 1)])
 
         def prep_w(A):
             src = wraw[A][:].rearrange("p t (u c i) -> p u c t i", u=4, i=4)
             dst = wbf[A][:].rearrange("p (u c i t) -> p u c t i", u=4, i=4, t=4)
+            src_g = wraw[A][:].rearrange("p t (u c) -> p u c t", u=4)
+            dst_g = wbf[A][:].rearrange("p (u c t) -> p u c t", u=4, t=4)
             for u in range(4):
-                cast(W_ENG[4 * A + u], dst[:, u], src[:, u])
+                if W_ENG[4 * A + u] == "g":
+                    cast("g", dst_g[:, u], src_g[:, u])
+                else:
+                    cast(W_ENG[4 * A + u], dst[:, u], src[:, u])
             nc.vector.quantize_mx(out=wq[A][:].bitcast(FP8X4), scales=ws[A][:], in_=wbf[A][:])
 
         prep_b(0)
@@ -177,7 +185,7 @@ def tile_list_ad_bid_scores_kernel(tc, tab_words, tab_scales, tab2_words, tab2_s
                     )
             ab = ring.tile([P, P, 4], F32, name="ab", bufs=3)
             nc.scalar.activation(ab[:], pp[:].rearrange("p t n -> p n t"), ACT.Abs)
-            lg = ring.tile([P, P, 4], F32, name="lg", bufs=10)
+            lg = ring.tile([P, P, 4], F32, name="lg", bufs=4)
             nc.scalar.activation(lg[:], ab[:], ACT.Ln, bias=1.0)
             qq = psum.tile([P, 4, P], F32, name="qq", bufs=3)
             for t in range(4):

@@ -44,8 +44,8 @@ def tile_list_ad_bid_scores_kernel(tc, tab_words, tab_scales, tab2_words, tab2_s
         tab = [big([P, T], I32, "tab0")]
         a4raw = big([P, 2, H // 2], I32, "a4raw")
         tab.append(big([P, T], I32, "tab1"))
-        braw = [big([P, 4, 512], F32, "braw0")]
         tab2 = big([P, T], I32, "tab2")
+        braw = [big([P, 4, 512], F32, "braw0")]
         braw.append(big([P, 4, 512], F32, "braw1"))
         wraw = [big([P, 4, N], F32, "wraw%d" % A) for A in range(2)]
         g = [big([P, T], F32, "g%d" % n) for n in range(4)]
@@ -76,8 +76,8 @@ def tile_list_ad_bid_scores_kernel(tc, tab_words, tab_scales, tab2_words, tab2_s
         gs = kt([P, S // 4], I32, "gs")
         for Q in range(4):
             nc.gpsimd.memset(tsw[32 * Q : 32 * Q + 24, :], 0)
+        nc.vector.memset(t2sw[:], 0)
         nc.vector.memset(one[:, 0:1], 1.0)
-        nc.gpsimd.memset(t2sw[:], 0)
         nc.vector.memset(vs[0][96:128, :], 0)
         nc.vector.memset(vs[1][96:128, :], 0)
         nc.vector.memset(a4sp[:], 0)
@@ -92,10 +92,10 @@ def tile_list_ad_bid_scores_kernel(tc, tab_words, tab_scales, tab2_words, tab2_s
         for Q in range(4):
             nc.sync.dma_start(out=a4sraw[32 * Q : 32 * Q + 4, :, :], in_=a4_scales[:, 4 * Q : 4 * Q + 4, :].rearrange("a r n -> r a n").bitcast(I32))
         nc.sync.dma_start(out=tab[1][:], in_=tab_words[1].rearrange("p t i -> p (t i)").bitcast(I32))
-        nc.sync.dma_start(out=braw[0][:], in_=b[:, 0:512].rearrange("(p j) r -> p j r", j=4))
         for Q in range(4):
             nc.sync.dma_start(out=t2sw[32 * Q : 32 * Q + 4, :], in_=tab2_scales[0, 4 * Q : 4 * Q + 4, :].bitcast(I32))
         nc.sync.dma_start(out=tab2[:], in_=tab2_words[0].rearrange("p t i -> p (t i)").bitcast(I32))
+        nc.sync.dma_start(out=braw[0][:], in_=b[:, 0:512].rearrange("(p j) r -> p j r", j=4))
         nc.sync.dma_start(out=braw[1][:], in_=b[:, 512:1024].rearrange("(p j) r -> p j r", j=4))
         for A in range(2):
             rows = w[512 * A : 512 * (A + 1), :].rearrange("(m t e) n -> e m t n", t=4, e=4)
@@ -121,8 +121,8 @@ def tile_list_ad_bid_scores_kernel(tc, tab_words, tab_scales, tab2_words, tab2_s
         gather_scales(gs, tsw[:], idx)
         nc.scalar.dma_start(out=vs[0][0:104, :], in_=gs[24:128, :])
         nc.scalar.dma_start(out=vs[1][0:100, :], in_=gs[28:128, :])
-        cuts = ((0, 256), (256, 512), (512, 1024))
-        gather_words(v[0], tab[0], idx, *cuts[0])
+        cuts = ((0, 256), (256, 1024))
+        gather_words(v[0], tab[0], idx, 0, S)
         nc.vector.tensor_copy(
             a4p[:].rearrange("p (x t m e) -> p x t m e", x=4, t=4, e=2),
             a4raw[:].rearrange("p a (x m t e) -> p (a x) t m e", x=2, t=4, e=2),
@@ -133,8 +133,6 @@ def tile_list_ad_bid_scores_kernel(tc, tab_words, tab_scales, tab2_words, tab2_s
                 a4sraw[32 * Q : 32 * Q + 4, :, :].rearrange("p a (x m t) -> p (a x) m t", x=2, t=4),
             )
         gather_words(v[1], tab[1], idx, *cuts[0])
-        for cut in cuts[1:]:
-            gather_words(v[0], tab[0], idx, *cut)
         for cut in cuts[1:]:
             gather_words(v[1], tab[1], idx, *cut)
 
@@ -148,25 +146,24 @@ def tile_list_ad_bid_scores_kernel(tc, tab_words, tab_scales, tab2_words, tab2_s
                     cast("g", dst_g[:, t], src_g[:, t])
                 else:
                     cast(B_ENG[4 * A + t], dst[:, t], src[:, t])
+
+        def quant_b(A):
             for u in range(2):
                 nc.vector.quantize_mx(out=bq[A][:, 256 * u : 256 * (u + 1)].bitcast(FP8X4), scales=bs[A][:, 256 * u : 256 * (u + 1)], in_=bbf[A][:, 1024 * u : 1024 * (u + 1)])
 
-        def prep_w(A):
-            src = wraw[A][:].rearrange("p t (u c i) -> p u c t i", u=4, i=4)
-            dst = wbf[A][:].rearrange("p (u c i t) -> p u c t i", u=4, i=4, t=4)
-            src_g = wraw[A][:].rearrange("p t (u c) -> p u c t", u=4)
-            dst_g = wbf[A][:].rearrange("p (u c t) -> p u c t", u=4, t=4)
+        def cast_w(A):
+            src = wraw[A][:].rearrange("p t (u c) -> p u c t", u=4)
+            dst = wbf[A][:].rearrange("p (u c t) -> p u c t", u=4, t=4)
             for u in range(4):
-                if W_ENG[4 * A + u] == "g":
-                    cast("g", dst_g[:, u], src_g[:, u])
-                else:
-                    cast(W_ENG[4 * A + u], dst[:, u], src[:, u])
+                cast("g", dst[:, u], src[:, u])
+
+        def quant_w(A):
             nc.vector.quantize_mx(out=wq[A][:].bitcast(FP8X4), scales=ws[A][:], in_=wbf[A][:])
 
         prep_b(0)
         gather_scales(v2s, t2sw[:], idx2)
-        for j0, j1 in ((0, 256), (256, 512), (512, 1024)):
-            gather_words(v2, tab2, idx2, j0, j1)
+        gather_words(v2, tab2, idx2, 0, S)
+        quant_b(0)
         prep_b(1)
 
         def unit(A, j0, hb, col):
@@ -185,7 +182,7 @@ def tile_list_ad_bid_scores_kernel(tc, tab_words, tab_scales, tab2_words, tab2_s
                     )
             ab = ring.tile([P, P, 4], F32, name="ab", bufs=3)
             nc.scalar.activation(ab[:], pp[:].rearrange("p t n -> p n t"), ACT.Abs)
-            lg = ring.tile([P, P, 4], F32, name="lg", bufs=4)
+            lg = ring.tile([P, P, 4], F32, name="lg", bufs=16)
             nc.scalar.activation(lg[:], ab[:], ACT.Ln, bias=1.0)
             qq = psum.tile([P, 4, P], F32, name="qq", bufs=3)
             for t in range(4):
@@ -200,10 +197,7 @@ def tile_list_ad_bid_scores_kernel(tc, tab_words, tab_scales, tab2_words, tab2_s
                 )
             nc.vector.tensor_tensor(hb[:, col : col + P, :], qq[:].rearrange("p t n -> p n t"), lg[:], MULT)
 
-        def h_part(A, j0, width):
-            hb = ring.tile([P, 256, 4], BF16, name="hb", bufs=4, align_bytes=64)
-            for col in range(0, width, P):
-                unit(A, j0 + col, hb, col)
+        def quant_h(A, j0, width, hb):
             nc.vector.quantize_mx(out=hq[A][:, j0 : j0 + width].bitcast(FP8X4), scales=hs[A][:, j0 : j0 + width], in_=hb[:, 0:width, :].rearrange("p n t -> p (n t)"))
 
         def scores(j0, width):
@@ -224,22 +218,41 @@ def tile_list_ad_bid_scores_kernel(tc, tab_words, tab_scales, tab2_words, tab2_s
                         )
                 nc.scalar.copy(ysb[:, n0 : n0 + per, j0 : j0 + width], yy[:].rearrange("p (i n) -> p i n", i=per))
 
-        def bids(j0, width):
-            for n in range(4):
+        def bids(j0, width, tiles):
+            for n in tiles:
                 nc.vector.tensor_tensor(osb[:, n, j0 : j0 + width], g[n][:].indirect(idx[:, j0 // 16 : (j0 + width) // 16]), ysb[:, n, j0 : j0 + width], MULT)
                 nc.sync.dma_start(out=out[P * n : P * (n + 1), j0 : j0 + width], in_=osb[:, n, j0 : j0 + width])
 
-        j0 = 0
-        prev = None
-        for ci, width in enumerate(CHUNKS):
-            for A in range(2):
-                for s0 in range(0, width, 256):
-                    h_part(A, j0 + s0, min(256, width - s0))
-                if ci == 0:
-                    prep_w(A)
-            scores(j0, width)
-            if prev is not None:
-                bids(*prev)
-            prev = (j0, width)
-            j0 += width
-        bids(*prev)
+        cast_w(0)
+        cast_w(1)
+        QW = 512
+        pending = None
+        count = 0
+        for A in range(2):
+            for half in range(2):
+                for s0 in range(0, 512, QW):
+                    j0 = 512 * half + s0
+                    hb = ring.tile([P, QW, 4], BF16, name="hb", bufs=3, align_bytes=64)
+                    for col in range(0, QW, P):
+                        unit(A, j0 + col, hb, col)
+                        count += 1
+                        if pending is not None:
+                            quant_h(*pending)
+                            pending = None
+                        if count == 6:
+                            quant_b(1)
+                        if count == 12:
+                            quant_w(0)
+                        if count == 13:
+                            quant_w(1)
+                            scores(0, 512)
+                        if count == 15:
+                            bids(0, 512, (0,))
+                    pending = (A, j0, QW, hb)
+        bids(0, 512, (1,))
+        quant_h(*pending)
+        scores(512, 512)
+        bids(0, 512, (2, 3))
+        bids(512, 512, (0, 1, 2))
+        bids(512, 256, (3,))
+        bids(768, 256, (3,))

@@ -19,7 +19,7 @@ ADD = mybir.AluOpType.add
 
 P = 128
 MOVE = True
-B_ENG = "ssgggggg"
+B_ENG = "svvvgggg"
 W_ENG = "gggggggg"
 CHUNKS = [512,256,256]
 SCALE_Q = ["sync","sync","sync"]
@@ -92,9 +92,9 @@ def tile_list_ad_bid_scores_kernel(tc, tab_words, tab_scales, tab2_words, tab2_s
         for Q in range(4):
             nc.sync.dma_start(out=a4sraw[32 * Q : 32 * Q + 4, :, :], in_=a4_scales[:, 4 * Q : 4 * Q + 4, :].rearrange("a r n -> r a n").bitcast(I32))
         nc.sync.dma_start(out=tab[1][:], in_=tab_words[1].rearrange("p t i -> p (t i)").bitcast(I32))
+        nc.sync.dma_start(out=tab2[:], in_=tab2_words[0].rearrange("p t i -> p (t i)").bitcast(I32))
         for Q in range(4):
             nc.sync.dma_start(out=t2sw[32 * Q : 32 * Q + 4, :], in_=tab2_scales[0, 4 * Q : 4 * Q + 4, :].bitcast(I32))
-        nc.sync.dma_start(out=tab2[:], in_=tab2_words[0].rearrange("p t i -> p (t i)").bitcast(I32))
         nc.sync.dma_start(out=braw[0][:], in_=b[:, 0:512].rearrange("(p j) r -> p j r", j=4))
         nc.sync.dma_start(out=braw[1][:], in_=b[:, 512:1024].rearrange("(p j) r -> p j r", j=4))
         for A in range(2):
@@ -122,7 +122,7 @@ def tile_list_ad_bid_scores_kernel(tc, tab_words, tab_scales, tab2_words, tab2_s
         nc.scalar.dma_start(out=vs[0][0:104, :], in_=gs[24:128, :])
         nc.scalar.dma_start(out=vs[1][0:100, :], in_=gs[28:128, :])
         cuts = ((0, 256), (256, 1024))
-        gather_words(v[0], tab[0], idx, 0, S)
+        gather_words(v[0], tab[0], idx, 0, 256)
         nc.vector.tensor_copy(
             a4p[:].rearrange("p (x t m e) -> p x t m e", x=4, t=4, e=2),
             a4raw[:].rearrange("p a (x m t e) -> p (a x) t m e", x=2, t=4, e=2),
@@ -132,9 +132,11 @@ def tile_list_ad_bid_scores_kernel(tc, tab_words, tab_scales, tab2_words, tab2_s
                 a4sp[32 * Q : 32 * Q + 4, :].rearrange("p (x t m) -> p x m t", x=4, t=4),
                 a4sraw[32 * Q : 32 * Q + 4, :, :].rearrange("p a (x m t) -> p (a x) m t", x=2, t=4),
             )
-        gather_words(v[1], tab[1], idx, *cuts[0])
-        for cut in cuts[1:]:
-            gather_words(v[1], tab[1], idx, *cut)
+        gather_words(v[0], tab[0], idx, 256, 512)
+        gather_words(v[1], tab[1], idx, 0, 256)
+        gather_words(v[1], tab[1], idx, 256, 512)
+        gather_words(v[0], tab[0], idx, 512, S)
+        gather_words(v[1], tab[1], idx, 512, S)
 
         def prep_b(A):
             src = braw[A][:].rearrange("p j (m t e) -> p t m j e", t=4, e=4)
@@ -148,8 +150,7 @@ def tile_list_ad_bid_scores_kernel(tc, tab_words, tab_scales, tab2_words, tab2_s
                     cast(B_ENG[4 * A + t], dst[:, t], src[:, t])
 
         def quant_b(A):
-            for u in range(2):
-                nc.vector.quantize_mx(out=bq[A][:, 256 * u : 256 * (u + 1)].bitcast(FP8X4), scales=bs[A][:, 256 * u : 256 * (u + 1)], in_=bbf[A][:, 1024 * u : 1024 * (u + 1)])
+            nc.vector.quantize_mx(out=bq[A][:].bitcast(FP8X4), scales=bs[A][:], in_=bbf[A][:])
 
         def cast_w(A):
             src = wraw[A][:].rearrange("p t (u c) -> p u c t", u=4)
@@ -160,14 +161,16 @@ def tile_list_ad_bid_scores_kernel(tc, tab_words, tab_scales, tab2_words, tab2_s
         def quant_w(A):
             nc.vector.quantize_mx(out=wq[A][:].bitcast(FP8X4), scales=ws[A][:], in_=wbf[A][:])
 
+        gather_words(v2, tab2, idx2, 0, S)
         prep_b(0)
         gather_scales(v2s, t2sw[:], idx2)
-        gather_words(v2, tab2, idx2, 0, S)
         quant_b(0)
         prep_b(1)
 
-        def unit(A, j0, hb, col):
-            pp = psum.tile([P, 4, P], F32, name="pp", bufs=3)
+        banks = [psum.tile([P, 512], F32, name="bank%d" % i) for i in range(8)]
+
+        def magnitude(A, j0, ab, bank):
+            pp = bank[:].rearrange("p (t n) -> p t n", t=4)
             for t in range(4):
                 for a in range(2):
                     o = (2 * a + A) * 4 + t
@@ -180,11 +183,10 @@ def tile_list_ad_bid_scores_kernel(tc, tab_words, tab_scales, tab2_words, tab2_s
                         start=(a == 0),
                         stop=(a == 1),
                     )
-            ab = ring.tile([P, P, 4], F32, name="ab", bufs=3)
-            nc.scalar.activation(ab[:], pp[:].rearrange("p t n -> p n t"), ACT.Abs)
-            lg = ring.tile([P, P, 4], F32, name="lg", bufs=16)
-            nc.scalar.activation(lg[:], ab[:], ACT.Ln, bias=1.0)
-            qq = psum.tile([P, 4, P], F32, name="qq", bufs=3)
+            nc.scalar.activation(ab.rearrange("p (n t) -> p n t", t=4), pp.rearrange("p t n -> p n t"), ACT.Abs)
+
+        def gate(A, j0, lg, hb, bank):
+            qq = bank[:].rearrange("p (t n) -> p t n", t=4)
             for t in range(4):
                 nc.tensor.matmul_mx(
                     out=qq[:, t, :],
@@ -195,15 +197,15 @@ def tile_list_ad_bid_scores_kernel(tc, tab_words, tab_scales, tab2_words, tab2_s
                     start=True,
                     stop=True,
                 )
-            nc.vector.tensor_tensor(hb[:, col : col + P, :], qq[:].rearrange("p t n -> p n t"), lg[:], MULT)
+            nc.vector.tensor_tensor(hb, qq.rearrange("p t n -> p n t"), lg.rearrange("p (n t) -> p n t", t=4), MULT)
 
-        def quant_h(A, j0, width, hb):
-            nc.vector.quantize_mx(out=hq[A][:, j0 : j0 + width].bitcast(FP8X4), scales=hs[A][:, j0 : j0 + width], in_=hb[:, 0:width, :].rearrange("p n t -> p (n t)"))
+        def quant_h(A, j0, width):
+            nc.vector.quantize_mx(out=hq[A][:, j0 : j0 + width].bitcast(FP8X4), scales=hs[A][:, j0 : j0 + width], in_=hb[A][:, j0 : j0 + width, :].rearrange("p n t -> p (n t)"))
 
         def scores(j0, width):
             per = 512 // width
             for n0 in range(0, 4, per):
-                yy = psum.tile([P, 512], F32, name="yy", bufs=2)
+                yy = banks[(6, 7, 0, 1, 2)[(n0 + j0 // 128) % 5]]
                 for i in range(per):
                     n = n0 + i
                     for A in range(2):
@@ -225,34 +227,36 @@ def tile_list_ad_bid_scores_kernel(tc, tab_words, tab_scales, tab2_words, tab2_s
 
         cast_w(0)
         cast_w(1)
-        QW = 512
-        pending = None
-        count = 0
-        for A in range(2):
-            for half in range(2):
-                for s0 in range(0, 512, QW):
-                    j0 = 512 * half + s0
-                    hb = ring.tile([P, QW, 4], BF16, name="hb", bufs=3, align_bytes=64)
-                    for col in range(0, QW, P):
-                        unit(A, j0 + col, hb, col)
-                        count += 1
-                        if pending is not None:
-                            quant_h(*pending)
-                            pending = None
-                        if count == 6:
-                            quant_b(1)
-                        if count == 12:
-                            quant_w(0)
-                        if count == 13:
-                            quant_w(1)
-                            scores(0, 512)
-                        if count == 15:
-                            bids(0, 512, (0,))
-                    pending = (A, j0, QW, hb)
-        bids(0, 512, (1,))
-        quant_h(*pending)
+        units = [(A, j0) for A in range(2) for j0 in range(0, S, P)]
+        abs_all = kt([P, 6, 512], F32, "abs_all")
+        log_all = kt([P, 16, 512], F32, "log_all")
+        hb = [kt([P, S, 4], BF16, "hb%d" % A) for A in range(2)]
+        groups = [(u, u + 2) for u in range(0, 14, 2)] + [(14, 15), (15, 16)]
+        made = 0
+        for first, last in groups:
+            while made < min(last + 1, 16):
+                magnitude(*units[made], abs_all[:, made % 6, :], banks[(0, 1, 2, 3, 4, 5, 6, 7, 0, 1, 2, 6, 7, 0, 1, 2)[made]])
+                made += 1
+            nc.scalar.activation(log_all[:, first:last, :], abs_all[:, first % 6 : first % 6 + last - first, :], ACT.Ln, bias=1.0)
+        if True:
+            for u in range(16):
+                A, j0 = units[u]
+                gate(A, j0, log_all[:, u, :], hb[A][:, j0 : j0 + P, :], banks[3 + u % 3])
+                if u % 4 == 0 and u > 0:
+                    pA, pj = units[u - 4]
+                    quant_h(pA, pj, 512)
+                if u == 5:
+                    quant_b(1)
+                if u == 10:
+                    quant_w(0)
+                if u == 13:
+                    quant_w(1)
+                if u == 14:
+                    quant_h(1, 512, 256)
+        scores(0, 512)
+        quant_h(1, 768, 256)
         scores(512, 512)
-        bids(0, 512, (2, 3))
+        bids(0, 512, (0, 1, 2, 3))
         bids(512, 512, (0, 1, 2))
         bids(512, 256, (3,))
         bids(768, 256, (3,))

@@ -19,7 +19,7 @@ ADD = mybir.AluOpType.add
 
 P = 128
 MOVE = True
-B_ENG = "svvvgggg"
+B_ENG = "svvvvvvv"
 W_ENG = "gggggggg"
 CHUNKS = [512,256,256]
 SCALE_Q = ["sync","sync","sync"]
@@ -152,11 +152,11 @@ def tile_list_ad_bid_scores_kernel(tc, tab_words, tab_scales, tab2_words, tab2_s
         def quant_b(A):
             nc.vector.quantize_mx(out=bq[A][:].bitcast(FP8X4), scales=bs[A][:], in_=bbf[A][:])
 
-        def cast_w(A):
-            src = wraw[A][:].rearrange("p t (u c) -> p u c t", u=4)
-            dst = wbf[A][:].rearrange("p (u c t) -> p u c t", u=4, t=4)
-            for u in range(4):
-                cast("g", dst[:, u], src[:, u])
+        def cast_w(eng, A, parts):
+            src = wraw[A][:].rearrange("p t (u c i) -> p u c t i", u=4, i=4)
+            dst = wbf[A][:].rearrange("p (u c i t) -> p u c t i", u=4, i=4, t=4)
+            for u in parts:
+                cast(eng, dst[:, u], src[:, u])
 
         def quant_w(A):
             nc.vector.quantize_mx(out=wq[A][:].bitcast(FP8X4), scales=ws[A][:], in_=wbf[A][:])
@@ -165,7 +165,6 @@ def tile_list_ad_bid_scores_kernel(tc, tab_words, tab_scales, tab2_words, tab2_s
         prep_b(0)
         gather_scales(v2s, t2sw[:], idx2)
         quant_b(0)
-        prep_b(1)
 
         banks = [psum.tile([P, 512], F32, name="bank%d" % i) for i in range(8)]
 
@@ -225,8 +224,6 @@ def tile_list_ad_bid_scores_kernel(tc, tab_words, tab_scales, tab2_words, tab2_s
                 nc.vector.tensor_tensor(osb[:, n, j0 : j0 + width], g[n][:].indirect(idx[:, j0 // 16 : (j0 + width) // 16]), ysb[:, n, j0 : j0 + width], MULT)
                 nc.sync.dma_start(out=out[P * n : P * (n + 1), j0 : j0 + width], in_=osb[:, n, j0 : j0 + width])
 
-        cast_w(0)
-        cast_w(1)
         units = [(A, j0) for A in range(2) for j0 in range(0, S, P)]
         abs_all = kt([P, 6, 512], F32, "abs_all")
         log_all = kt([P, 16, 512], F32, "log_all")
@@ -238,6 +235,10 @@ def tile_list_ad_bid_scores_kernel(tc, tab_words, tab_scales, tab2_words, tab2_s
                 magnitude(*units[made], abs_all[:, made % 6, :], banks[(0, 1, 2, 3, 4, 5, 6, 7, 0, 1, 2, 6, 7, 0, 1, 2)[made]])
                 made += 1
             nc.scalar.activation(log_all[:, first:last, :], abs_all[:, first % 6 : first % 6 + last - first, :], ACT.Ln, bias=1.0)
+            if first == 8:
+                cast_w("s", 0, (0, 1, 2, 3))
+            if first == 10:
+                cast_w("s", 1, (0, 1))
         if True:
             for u in range(16):
                 A, j0 = units[u]
@@ -245,9 +246,13 @@ def tile_list_ad_bid_scores_kernel(tc, tab_words, tab_scales, tab2_words, tab2_s
                 if u % 4 == 0 and u > 0:
                     pA, pj = units[u - 4]
                     quant_h(pA, pj, 512)
+                if u == 3:
+                    prep_b(1)
+                if u == 9:
+                    cast_w("v", 1, (2, 3))
                 if u == 5:
                     quant_b(1)
-                if u == 10:
+                if u == 11:
                     quant_w(0)
                 if u == 13:
                     quant_w(1)

@@ -15,53 +15,33 @@ FP8X4 = mybir.dt.float8_e4m3fn_x4
 FP4X4 = mybir.dt.float4_e2m1fn_x4
 ACT = mybir.ActivationFunctionType
 MULT = mybir.AluOpType.mult
-ADD = mybir.AluOpType.add
 
 P = 128
-MOVE = True
-B_ENG = "svvvvvvv"
-W_ENG = "gggggggg"
-CHUNKS = [512,256,256]
-SCALE_Q = ["sync","sync","sync"]
 
 
 def tile_list_ad_bid_scores_kernel(tc, tab_words, tab_scales, tab2_words, tab2_scales, offs, offs2, a4_words, a4_scales, b, w, gT, out):
     nc = tc.nc
     with ExitStack() as ctx:
         keep = ctx.enter_context(tc.tile_pool(name="keep", bufs=1))
-        ring = ctx.enter_context(tc.tile_pool(name="ring", bufs=1))
+        share = ctx.enter_context(tc.tile_pool(name="share", bufs=1))
         psum = ctx.enter_context(tc.psum_pool(name="psum", bufs=1))
-        queues = {"sync": nc.sync, "scalar": nc.scalar, "gpsimd": nc.gpsimd}
 
         def kt(shape, dtype, name):
             return keep.tile(shape, dtype, name=name, align_bytes=64)
 
-        def big(shape, dtype, name):
-            return ring.tile(shape, dtype, name=name, tag="big", bufs=4, align_bytes=64)
+        def st(slot, shape, dtype, name):
+            return share.tile(shape, dtype, name=name, tag="slot%d" % slot, bufs=1, align_bytes=64)
 
         idx = keep.tile([P, S // 16], U16, name="idx")
         idx2 = keep.tile([P, S // 16], U16, name="idx2")
-        tab = [big([P, T], I32, "tab0")]
-        a4raw = big([P, 2, H // 2], I32, "a4raw")
-        tab.append(big([P, T], I32, "tab1"))
-        tab2 = big([P, T], I32, "tab2")
-        braw = [big([P, 4, 512], F32, "braw0")]
-        braw.append(big([P, 4, 512], F32, "braw1"))
-        wraw = [big([P, 4, N], F32, "wraw%d" % A) for A in range(2)]
-        g = [big([P, T], F32, "g%d" % n) for n in range(4)]
-        if MOVE:
-            tsw = kt([P, T // 4], I32, "tsw")
-        else:
-            tsw = kt([P, 2, T // 4], I32, "tsw")
-        t2sw = kt([P, T // 4], I32, "t2sw")
+        tsw = kt([P, T // 4], I32, "tsw")
+        gs = kt([P, S // 4], I32, "gs")
         v = [kt([P, S], I32, "v%d" % a) for a in range(2)]
         vs = [kt([P, S // 4], I32, "vs%d" % a) for a in range(2)]
         v2 = kt([P, S], I32, "v2")
         v2s = kt([P, S // 4], I32, "v2s")
-        a4p = kt([P, 2 * H // 2], I32, "a4p")
-        a4sraw = kt([P, 2, H // 4], I32, "a4sraw")
+        a4p = kt([P, H], I32, "a4p")
         a4sp = kt([P, 2 * H // 4], I32, "a4sp")
-        bbf = [kt([P, 2048], BF16, "bbf%d" % A) for A in range(2)]
         bq = [kt([P, 512], I32, "bq%d" % A) for A in range(2)]
         bs = [kt([P, 512], U8, "bs%d" % A) for A in range(2)]
         wbf = [kt([P, 4 * N], BF16, "wbf%d" % A) for A in range(2)]
@@ -69,102 +49,111 @@ def tile_list_ad_bid_scores_kernel(tc, tab_words, tab_scales, tab2_words, tab2_s
         ws = [kt([P, N], U8, "ws%d" % A) for A in range(2)]
         hq = [kt([P, S], I32, "hq%d" % A) for A in range(2)]
         hs = [kt([P, S], U8, "hs%d" % A) for A in range(2)]
-        ysb = kt([P, 4, S], F32, "ysb")
-        osb = kt([P, 4, S], F32, "osb")
+        hb = [kt([P, S, 4], BF16, "hb%d" % A) for A in range(2)]
         one = kt([P, 2], F32, "one")
 
-        gs = kt([P, S // 4], I32, "gs")
-        for Q in range(4):
-            nc.gpsimd.memset(tsw[32 * Q : 32 * Q + 24, :], 0)
-        nc.vector.memset(t2sw[:], 0)
-        nc.vector.memset(one[:, 0:1], 1.0)
-        nc.vector.memset(vs[0][96:128, :], 0)
-        nc.vector.memset(vs[1][96:128, :], 0)
+        tab0 = st(0, [P, T], I32, "tab0")
+        a4raw = st(1, [P, 2, H // 2], I32, "a4raw")
+        a4sraw = kt([P, 2 * H // 4], I32, "a4sraw")
+        tab1 = st(2, [P, T], I32, "tab1")
+        t2sw = st(3, [P, T // 4], I32, "t2sw")
+        tab2 = st(0, [P, T], I32, "tab2")
+        abs_pair = [st(10 + i % 3, [P, 2, 512], F32, "abs%d" % i) for i in range(8)]
+        ysb = [st(10 + (8 + c) % 3, [P, 4, 256], F32, "ysb%d" % c) for c in range(3)] + [kt([P, 4, 256], F32, "ysb3")]
+        log_pair = [st(20 + i, [P, 2, 512], F32, "log%d" % i) for i in range(8)]
+        bbf = [st(4 + A, [P, 2048], BF16, "bbf%d" % A) for A in range(2)]
+        braw = [st(1 + A, [P, 4, 512], F32, "braw%d" % A) for A in range(2)]
+        wraw = [st(6, [P, 4, N], F32, "wraw0"), st(0, [P, 4, N], F32, "wraw1")]
+        g = [st(slot, [P, T], F32, "g%d" % n) for n, slot in enumerate((3, 1, 4, 2))]
+
         nc.vector.memset(a4sp[:], 0)
+        nc.vector.memset(tsw[0:16, :], 0)
+        nc.vector.memset(tsw[32:48, :], 0)
+        nc.vector.memset(tsw[64:128, :], 0)
+        nc.gpsimd.memset(t2sw[:], 0)
+        nc.gpsimd.memset(one[:, 0:1], 1.0)
         nc.scalar.activation(one[:, 1:2], one[:, 0:1], ACT.Ln)
 
+        for Q in range(4):
+            nc.sync.dma_start(
+                out=a4sraw[32 * Q : 32 * Q + 4, :].rearrange("p (a n) -> p a n", a=2),
+                in_=a4_scales[:, 4 * Q : 4 * Q + 4, :].rearrange("a r n -> r a n").bitcast(I32),
+            )
         nc.sync.dma_start(idx[:], offs)
-        for Q in range(4):
-            nc.sync.dma_start(out=tsw[32 * Q + 24 : 32 * Q + 32, :], in_=tab_scales[:, 4 * Q : 4 * Q + 4, :].bitcast(I32))
-        nc.sync.dma_start(out=tab[0][:], in_=tab_words[0].rearrange("p t i -> p (t i)").bitcast(I32))
+        rows = tab_scales.rearrange("a (u h r) n -> h (a u) r n", u=2, h=2)
+        for h in range(2):
+            nc.sync.dma_start(out=tsw[32 * h + 16 : 32 * h + 32, :], in_=rows[h].bitcast(I32))
+        nc.sync.dma_start(out=tab0[:], in_=tab_words[0].rearrange("p t i -> p (t i)").bitcast(I32))
         nc.sync.dma_start(out=a4raw[:], in_=a4_words.rearrange("a p n -> p a n").bitcast(I32))
+        nc.sync.dma_start(out=tab1[:], in_=tab_words[1].rearrange("p t i -> p (t i)").bitcast(I32))
         nc.sync.dma_start(idx2[:], offs2)
-        for Q in range(4):
-            nc.sync.dma_start(out=a4sraw[32 * Q : 32 * Q + 4, :, :], in_=a4_scales[:, 4 * Q : 4 * Q + 4, :].rearrange("a r n -> r a n").bitcast(I32))
-        nc.sync.dma_start(out=tab[1][:], in_=tab_words[1].rearrange("p t i -> p (t i)").bitcast(I32))
-        nc.sync.dma_start(out=tab2[:], in_=tab2_words[0].rearrange("p t i -> p (t i)").bitcast(I32))
-        for Q in range(4):
-            nc.sync.dma_start(out=t2sw[32 * Q : 32 * Q + 4, :], in_=tab2_scales[0, 4 * Q : 4 * Q + 4, :].bitcast(I32))
-        nc.sync.dma_start(out=braw[0][:], in_=b[:, 0:512].rearrange("(p j) r -> p j r", j=4))
-        nc.sync.dma_start(out=braw[1][:], in_=b[:, 512:1024].rearrange("(p j) r -> p j r", j=4))
-        for A in range(2):
-            rows = w[512 * A : 512 * (A + 1), :].rearrange("(m t e) n -> e m t n", t=4, e=4)
-            for e in range(4):
-                nc.sync.dma_start(out=wraw[A][e:P:4, :, :], in_=rows[e])
-        for n in range(4):
-            nc.sync.dma_start(out=g[n][:], in_=gT[P * n : P * (n + 1), :])
 
         def gather_words(dst, window, lst, j0, j1):
             nc.vector.tensor_copy(dst[:, j0:j1].bitcast(U32), window[:].bitcast(U32).indirect(lst[:, j0 // 16 : j1 // 16]))
 
         def gather_scales(dst, window, lst):
-            nc.vector.tensor_copy(dst[:].bitcast(U8), window.bitcast(U8).indirect(lst[:]))
+            nc.vector.tensor_copy(dst[:].bitcast(U8), window[:].bitcast(U8).indirect(lst[:]))
 
-        def cast(eng, dst, src):
-            if eng == "s":
-                nc.scalar.copy(dst, src)
-            elif eng == "v":
-                nc.vector.tensor_copy(dst, src)
-            else:
-                nc.gpsimd.tensor_scalar(dst, src, 1.0, 0.0, MULT, ADD)
-
-        gather_scales(gs, tsw[:], idx)
-        nc.scalar.dma_start(out=vs[0][0:104, :], in_=gs[24:128, :])
-        nc.scalar.dma_start(out=vs[1][0:100, :], in_=gs[28:128, :])
-        cuts = ((0, 256), (256, 1024))
-        gather_words(v[0], tab[0], idx, 0, 256)
+        for Q in range(4):
+            nc.vector.tensor_copy(
+                a4sp[32 * Q : 32 * Q + 4, :].rearrange("p (x t m) -> p x m t", x=4, t=4),
+                a4sraw[32 * Q : 32 * Q + 4, :].rearrange("p (x m t) -> p x m t", x=4, t=4),
+            )
+        gather_scales(gs, tsw, idx)
+        for u in range(2):
+            for a in range(2):
+                first = 16 + 4 * (2 * a + u)
+                nc.scalar.dma_start(out=vs[a][64 * u : 64 * (u + 1), :], in_=gs[first : first + 64, :])
+        gather_words(v[0], tab0, idx, 0, S)
+        nc.sync.dma_start(out=tab2[:], in_=tab2_words[0].rearrange("p t i -> p (t i)").bitcast(I32))
+        for Q in range(4):
+            nc.sync.dma_start(out=t2sw[32 * Q : 32 * Q + 4, :], in_=tab2_scales[0, 4 * Q : 4 * Q + 4, :].bitcast(I32))
         nc.vector.tensor_copy(
             a4p[:].rearrange("p (x t m e) -> p x t m e", x=4, t=4, e=2),
             a4raw[:].rearrange("p a (x m t e) -> p (a x) t m e", x=2, t=4, e=2),
         )
-        for Q in range(4):
-            nc.vector.tensor_copy(
-                a4sp[32 * Q : 32 * Q + 4, :].rearrange("p (x t m) -> p x m t", x=4, t=4),
-                a4sraw[32 * Q : 32 * Q + 4, :, :].rearrange("p a (x m t) -> p (a x) m t", x=2, t=4),
-            )
-        gather_words(v[0], tab[0], idx, 256, 512)
-        gather_words(v[1], tab[1], idx, 0, 256)
-        gather_words(v[1], tab[1], idx, 256, 512)
-        gather_words(v[0], tab[0], idx, 512, S)
-        gather_words(v[1], tab[1], idx, 512, S)
+        nc.sync.dma_start(out=braw[0][:], in_=b[:, 0:512].rearrange("(p j) r -> p j r", j=4))
+        gather_words(v[1], tab1, idx, 0, 256)
+        gather_words(v[1], tab1, idx, 256, S)
+        nc.sync.dma_start(out=braw[1][:], in_=b[:, 512:1024].rearrange("(p j) r -> p j r", j=4))
 
-        def prep_b(A):
+        def load_w(A):
+            wrows = w[512 * A : 512 * (A + 1), :].rearrange("(m t e) n -> t m e n", t=4, e=4)
+            for t in range(4):
+                nc.sync.dma_start(out=wraw[A][:, t, :], in_=wrows[t])
+
+        def load_g(n):
+            nc.sync.dma_start(out=g[n][:], in_=gT[P * n : P * (n + 1), :])
+
+        def cast(eng, dst, src):
+            if eng == "s":
+                nc.scalar.copy(dst, src)
+            else:
+                nc.vector.tensor_copy(dst, src)
+
+        def cast_b(A, engines):
             src = braw[A][:].rearrange("p j (m t e) -> p t m j e", t=4, e=4)
             dst = bbf[A][:].rearrange("p (t m e j) -> p t m j e", t=4, e=4, j=4)
-            src_g = braw[A][:].rearrange("p j (m t e) -> p t m e j", t=4, e=4)
-            dst_g = bbf[A][:].rearrange("p (t m e j) -> p t m e j", t=4, e=4, j=4)
-            for t in range(4):
-                if B_ENG[4 * A + t] == "g":
-                    cast("g", dst_g[:, t], src_g[:, t])
-                else:
-                    cast(B_ENG[4 * A + t], dst[:, t], src[:, t])
+            for half in range(2):
+                cast(engines[half], dst[:, 2 * half : 2 * half + 2], src[:, 2 * half : 2 * half + 2])
 
         def quant_b(A):
             nc.vector.quantize_mx(out=bq[A][:].bitcast(FP8X4), scales=bs[A][:], in_=bbf[A][:])
 
-        def cast_w(eng, A, parts):
+        def cast_w(A, engines):
             src = wraw[A][:].rearrange("p t (u c i) -> p u c t i", u=4, i=4)
             dst = wbf[A][:].rearrange("p (u c i t) -> p u c t i", u=4, i=4, t=4)
-            for u in parts:
-                cast(eng, dst[:, u], src[:, u])
+            for half in range(2):
+                cast(engines[half], dst[:, 2 * half : 2 * half + 2], src[:, 2 * half : 2 * half + 2])
 
         def quant_w(A):
             nc.vector.quantize_mx(out=wq[A][:].bitcast(FP8X4), scales=ws[A][:], in_=wbf[A][:])
 
         gather_words(v2, tab2, idx2, 0, S)
-        prep_b(0)
-        gather_scales(v2s, t2sw[:], idx2)
-        quant_b(0)
+        load_w(0)
+        load_w(1)
+        gather_scales(v2s, t2sw, idx2)
+        load_g(0)
 
         banks = [psum.tile([P, 512], F32, name="bank%d" % i) for i in range(8)]
 
@@ -184,8 +173,9 @@ def tile_list_ad_bid_scores_kernel(tc, tab_words, tab_scales, tab2_words, tab2_s
                     )
             nc.scalar.activation(ab.rearrange("p (n t) -> p n t", t=4), pp.rearrange("p t n -> p n t"), ACT.Abs)
 
-        def gate(A, j0, lg, hb, bank):
-            qq = bank[:].rearrange("p (t n) -> p t n", t=4)
+        def gate(u):
+            A, j0 = u % 2, P * (u // 2)
+            qq = banks[5 + u if u < 3 else (u - 3) % 3][:].rearrange("p (t n) -> p t n", t=4)
             for t in range(4):
                 nc.tensor.matmul_mx(
                     out=qq[:, t, :],
@@ -196,72 +186,109 @@ def tile_list_ad_bid_scores_kernel(tc, tab_words, tab_scales, tab2_words, tab2_s
                     start=True,
                     stop=True,
                 )
-            nc.vector.tensor_tensor(hb, qq.rearrange("p t n -> p n t"), lg.rearrange("p (n t) -> p n t", t=4), MULT)
+            nc.vector.tensor_tensor(hb[A][:, j0 : j0 + P, :], qq.rearrange("p t n -> p n t"), log_pair[u // 2][:, u % 2, :].rearrange("p (n t) -> p n t", t=4), MULT)
 
         def quant_h(A, j0, width):
             nc.vector.quantize_mx(out=hq[A][:, j0 : j0 + width].bitcast(FP8X4), scales=hs[A][:, j0 : j0 + width], in_=hb[A][:, j0 : j0 + width, :].rearrange("p n t -> p (n t)"))
 
-        def scores(j0, width):
-            per = 512 // width
-            for n0 in range(0, 4, per):
-                yy = banks[(6, 7, 0, 1, 2)[(n0 + j0 // 128) % 5]]
-                for i in range(per):
-                    n = n0 + i
-                    for A in range(2):
-                        nc.tensor.matmul_mx(
-                            out=yy[:, width * i : width * (i + 1)],
-                            lhsT=wq[A][:, P * n : P * (n + 1)].bitcast(FP8X4),
-                            lhsT_scale=ws[A][:, P * n : P * (n + 1)],
-                            rhs=hq[A][:, j0 : j0 + width].bitcast(FP8X4),
-                            rhs_scale=hs[A][:, j0 : j0 + width],
-                            start=(A == 0),
-                            stop=(A == 1),
-                        )
-                nc.scalar.copy(ysb[:, n0 : n0 + per, j0 : j0 + width], yy[:].rearrange("p (i n) -> p i n", i=per))
+        ring = [16]
 
-        def bids(j0, width, tiles):
-            for n in tiles:
-                nc.vector.tensor_tensor(osb[:, n, j0 : j0 + width], g[n][:].indirect(idx[:, j0 // 16 : (j0 + width) // 16]), ysb[:, n, j0 : j0 + width], MULT)
-                nc.sync.dma_start(out=out[P * n : P * (n + 1), j0 : j0 + width], in_=osb[:, n, j0 : j0 + width])
+        def next_bank():
+            ring[0] = ring[0] + 1
+            return banks[3 + (ring[0] - 1) % 2]
 
-        units = [(A, j0) for A in range(2) for j0 in range(0, S, P)]
-        abs_all = kt([P, 6, 512], F32, "abs_all")
-        log_all = kt([P, 16, 512], F32, "log_all")
-        hb = [kt([P, S, 4], BF16, "hb%d" % A) for A in range(2)]
-        groups = [(u, u + 2) for u in range(0, 14, 2)] + [(14, 15), (15, 16)]
-        made = 0
-        for first, last in groups:
-            while made < min(last + 1, 16):
-                magnitude(*units[made], abs_all[:, made % 6, :], banks[(0, 1, 2, 3, 4, 5, 6, 7, 0, 1, 2, 6, 7, 0, 1, 2)[made]])
-                made += 1
-            nc.scalar.activation(log_all[:, first:last, :], abs_all[:, first % 6 : first % 6 + last - first, :], ACT.Ln, bias=1.0)
-            if first == 8:
-                cast_w("s", 0, (0, 1, 2, 3))
-            if first == 10:
-                cast_w("s", 1, (0, 1))
-        if True:
-            for u in range(16):
-                A, j0 = units[u]
-                gate(A, j0, log_all[:, u, :], hb[A][:, j0 : j0 + P, :], banks[3 + u % 3])
-                if u % 4 == 0 and u > 0:
-                    pA, pj = units[u - 4]
-                    quant_h(pA, pj, 512)
-                if u == 3:
-                    prep_b(1)
-                if u == 9:
-                    cast_w("v", 1, (2, 3))
-                if u == 5:
-                    quant_b(1)
-                if u == 11:
-                    quant_w(0)
-                if u == 13:
-                    quant_w(1)
-                if u == 14:
-                    quant_h(1, 512, 256)
-        scores(0, 512)
+        def products(yy, n, j0, width):
+            for A in range(2):
+                nc.tensor.matmul_mx(
+                    out=yy,
+                    lhsT=wq[A][:, P * n : P * (n + 1)].bitcast(FP8X4),
+                    lhsT_scale=ws[A][:, P * n : P * (n + 1)],
+                    rhs=hq[A][:, j0 : j0 + width].bitcast(FP8X4),
+                    rhs_scale=hs[A][:, j0 : j0 + width],
+                    start=(A == 0),
+                    stop=(A == 1),
+                )
+
+
+        def scores(j0):
+            for pair in range(2):
+                yy = next_bank()[:].rearrange("p (i n) -> p i n", i=2)
+                for i in range(2):
+                    products(yy[:, i, :], 2 * pair + i, j0, 256)
+                nc.scalar.copy(ysb[j0 // 256][:, 2 * pair : 2 * pair + 2, :], yy)
+
+        def bids(c, pairs, slot):
+            for pair in pairs:
+                osb = st(slot + pair, [P, 2, 256], F32, "osb%d_%d" % (c, pair))
+                for i in range(2):
+                    n = 2 * pair + i
+                    nc.vector.tensor_tensor(osb[:, i, :], g[n][:].indirect(idx[:, 16 * c : 16 * (c + 1)]), ysb[c][:, n, :], MULT)
+                nc.sync.dma_start(out=out[2 * P * pair : 2 * P * (pair + 1), 256 * c : 256 * (c + 1)].rearrange("(i p) j -> p i j", i=2), in_=osb[:])
+
+        def magnitudes(first, last):
+            for u in range(first, last):
+                A, j0 = u % 2, P * (u // 2)
+                magnitude(A, j0, abs_pair[u // 2][:, u % 2, :], banks[u % 5 if u < 10 else 5 + (u - 10) % 3])
+
+        def logs(pair):
+            nc.scalar.activation(log_pair[pair][:], abs_pair[pair][:], ACT.Ln, bias=1.0)
+
+        magnitudes(0, 3)
+        logs(0)
+        cast_b(0, "vv")
+        load_g(1)
+        quant_b(0)
+        load_g(2)
+        magnitudes(3, 5)
+        logs(1)
+        cast_b(1, "vv")
+        load_g(3)
+        magnitudes(5, 7)
+        logs(2)
+        gate(0)
+        quant_b(1)
+        gate(2)
+        gate(1)
+        gate(3)
+        magnitudes(7, 9)
+        logs(3)
+        quant_h(0, 0, 256)
+        quant_h(1, 0, 256)
+        gate(4)
+        gate(5)
+        gate(6)
+        gate(7)
+        magnitudes(9, 11)
+        logs(4)
+        cast_w(0, "sv")
+        cast_w(1, "ss")
+        quant_h(0, 256, 256)
+        quant_h(1, 256, 256)
+        gate(8)
+        gate(9)
+        quant_w(0)
+        quant_w(1)
+        magnitudes(11, 13)
+        logs(5)
+        scores(0)
+        gate(10)
+        gate(11)
+        magnitudes(13, 15)
+        logs(6)
+        scores(256)
+        quant_h(0, 512, 256)
+        quant_h(1, 512, 256)
+        gate(12)
+        gate(13)
+        magnitudes(15, 16)
+        logs(7)
+        scores(512)
+        gate(14)
+        gate(15)
+        quant_h(0, 768, 256)
         quant_h(1, 768, 256)
-        scores(512, 512)
-        bids(0, 512, (0, 1, 2, 3))
-        bids(512, 512, (0, 1, 2))
-        bids(512, 256, (3,))
-        bids(768, 256, (3,))
+        scores(768)
+        bids(0, (0, 1), 30)
+        bids(1, (0, 1), 32)
+        bids(2, (0, 1), 34)
+        bids(3, (0, 1), 36)

@@ -47,9 +47,9 @@ def tile_list_ad_bid_scores_kernel(tc, tab_words, tab_scales, tab2_words, tab2_s
         wbf = [kt([P, 4 * N], BF16, "wbf%d" % A) for A in range(2)]
         wq = [kt([P, N], I32, "wq%d" % A) for A in range(2)]
         ws = [kt([P, N], U8, "ws%d" % A) for A in range(2)]
-        hq = [kt([P, S], I32, "hq%d" % A) for A in range(2)]
-        hs = [kt([P, S], U8, "hs%d" % A) for A in range(2)]
-        hb = [kt([P, S, 4], BF16, "hb%d" % A) for A in range(2)]
+        hq = [kt([P, 2, 256], I32, "hq%d" % c) for c in range(4)]
+        hs = [kt([P, 2, 256], U8, "hs%d" % c) for c in range(4)]
+        hb = [kt([P, 2, 256, 4], BF16, "hb%d" % c) for c in range(4)]
         one = kt([P, 2], F32, "one")
 
         tab0 = st(0, [P, T], I32, "tab0")
@@ -57,32 +57,32 @@ def tile_list_ad_bid_scores_kernel(tc, tab_words, tab_scales, tab2_words, tab2_s
         a4sraw = kt([P, 2 * H // 4], I32, "a4sraw")
         tab1 = st(2, [P, T], I32, "tab1")
         t2sw = st(3, [P, T // 4], I32, "t2sw")
-        tab2 = st(0, [P, T], I32, "tab2")
+        tab2 = st(6, [P, T], I32, "tab2")
         abs_pair = [st(10 + i % 3, [P, 2, 512], F32, "abs%d" % i) for i in range(8)]
         ysb = [st(10 + (8 + c) % 3, [P, 4, 256], F32, "ysb%d" % c) for c in range(3)] + [kt([P, 4, 256], F32, "ysb3")]
         log_pair = [st(20 + i, [P, 2, 512], F32, "log%d" % i) for i in range(8)]
         bbf = [st(4 + A, [P, 2048], BF16, "bbf%d" % A) for A in range(2)]
-        braw = [st(1 + A, [P, 4, 512], F32, "braw%d" % A) for A in range(2)]
-        wraw = [st(6, [P, 4, N], F32, "wraw0"), st(0, [P, 4, N], F32, "wraw1")]
-        g = [st(slot, [P, T], F32, "g%d" % n) for n, slot in enumerate((3, 1, 4, 2))]
+        braw = [st(A, [P, 4, 512], F32, "braw%d" % A) for A in range(2)]
+        wraw = [st(2, [P, 4, N], F32, "wraw0"), st(6, [P, 4, N], F32, "wraw1")]
+        g = [st(slot, [P, T], F32, "g%d" % n) for n, slot in enumerate((3, 0, 4, 1))]
 
-        nc.vector.memset(a4sp[:], 0)
         nc.vector.memset(tsw[0:16, :], 0)
         nc.vector.memset(tsw[32:48, :], 0)
         nc.vector.memset(tsw[64:128, :], 0)
-        nc.gpsimd.memset(t2sw[:], 0)
+        nc.gpsimd.memset(a4sraw[:], 0)
         nc.gpsimd.memset(one[:, 0:1], 1.0)
+        nc.vector.memset(t2sw[:], 0)
         nc.scalar.activation(one[:, 1:2], one[:, 0:1], ACT.Ln)
 
+        nc.sync.dma_start(idx[:], offs)
+        rows = tab_scales.rearrange("a (u h r) n -> h (a u) r n", u=2, h=2)
+        for h in range(2):
+            nc.sync.dma_start(out=tsw[32 * h + 16 : 32 * h + 32, :], in_=rows[h].bitcast(I32))
         for Q in range(4):
             nc.sync.dma_start(
                 out=a4sraw[32 * Q : 32 * Q + 4, :].rearrange("p (a n) -> p a n", a=2),
                 in_=a4_scales[:, 4 * Q : 4 * Q + 4, :].rearrange("a r n -> r a n").bitcast(I32),
             )
-        nc.sync.dma_start(idx[:], offs)
-        rows = tab_scales.rearrange("a (u h r) n -> h (a u) r n", u=2, h=2)
-        for h in range(2):
-            nc.sync.dma_start(out=tsw[32 * h + 16 : 32 * h + 32, :], in_=rows[h].bitcast(I32))
         nc.sync.dma_start(out=tab0[:], in_=tab_words[0].rearrange("p t i -> p (t i)").bitcast(I32))
         nc.sync.dma_start(out=a4raw[:], in_=a4_words.rearrange("a p n -> p a n").bitcast(I32))
         nc.sync.dma_start(out=tab1[:], in_=tab_words[1].rearrange("p t i -> p (t i)").bitcast(I32))
@@ -94,16 +94,15 @@ def tile_list_ad_bid_scores_kernel(tc, tab_words, tab_scales, tab2_words, tab2_s
         def gather_scales(dst, window, lst):
             nc.vector.tensor_copy(dst[:].bitcast(U8), window[:].bitcast(U8).indirect(lst[:]))
 
-        for Q in range(4):
-            nc.vector.tensor_copy(
-                a4sp[32 * Q : 32 * Q + 4, :].rearrange("p (x t m) -> p x m t", x=4, t=4),
-                a4sraw[32 * Q : 32 * Q + 4, :].rearrange("p (x m t) -> p x m t", x=4, t=4),
-            )
         gather_scales(gs, tsw, idx)
         for u in range(2):
             for a in range(2):
                 first = 16 + 4 * (2 * a + u)
                 nc.scalar.dma_start(out=vs[a][64 * u : 64 * (u + 1), :], in_=gs[first : first + 64, :])
+        nc.vector.tensor_copy(
+            a4sp[:].rearrange("p (x t m) -> p x m t", x=4, t=4),
+            a4sraw[:].rearrange("p (x m t) -> p x m t", x=4, t=4),
+        )
         gather_words(v[0], tab0, idx, 0, S)
         nc.sync.dma_start(out=tab2[:], in_=tab2_words[0].rearrange("p t i -> p (t i)").bitcast(I32))
         for Q in range(4):
@@ -175,7 +174,7 @@ def tile_list_ad_bid_scores_kernel(tc, tab_words, tab_scales, tab2_words, tab2_s
 
         def gate(u):
             A, j0 = u % 2, P * (u // 2)
-            qq = banks[5 + u if u < 3 else (u - 3) % 3][:].rearrange("p (t n) -> p t n", t=4)
+            qq = banks[u % 8][:].rearrange("p (t n) -> p t n", t=4)
             for t in range(4):
                 nc.tensor.matmul_mx(
                     out=qq[:, t, :],
@@ -186,16 +185,14 @@ def tile_list_ad_bid_scores_kernel(tc, tab_words, tab_scales, tab2_words, tab2_s
                     start=True,
                     stop=True,
                 )
-            nc.vector.tensor_tensor(hb[A][:, j0 : j0 + P, :], qq.rearrange("p t n -> p n t"), log_pair[u // 2][:, u % 2, :].rearrange("p (n t) -> p n t", t=4), MULT)
+            nc.vector.tensor_tensor(hb[j0 // 256][:, A, j0 % 256 : j0 % 256 + P, :], qq.rearrange("p t n -> p n t"), log_pair[u // 2][:, u % 2, :].rearrange("p (n t) -> p n t", t=4), MULT)
 
-        def quant_h(A, j0, width):
-            nc.vector.quantize_mx(out=hq[A][:, j0 : j0 + width].bitcast(FP8X4), scales=hs[A][:, j0 : j0 + width], in_=hb[A][:, j0 : j0 + width, :].rearrange("p n t -> p (n t)"))
-
-        ring = [16]
-
-        def next_bank():
-            ring[0] = ring[0] + 1
-            return banks[3 + (ring[0] - 1) % 2]
+        def quant_h(c):
+            nc.vector.quantize_mx(
+                out=hq[c][:].rearrange("p a n -> p (a n)").bitcast(FP8X4),
+                scales=hs[c][:].rearrange("p a n -> p (a n)"),
+                in_=hb[c][:].rearrange("p a n t -> p (a n t)"),
+            )
 
         def products(yy, n, j0, width):
             for A in range(2):
@@ -203,8 +200,8 @@ def tile_list_ad_bid_scores_kernel(tc, tab_words, tab_scales, tab2_words, tab2_s
                     out=yy,
                     lhsT=wq[A][:, P * n : P * (n + 1)].bitcast(FP8X4),
                     lhsT_scale=ws[A][:, P * n : P * (n + 1)],
-                    rhs=hq[A][:, j0 : j0 + width].bitcast(FP8X4),
-                    rhs_scale=hs[A][:, j0 : j0 + width],
+                    rhs=hq[j0 // 256][:, A, :].bitcast(FP8X4),
+                    rhs_scale=hs[j0 // 256][:, A, :],
                     start=(A == 0),
                     stop=(A == 1),
                 )
@@ -212,7 +209,7 @@ def tile_list_ad_bid_scores_kernel(tc, tab_words, tab_scales, tab2_words, tab2_s
 
         def scores(j0):
             for pair in range(2):
-                yy = next_bank()[:].rearrange("p (i n) -> p i n", i=2)
+                yy = banks[j0 // P + pair][:].rearrange("p (i n) -> p i n", i=2)
                 for i in range(2):
                     products(yy[:, i, :], 2 * pair + i, j0, 256)
                 nc.scalar.copy(ysb[j0 // 256][:, 2 * pair : 2 * pair + 2, :], yy)
@@ -223,12 +220,15 @@ def tile_list_ad_bid_scores_kernel(tc, tab_words, tab_scales, tab2_words, tab2_s
                 for i in range(2):
                     n = 2 * pair + i
                     nc.vector.tensor_tensor(osb[:, i, :], g[n][:].indirect(idx[:, 16 * c : 16 * (c + 1)]), ysb[c][:, n, :], MULT)
-                nc.sync.dma_start(out=out[2 * P * pair : 2 * P * (pair + 1), 256 * c : 256 * (c + 1)].rearrange("(i p) j -> p i j", i=2), in_=osb[:])
+                    if c == 3:
+                        nc.sync.dma_start(out=out[P * n : P * (n + 1), 256 * c : 256 * (c + 1)], in_=osb[:, i, :])
+                if c < 3:
+                    nc.sync.dma_start(out=out[2 * P * pair : 2 * P * (pair + 1), 256 * c : 256 * (c + 1)].rearrange("(i p) j -> p i j", i=2), in_=osb[:])
 
         def magnitudes(first, last):
             for u in range(first, last):
                 A, j0 = u % 2, P * (u // 2)
-                magnitude(A, j0, abs_pair[u // 2][:, u % 2, :], banks[u % 5 if u < 10 else 5 + (u - 10) % 3])
+                magnitude(A, j0, abs_pair[u // 2][:, u % 2, :], banks[u % 8])
 
         def logs(pair):
             nc.scalar.activation(log_pair[pair][:], abs_pair[pair][:], ACT.Ln, bias=1.0)
@@ -252,8 +252,7 @@ def tile_list_ad_bid_scores_kernel(tc, tab_words, tab_scales, tab2_words, tab2_s
         gate(3)
         magnitudes(7, 9)
         logs(3)
-        quant_h(0, 0, 256)
-        quant_h(1, 0, 256)
+        quant_h(0)
         gate(4)
         gate(5)
         gate(6)
@@ -262,8 +261,7 @@ def tile_list_ad_bid_scores_kernel(tc, tab_words, tab_scales, tab2_words, tab2_s
         logs(4)
         cast_w(0, "sv")
         cast_w(1, "ss")
-        quant_h(0, 256, 256)
-        quant_h(1, 256, 256)
+        quant_h(1)
         gate(8)
         gate(9)
         quant_w(0)
@@ -276,8 +274,7 @@ def tile_list_ad_bid_scores_kernel(tc, tab_words, tab_scales, tab2_words, tab2_s
         magnitudes(13, 15)
         logs(6)
         scores(256)
-        quant_h(0, 512, 256)
-        quant_h(1, 512, 256)
+        quant_h(2)
         gate(12)
         gate(13)
         magnitudes(15, 16)
@@ -285,8 +282,7 @@ def tile_list_ad_bid_scores_kernel(tc, tab_words, tab_scales, tab2_words, tab2_s
         scores(512)
         gate(14)
         gate(15)
-        quant_h(0, 768, 256)
-        quant_h(1, 768, 256)
+        quant_h(3)
         scores(768)
         bids(0, (0, 1), 30)
         bids(1, (0, 1), 32)

@@ -15,6 +15,7 @@ FP8X4 = mybir.dt.float8_e4m3fn_x4
 FP4X4 = mybir.dt.float4_e2m1fn_x4
 ACT = mybir.ActivationFunctionType
 MULT = mybir.AluOpType.mult
+ADD = mybir.AluOpType.add
 
 P = 128
 
@@ -57,14 +58,14 @@ def tile_list_ad_bid_scores_kernel(tc, tab_words, tab_scales, tab2_words, tab2_s
         a4sraw = kt([P, 2 * H // 4], I32, "a4sraw")
         tab1 = st(2, [P, T], I32, "tab1")
         t2sw = st(3, [P, T // 4], I32, "t2sw")
-        tab2 = st(6, [P, T], I32, "tab2")
+        tab2 = st(0, [P, T], I32, "tab2")
         abs_pair = [st(10 + i % 3, [P, 2, 512], F32, "abs%d" % i) for i in range(8)]
         ysb = [st(10 + (8 + c) % 3, [P, 4, 256], F32, "ysb%d" % c) for c in range(3)] + [kt([P, 4, 256], F32, "ysb3")]
         log_pair = [st(20 + i, [P, 2, 512], F32, "log%d" % i) for i in range(8)]
         bbf = [st(4 + A, [P, 2048], BF16, "bbf%d" % A) for A in range(2)]
-        braw = [st(A, [P, 4, 512], F32, "braw%d" % A) for A in range(2)]
-        wraw = [st(2, [P, 4, N], F32, "wraw0"), st(6, [P, 4, N], F32, "wraw1")]
-        g = [st(slot, [P, T], F32, "g%d" % n) for n, slot in enumerate((3, 0, 4, 1))]
+        braw = [st(1 + A, [P, 4, 512], F32, "braw%d" % A) for A in range(2)]
+        wraw = [st(6, [P, 4, N], F32, "wraw0"), st(0, [P, 4, N], F32, "wraw1")]
+        g = [st(slot, [P, T], F32, "g%d" % n) for n, slot in enumerate((3, 1, 4, 2))]
 
         nc.vector.memset(tsw[0:16, :], 0)
         nc.vector.memset(tsw[32:48, :], 0)
@@ -134,7 +135,15 @@ def tile_list_ad_bid_scores_kernel(tc, tab_words, tab_scales, tab2_words, tab2_s
             src = braw[A][:].rearrange("p j (m t e) -> p t m j e", t=4, e=4)
             dst = bbf[A][:].rearrange("p (t m e j) -> p t m j e", t=4, e=4, j=4)
             for half in range(2):
-                cast(engines[half], dst[:, 2 * half : 2 * half + 2], src[:, 2 * half : 2 * half + 2])
+                if engines[half] == "g":
+                    for t in range(2 * half, 2 * half + 2):
+                        nc.gpsimd.tensor_scalar(
+                            dst[:, t].rearrange("p m j e -> p m e j"),
+                            src[:, t].rearrange("p m j e -> p m e j"),
+                            1.0, 0.0, MULT, ADD,
+                        )
+                else:
+                    cast(engines[half], dst[:, 2 * half : 2 * half + 2], src[:, 2 * half : 2 * half + 2])
 
         def quant_b(A):
             nc.vector.quantize_mx(out=bq[A][:].bitcast(FP8X4), scales=bs[A][:], in_=bbf[A][:])
@@ -143,7 +152,15 @@ def tile_list_ad_bid_scores_kernel(tc, tab_words, tab_scales, tab2_words, tab2_s
             src = wraw[A][:].rearrange("p t (u c i) -> p u c t i", u=4, i=4)
             dst = wbf[A][:].rearrange("p (u c i t) -> p u c t i", u=4, i=4, t=4)
             for half in range(2):
-                cast(engines[half], dst[:, 2 * half : 2 * half + 2], src[:, 2 * half : 2 * half + 2])
+                if engines[half] == "g":
+                    for u in range(2 * half, 2 * half + 2):
+                        nc.gpsimd.tensor_scalar(
+                            wbf[A][:, 512 * u : 512 * (u + 1)].rearrange("p (n t) -> p n t", t=4),
+                            wraw[A][:, :, P * u : P * (u + 1)].rearrange("p t n -> p n t"),
+                            1.0, 0.0, MULT, ADD,
+                        )
+                else:
+                    cast(engines[half], dst[:, 2 * half : 2 * half + 2], src[:, 2 * half : 2 * half + 2])
 
         def quant_w(A):
             nc.vector.quantize_mx(out=wq[A][:].bitcast(FP8X4), scales=ws[A][:], in_=wbf[A][:])
@@ -235,7 +252,7 @@ def tile_list_ad_bid_scores_kernel(tc, tab_words, tab_scales, tab2_words, tab2_s
 
         magnitudes(0, 3)
         logs(0)
-        cast_b(0, "vv")
+        cast_b(0, "gg")
         load_g(1)
         quant_b(0)
         load_g(2)
@@ -259,8 +276,8 @@ def tile_list_ad_bid_scores_kernel(tc, tab_words, tab_scales, tab2_words, tab2_s
         gate(7)
         magnitudes(9, 11)
         logs(4)
-        cast_w(0, "sv")
-        cast_w(1, "ss")
+        cast_w(0, "gg")
+        cast_w(1, "gg")
         quant_h(1)
         gate(8)
         gate(9)

@@ -18,6 +18,7 @@ MULT = mybir.AluOpType.mult
 ADD = mybir.AluOpType.add
 
 P = 128
+UNITS = [(A, P * j) for A in range(2) for j in range(4)] + [(A, P * j) for j in range(4, 8) for A in range(2)]
 
 
 def tile_list_ad_bid_scores_kernel(tc, tab_words, tab_scales, tab2_words, tab2_scales, offs, offs2, a4_words, a4_scales, b, w, gT, out):
@@ -25,6 +26,7 @@ def tile_list_ad_bid_scores_kernel(tc, tab_words, tab_scales, tab2_words, tab2_s
     with ExitStack() as ctx:
         keep = ctx.enter_context(tc.tile_pool(name="keep", bufs=1))
         share = ctx.enter_context(tc.tile_pool(name="share", bufs=1))
+        hand = ctx.enter_context(tc.tile_pool(name="hand", bufs=1))
         psum = ctx.enter_context(tc.psum_pool(name="psum", bufs=1))
 
         def kt(shape, dtype, name):
@@ -32,6 +34,9 @@ def tile_list_ad_bid_scores_kernel(tc, tab_words, tab_scales, tab2_words, tab2_s
 
         def st(slot, shape, dtype, name):
             return share.tile(shape, dtype, name=name, tag="slot%d" % slot, bufs=1, align_bytes=64)
+
+        def ht(kib, shape, dtype, name):
+            return hand.tile(shape, dtype, name=name, align_bytes=64, offset=1024 * kib)
 
         idx = keep.tile([P, S // 16], U16, name="idx")
         idx2 = keep.tile([P, S // 16], U16, name="idx2")
@@ -56,16 +61,16 @@ def tile_list_ad_bid_scores_kernel(tc, tab_words, tab_scales, tab2_words, tab2_s
         tab0 = st(0, [P, T], I32, "tab0")
         a4raw = st(1, [P, 2, H // 2], I32, "a4raw")
         a4sraw = kt([P, 2 * H // 4], I32, "a4sraw")
-        tab1 = st(2, [P, T], I32, "tab1")
+        tab1 = ht(0, [P, T], I32, "tab1")
         t2sw = st(3, [P, T // 4], I32, "t2sw")
-        tab2 = st(0, [P, T], I32, "tab2")
-        abs_pair = [st(10 + i % 3, [P, 2, 512], F32, "abs%d" % i) for i in range(8)]
-        ysb = [st(10 + (8 + c) % 3, [P, 4, 256], F32, "ysb%d" % c) for c in range(3)] + [kt([P, 4, 256], F32, "ysb3")]
+        tab2 = st(1, [P, T], I32, "tab2")
         log_pair = [st(20 + i, [P, 2, 512], F32, "log%d" % i) for i in range(8)]
         bbf = [st(4 + A, [P, 2048], BF16, "bbf%d" % A) for A in range(2)]
-        braw = [st(1 + A, [P, 4, 512], F32, "braw%d" % A) for A in range(2)]
-        wraw = [st(6, [P, 4, N], F32, "wraw0"), st(0, [P, 4, N], F32, "wraw1")]
-        g = [st(slot, [P, T], F32, "g%d" % n) for n, slot in enumerate((3, 1, 4, 2))]
+        braw = [st(0, [P, 4, 512], F32, "braw0"), ht(0, [P, 4, 512], F32, "braw1")]
+        wraw = [st(6, [P, 4, N], F32, "wraw0"), st(3, [P, 4, N], F32, "wraw1")]
+        abs_pair = [ht(4 * (i - 4), [P, 2, 512], F32, "abs%d" % i) if i in (4, 5) else st((10, 11, 12, 10, 0, 0, 11, 12)[i], [P, 2, 512], F32, "abs%d" % i) for i in range(8)]
+        ysb = [ht(4, [P, 4, 256], F32, "ysb0"), st(11, [P, 4, 256], F32, "ysb1"), st(12, [P, 4, 256], F32, "ysb2"), kt([P, 4, 256], F32, "ysb3")]
+        g = [st(slot, [P, T], F32, "g%d" % n) for n, slot in enumerate((0, 1, 4, 5))]
 
         nc.vector.memset(tsw[0:16, :], 0)
         nc.vector.memset(tsw[32:48, :], 0)
@@ -105,14 +110,14 @@ def tile_list_ad_bid_scores_kernel(tc, tab_words, tab_scales, tab2_words, tab2_s
             a4sraw[:].rearrange("p (x m t) -> p x m t", x=4, t=4),
         )
         gather_words(v[0], tab0, idx, 0, S)
-        nc.sync.dma_start(out=tab2[:], in_=tab2_words[0].rearrange("p t i -> p (t i)").bitcast(I32))
+        nc.sync.dma_start(out=braw[0][:], in_=b[:, 0:512].rearrange("(p j) r -> p j r", j=4))
         for Q in range(4):
             nc.sync.dma_start(out=t2sw[32 * Q : 32 * Q + 4, :], in_=tab2_scales[0, 4 * Q : 4 * Q + 4, :].bitcast(I32))
         nc.vector.tensor_copy(
             a4p[:].rearrange("p (x t m e) -> p x t m e", x=4, t=4, e=2),
             a4raw[:].rearrange("p a (x m t e) -> p (a x) t m e", x=2, t=4, e=2),
         )
-        nc.sync.dma_start(out=braw[0][:], in_=b[:, 0:512].rearrange("(p j) r -> p j r", j=4))
+        nc.sync.dma_start(out=tab2[:], in_=tab2_words[0].rearrange("p t i -> p (t i)").bitcast(I32))
         gather_words(v[1], tab1, idx, 0, 256)
         gather_words(v[1], tab1, idx, 256, S)
         nc.sync.dma_start(out=braw[1][:], in_=b[:, 512:1024].rearrange("(p j) r -> p j r", j=4))
@@ -142,6 +147,11 @@ def tile_list_ad_bid_scores_kernel(tc, tab_words, tab_scales, tab2_words, tab2_s
                             src[:, t].rearrange("p m j e -> p m e j"),
                             1.0, 0.0, MULT, ADD,
                         )
+                elif engines[half] == "w":
+                    nc.vector.tensor_copy(
+                        dst[:, 2 * half : 2 * half + 2].rearrange("p t m j e -> p t m e j"),
+                        src[:, 2 * half : 2 * half + 2].rearrange("p t m j e -> p t m e j"),
+                    )
                 else:
                     cast(engines[half], dst[:, 2 * half : 2 * half + 2], src[:, 2 * half : 2 * half + 2])
 
@@ -159,17 +169,27 @@ def tile_list_ad_bid_scores_kernel(tc, tab_words, tab_scales, tab2_words, tab2_s
                             wraw[A][:, :, P * u : P * (u + 1)].rearrange("p t n -> p n t"),
                             1.0, 0.0, MULT, ADD,
                         )
+                elif engines[half] == "w":
+                    nc.vector.tensor_copy(
+                        wbf[A][:, 1024 * half : 1024 * (half + 1)].rearrange("p (n t) -> p n t", t=4),
+                        wraw[A][:, :, 256 * half : 256 * (half + 1)].rearrange("p t n -> p n t"),
+                    )
                 else:
                     cast(engines[half], dst[:, 2 * half : 2 * half + 2], src[:, 2 * half : 2 * half + 2])
 
         def quant_w(A):
             nc.vector.quantize_mx(out=wq[A][:].bitcast(FP8X4), scales=ws[A][:], in_=wbf[A][:])
 
-        gather_words(v2, tab2, idx2, 0, S)
+        gather_scales(v2s, t2sw, idx2)
         load_w(0)
         load_w(1)
-        gather_scales(v2s, t2sw, idx2)
+        cast_b(0, "gg")
         load_g(0)
+        quant_b(0)
+        gather_words(v2, tab2, idx2, 0, 256)
+        gather_words(v2, tab2, idx2, 256, S)
+        load_g(1)
+        load_g(2)
 
         banks = [psum.tile([P, 512], F32, name="bank%d" % i) for i in range(8)]
 
@@ -190,7 +210,7 @@ def tile_list_ad_bid_scores_kernel(tc, tab_words, tab_scales, tab2_words, tab2_s
             nc.scalar.activation(ab.rearrange("p (n t) -> p n t", t=4), pp.rearrange("p t n -> p n t"), ACT.Abs)
 
         def gate(u):
-            A, j0 = u % 2, P * (u // 2)
+            A, j0 = UNITS[u]
             qq = banks[u % 8][:].rearrange("p (t n) -> p t n", t=4)
             for t in range(4):
                 nc.tensor.matmul_mx(
@@ -244,7 +264,7 @@ def tile_list_ad_bid_scores_kernel(tc, tab_words, tab_scales, tab2_words, tab2_s
 
         def magnitudes(first, last):
             for u in range(first, last):
-                A, j0 = u % 2, P * (u // 2)
+                A, j0 = UNITS[u]
                 magnitude(A, j0, abs_pair[u // 2][:, u % 2, :], banks[u % 8])
 
         def logs(pair):
@@ -252,32 +272,29 @@ def tile_list_ad_bid_scores_kernel(tc, tab_words, tab_scales, tab2_words, tab2_s
 
         magnitudes(0, 3)
         logs(0)
-        cast_b(0, "gg")
-        load_g(1)
-        quant_b(0)
-        load_g(2)
         magnitudes(3, 5)
         logs(1)
-        cast_b(1, "vv")
-        load_g(3)
+        cast_b(1, "gg")
         magnitudes(5, 7)
         logs(2)
-        gate(0)
-        quant_b(1)
-        gate(2)
-        gate(1)
-        gate(3)
-        magnitudes(7, 9)
+        magnitudes(7, 8)
         logs(3)
-        quant_h(0)
+        gate(0)
+        gate(1)
+        gate(2)
+        gate(3)
+        quant_b(1)
+        load_g(3)
+        magnitudes(8, 10)
+        cast_w(0, "gg")
         gate(4)
         gate(5)
         gate(6)
         gate(7)
-        magnitudes(9, 11)
+        magnitudes(10, 11)
         logs(4)
-        cast_w(0, "gg")
-        cast_w(1, "gg")
+        cast_w(1, "ss")
+        quant_h(0)
         quant_h(1)
         gate(8)
         gate(9)

@@ -49,7 +49,6 @@ def tile_list_ad_bid_scores_kernel(tc, tab_words, tab_scales, tab2_words, tab2_s
         a4p = kt([P, H], I32, "a4p")
         a4sp = kt([P, 2 * H // 4], I32, "a4sp")
         bq = [kt([P, 512], I32, "bq%d" % A) for A in range(2)]
-        bs = [kt([P, 512], U8, "bs%d" % A) for A in range(2)]
         wbf = [kt([P, 4 * N], BF16, "wbf%d" % A) for A in range(2)]
         wq = [kt([P, N], I32, "wq%d" % A) for A in range(2)]
         ws = [kt([P, N], U8, "ws%d" % A) for A in range(2)]
@@ -59,18 +58,19 @@ def tile_list_ad_bid_scores_kernel(tc, tab_words, tab_scales, tab2_words, tab2_s
         one = kt([P, 2], F32, "one")
 
         tab0 = st(0, [P, T], I32, "tab0")
-        a4raw = st(1, [P, 2, H // 2], I32, "a4raw")
+        a4raw = ht(8, [P, 2, H // 2], I32, "a4raw")
         a4sraw = kt([P, 2 * H // 4], I32, "a4sraw")
         tab1 = ht(0, [P, T], I32, "tab1")
         t2sw = st(3, [P, T // 4], I32, "t2sw")
-        tab2 = st(1, [P, T], I32, "tab2")
+        tab2 = ht(8, [P, T], I32, "tab2")
         log_pair = [st(20 + i, [P, 2, 512], F32, "log%d" % i) for i in range(8)]
         bbf = [st(4 + A, [P, 2048], BF16, "bbf%d" % A) for A in range(2)]
         braw = [st(0, [P, 4, 512], F32, "braw0"), ht(0, [P, 4, 512], F32, "braw1")]
         wraw = [st(6, [P, 4, N], F32, "wraw0"), st(3, [P, 4, N], F32, "wraw1")]
         abs_pair = [ht(4 * (i - 4), [P, 2, 512], F32, "abs%d" % i) if i in (4, 5) else st((10, 11, 12, 10, 0, 0, 11, 12)[i], [P, 2, 512], F32, "abs%d" % i) for i in range(8)]
         ysb = [ht(4, [P, 4, 256], F32, "ysb0"), st(11, [P, 4, 256], F32, "ysb1"), st(12, [P, 4, 256], F32, "ysb2"), kt([P, 4, 256], F32, "ysb3")]
-        g = [st(slot, [P, T], F32, "g%d" % n) for n, slot in enumerate((0, 1, 4, 5))]
+        bs = [ht(8, [P, 512], U8, "bs0"), kt([P, 512], U8, "bs1")]
+        g = [st(0, [P, T], F32, "g0"), ht(9, [P, T], F32, "g1"), st(4, [P, T], F32, "g2"), st(5, [P, T], F32, "g3")]
 
         nc.vector.memset(tsw[0:16, :], 0)
         nc.vector.memset(tsw[32:48, :], 0)
@@ -185,9 +185,8 @@ def tile_list_ad_bid_scores_kernel(tc, tab_words, tab_scales, tab2_words, tab2_s
         load_w(1)
         cast_b(0, "gg")
         load_g(0)
+        gather_words(v2, tab2, idx2, 0, S)
         quant_b(0)
-        gather_words(v2, tab2, idx2, 0, 256)
-        gather_words(v2, tab2, idx2, 256, S)
         load_g(1)
         load_g(2)
 

@@ -44,7 +44,6 @@ def tile_list_ad_bid_scores_kernel(tc, tab_words, tab_scales, tab2_words, tab2_s
         gs = kt([P, S // 4], I32, "gs")
         v = [kt([P, S], I32, "v%d" % a) for a in range(2)]
         vs = [kt([P, S // 4], I32, "vs%d" % a) for a in range(2)]
-        v2 = kt([P, S], I32, "v2")
         v2s = kt([P, S // 4], I32, "v2s")
         a4p = kt([P, H], I32, "a4p")
         a4sp = kt([P, 2 * H // 4], I32, "a4sp")
@@ -61,16 +60,17 @@ def tile_list_ad_bid_scores_kernel(tc, tab_words, tab_scales, tab2_words, tab2_s
         a4raw = ht(8, [P, 2, H // 2], I32, "a4raw")
         a4sraw = kt([P, 2 * H // 4], I32, "a4sraw")
         tab1 = ht(0, [P, T], I32, "tab1")
-        t2sw = st(3, [P, T // 4], I32, "t2sw")
+        t2sw = ht(18, [P, T // 4], I32, "t2sw")
         tab2 = ht(8, [P, T], I32, "tab2")
-        log_pair = [st(20 + i, [P, 2, 512], F32, "log%d" % i) for i in range(8)]
+        log_pair = [st(20 + i, [P, 2, 512], F32, "log%d" % i) for i in range(7)] + [ht(28, [P, 2, 512], F32, "log7")]
         bbf = [st(4 + A, [P, 2048], BF16, "bbf%d" % A) for A in range(2)]
         braw = [st(0, [P, 4, 512], F32, "braw0"), ht(0, [P, 4, 512], F32, "braw1")]
-        wraw = [st(6, [P, 4, N], F32, "wraw0"), st(3, [P, 4, N], F32, "wraw1")]
+        wraw = [st(6, [P, 4, N], F32, "wraw0"), ht(19, [P, 4, N], F32, "wraw1")]
         abs_pair = [ht(4 * (i - 4), [P, 2, 512], F32, "abs%d" % i) if i in (4, 5) else st((10, 11, 12, 10, 0, 0, 11, 12)[i], [P, 2, 512], F32, "abs%d" % i) for i in range(8)]
         ysb = [ht(4, [P, 4, 256], F32, "ysb0"), st(11, [P, 4, 256], F32, "ysb1"), st(12, [P, 4, 256], F32, "ysb2"), kt([P, 4, 256], F32, "ysb3")]
-        bs = [ht(8, [P, 512], U8, "bs0"), kt([P, 512], U8, "bs1")]
-        g = [st(0, [P, T], F32, "g0"), ht(9, [P, T], F32, "g1"), st(4, [P, T], F32, "g2"), st(5, [P, T], F32, "g3")]
+        v2 = [kt([P, 512], I32, "v2a"), st(5, [P, 512], I32, "v2b")]
+        bs = [ht(18, [P, 512], U8, "bs0"), kt([P, 512], U8, "bs1")]
+        g = [st(0, [P, T], F32, "g0"), ht(8, [P, T], F32, "g1"), st(4, [P, T], F32, "g2"), st(20, [P, T], F32, "g3")]
 
         nc.vector.memset(tsw[0:16, :], 0)
         nc.vector.memset(tsw[32:48, :], 0)
@@ -96,6 +96,9 @@ def tile_list_ad_bid_scores_kernel(tc, tab_words, tab_scales, tab2_words, tab2_s
 
         def gather_words(dst, window, lst, j0, j1):
             nc.vector.tensor_copy(dst[:, j0:j1].bitcast(U32), window[:].bitcast(U32).indirect(lst[:, j0 // 16 : j1 // 16]))
+
+        def gather_half(dst, window, lst, j0, j1):
+            nc.vector.tensor_copy(dst[:, j0 % 512 : j0 % 512 + j1 - j0].bitcast(U32), window[:].bitcast(U32).indirect(lst[:, j0 // 16 : j1 // 16]))
 
         def gather_scales(dst, window, lst):
             nc.vector.tensor_copy(dst[:].bitcast(U8), window[:].bitcast(U8).indirect(lst[:]))
@@ -185,10 +188,9 @@ def tile_list_ad_bid_scores_kernel(tc, tab_words, tab_scales, tab2_words, tab2_s
         load_w(1)
         cast_b(0, "gg")
         load_g(0)
-        gather_words(v2, tab2, idx2, 0, S)
         quant_b(0)
-        load_g(1)
-        load_g(2)
+        gather_half(v2[0], tab2, idx2, 0, 256)
+        gather_half(v2[0], tab2, idx2, 256, 512)
 
         banks = [psum.tile([P, 512], F32, name="bank%d" % i) for i in range(8)]
 
@@ -216,7 +218,7 @@ def tile_list_ad_bid_scores_kernel(tc, tab_words, tab_scales, tab2_words, tab2_s
                     out=qq[:, t, :],
                     lhsT=bq[A][:, P * t : P * (t + 1)].bitcast(FP8X4),
                     lhsT_scale=bs[A][:, P * t : P * (t + 1)],
-                    rhs=v2[:, j0 : j0 + P].bitcast(FP8X4),
+                    rhs=v2[j0 // 512][:, j0 % 512 : j0 % 512 + P].bitcast(FP8X4),
                     rhs_scale=v2s[:, j0 // 4 : (j0 + P) // 4].bitcast(U8),
                     start=True,
                     stop=True,
@@ -252,7 +254,7 @@ def tile_list_ad_bid_scores_kernel(tc, tab_words, tab_scales, tab2_words, tab2_s
 
         def bids(c, pairs, slot):
             for pair in pairs:
-                osb = st(slot + pair, [P, 2, 256], F32, "osb%d_%d" % (c, pair))
+                osb = ht(28 + 2 * pair, [P, 2, 256], F32, "osb%d_%d" % (c, pair)) if c == 2 else st(slot + pair, [P, 2, 256], F32, "osb%d_%d" % (c, pair))
                 for i in range(2):
                     n = 2 * pair + i
                     nc.vector.tensor_tensor(osb[:, i, :], g[n][:].indirect(idx[:, 16 * c : 16 * (c + 1)]), ysb[c][:, n, :], MULT)
@@ -283,6 +285,9 @@ def tile_list_ad_bid_scores_kernel(tc, tab_words, tab_scales, tab2_words, tab2_s
         gate(2)
         gate(3)
         quant_b(1)
+        gather_half(v2[1], tab2, idx2, 512, S)
+        load_g(1)
+        load_g(2)
         load_g(3)
         magnitudes(8, 10)
         cast_w(0, "gg")
@@ -292,7 +297,7 @@ def tile_list_ad_bid_scores_kernel(tc, tab_words, tab_scales, tab2_words, tab2_s
         gate(7)
         magnitudes(10, 11)
         logs(4)
-        cast_w(1, "ss")
+        cast_w(1, "gs")
         quant_h(0)
         quant_h(1)
         gate(8)

@@ -48,7 +48,6 @@ def tile_list_ad_bid_scores_kernel(tc, tab_words, tab_scales, tab2_words, tab2_s
         a4p = kt([P, H], I32, "a4p")
         a4sp = kt([P, 2 * H // 4], I32, "a4sp")
         bq = [kt([P, 512], I32, "bq%d" % A) for A in range(2)]
-        wbf = [kt([P, 4 * N], BF16, "wbf%d" % A) for A in range(2)]
         wq = [kt([P, N], I32, "wq%d" % A) for A in range(2)]
         ws = [kt([P, N], U8, "ws%d" % A) for A in range(2)]
         hq = [kt([P, 2, 256], I32, "hq%d" % c) for c in range(4)]
@@ -63,12 +62,13 @@ def tile_list_ad_bid_scores_kernel(tc, tab_words, tab_scales, tab2_words, tab2_s
         t2sw = ht(18, [P, T // 4], I32, "t2sw")
         tab2 = ht(8, [P, T], I32, "tab2")
         log_pair = [st(20 + i, [P, 2, 512], F32, "log%d" % i) for i in range(7)] + [ht(28, [P, 2, 512], F32, "log7")]
-        bbf = [st(4 + A, [P, 2048], BF16, "bbf%d" % A) for A in range(2)]
+        bbf = [st(4, [P, 2048], BF16, "bbf0"), ht(32, [P, 2048], BF16, "bbf1")]
+        wbf = [ht(34, [P, 4 * N], BF16, "wbf0"), kt([P, 4 * N], BF16, "wbf1")]
         braw = [st(0, [P, 4, 512], F32, "braw0"), ht(0, [P, 4, 512], F32, "braw1")]
         wraw = [st(6, [P, 4, N], F32, "wraw0"), ht(19, [P, 4, N], F32, "wraw1")]
         abs_pair = [ht(4 * (i - 4), [P, 2, 512], F32, "abs%d" % i) if i in (4, 5) else st((10, 11, 12, 10, 0, 0, 11, 12)[i], [P, 2, 512], F32, "abs%d" % i) for i in range(8)]
         ysb = [ht(4, [P, 4, 256], F32, "ysb0"), st(11, [P, 4, 256], F32, "ysb1"), st(12, [P, 4, 256], F32, "ysb2"), kt([P, 4, 256], F32, "ysb3")]
-        v2 = [kt([P, 512], I32, "v2a"), st(5, [P, 512], I32, "v2b")]
+        v2 = [kt([P, 512], I32, "v2a"), ht(32, [P, 512], I32, "v2b")]
         bs = [ht(18, [P, 512], U8, "bs0"), kt([P, 512], U8, "bs1")]
         g = [st(0, [P, T], F32, "g0"), ht(8, [P, T], F32, "g1"), st(4, [P, T], F32, "g2"), st(20, [P, T], F32, "g3")]
 
@@ -142,21 +142,15 @@ def tile_list_ad_bid_scores_kernel(tc, tab_words, tab_scales, tab2_words, tab2_s
         def cast_b(A, engines):
             src = braw[A][:].rearrange("p j (m t e) -> p t m j e", t=4, e=4)
             dst = bbf[A][:].rearrange("p (t m e j) -> p t m j e", t=4, e=4, j=4)
-            for half in range(2):
-                if engines[half] == "g":
-                    for t in range(2 * half, 2 * half + 2):
-                        nc.gpsimd.tensor_scalar(
-                            dst[:, t].rearrange("p m j e -> p m e j"),
-                            src[:, t].rearrange("p m j e -> p m e j"),
-                            1.0, 0.0, MULT, ADD,
-                        )
-                elif engines[half] == "w":
-                    nc.vector.tensor_copy(
-                        dst[:, 2 * half : 2 * half + 2].rearrange("p t m j e -> p t m e j"),
-                        src[:, 2 * half : 2 * half + 2].rearrange("p t m j e -> p t m e j"),
+            for t in range(4):
+                if engines[t] == "g":
+                    nc.gpsimd.tensor_scalar(
+                        dst[:, t].rearrange("p m j e -> p m e j"),
+                        src[:, t].rearrange("p m j e -> p m e j"),
+                        1.0, 0.0, MULT, ADD,
                     )
                 else:
-                    cast(engines[half], dst[:, 2 * half : 2 * half + 2], src[:, 2 * half : 2 * half + 2])
+                    nc.vector.tensor_copy(dst[:, t], src[:, t])
 
         def quant_b(A):
             nc.vector.quantize_mx(out=bq[A][:].bitcast(FP8X4), scales=bs[A][:], in_=bbf[A][:])
@@ -172,12 +166,7 @@ def tile_list_ad_bid_scores_kernel(tc, tab_words, tab_scales, tab2_words, tab2_s
                             wraw[A][:, :, P * u : P * (u + 1)].rearrange("p t n -> p n t"),
                             1.0, 0.0, MULT, ADD,
                         )
-                elif engines[half] == "w":
-                    nc.vector.tensor_copy(
-                        wbf[A][:, 1024 * half : 1024 * (half + 1)].rearrange("p (n t) -> p n t", t=4),
-                        wraw[A][:, :, 256 * half : 256 * (half + 1)].rearrange("p t n -> p n t"),
-                    )
-                else:
+                elif engines[half] == "s":
                     cast(engines[half], dst[:, 2 * half : 2 * half + 2], src[:, 2 * half : 2 * half + 2])
 
         def quant_w(A):
@@ -186,7 +175,7 @@ def tile_list_ad_bid_scores_kernel(tc, tab_words, tab_scales, tab2_words, tab2_s
         gather_scales(v2s, t2sw, idx2)
         load_w(0)
         load_w(1)
-        cast_b(0, "gg")
+        cast_b(0, "vggg")
         load_g(0)
         quant_b(0)
         gather_half(v2[0], tab2, idx2, 0, 256)
@@ -223,7 +212,7 @@ def tile_list_ad_bid_scores_kernel(tc, tab_words, tab_scales, tab2_words, tab2_s
                     start=True,
                     stop=True,
                 )
-            nc.vector.tensor_tensor(hb[j0 // 256][:, A, j0 % 256 : j0 % 256 + P, :], qq.rearrange("p t n -> p n t"), log_pair[u // 2][:, u % 2, :].rearrange("p (n t) -> p n t", t=4), MULT)
+            nc.vector.tensor_tensor(hb[j0 // 256][:, A, j0 % 256 : j0 % 256 + P, :], log_pair[u // 2][:, u % 2, :].rearrange("p (n t) -> p n t", t=4), qq.rearrange("p t n -> p n t"), MULT)
 
         def quant_h(c):
             nc.vector.quantize_mx(
@@ -275,7 +264,7 @@ def tile_list_ad_bid_scores_kernel(tc, tab_words, tab_scales, tab2_words, tab2_s
         logs(0)
         magnitudes(3, 5)
         logs(1)
-        cast_b(1, "gg")
+        cast_b(1, "gggg")
         magnitudes(5, 7)
         logs(2)
         magnitudes(7, 8)
@@ -298,11 +287,11 @@ def tile_list_ad_bid_scores_kernel(tc, tab_words, tab_scales, tab2_words, tab2_s
         magnitudes(10, 11)
         logs(4)
         cast_w(1, "gs")
-        quant_h(0)
-        quant_h(1)
         gate(8)
         gate(9)
+        quant_h(0)
         quant_w(0)
+        quant_h(1)
         quant_w(1)
         magnitudes(11, 13)
         logs(5)

@@ -53,7 +53,6 @@ def tile_list_ad_bid_scores_kernel(tc, tab_words, tab_scales, tab2_words, tab2_s
         hq = [kt([P, 2, 256], I32, "hq%d" % c) for c in range(4)]
         hs = [kt([P, 2, 256], U8, "hs%d" % c) for c in range(4)]
         hb = [kt([P, 2, 256, 4], BF16, "hb%d" % c) for c in range(4)]
-        one = kt([P, 2], F32, "one")
 
         tab0 = st(0, [P, T], I32, "tab0")
         a4raw = ht(8, [P, 2, H // 2], I32, "a4raw")
@@ -76,9 +75,7 @@ def tile_list_ad_bid_scores_kernel(tc, tab_words, tab_scales, tab2_words, tab2_s
         nc.vector.memset(tsw[32:48, :], 0)
         nc.vector.memset(tsw[64:128, :], 0)
         nc.gpsimd.memset(a4sraw[:], 0)
-        nc.gpsimd.memset(one[:, 0:1], 1.0)
         nc.vector.memset(t2sw[:], 0)
-        nc.scalar.activation(one[:, 1:2], one[:, 0:1], ACT.Ln)
 
         nc.sync.dma_start(idx[:], offs)
         rows = tab_scales.rearrange("a (u h r) n -> h (a u) r n", u=2, h=2)

@@ -142,8 +142,8 @@ def tile_list_ad_bid_scores_kernel(tc, tab_words, tab_scales, tab2_words, tab2_s
             for t in range(4):
                 if engines[t] == "g":
                     nc.gpsimd.tensor_scalar(
-                        dst[:, t].rearrange("p m j e -> p m e j"),
-                        src[:, t].rearrange("p m j e -> p m e j"),
+                        dst[:, t],
+                        src[:, t],
                         1.0, 0.0, MULT, ADD,
                     )
                 else:
@@ -159,8 +159,8 @@ def tile_list_ad_bid_scores_kernel(tc, tab_words, tab_scales, tab2_words, tab2_s
                 if engines[half] == "g":
                     for u in range(2 * half, 2 * half + 2):
                         nc.gpsimd.tensor_scalar(
-                            wbf[A][:, 512 * u : 512 * (u + 1)].rearrange("p (n t) -> p n t", t=4),
-                            wraw[A][:, :, P * u : P * (u + 1)].rearrange("p t n -> p n t"),
+                            dst[:, u],
+                            src[:, u],
                             1.0, 0.0, MULT, ADD,
                         )
                 elif engines[half] == "s":

@@ -75,6 +75,9 @@ def tile_list_ad_bid_scores_kernel(tc, tab_words, tab_scales, tab2_words, tab2_s
         nc.vector.memset(tsw[32:48, :], 0)
         nc.vector.memset(tsw[64:128, :], 0)
         nc.gpsimd.memset(a4sraw[:], 0)
+        warm = kt([P, 2], F32, "warm")
+        nc.gpsimd.memset(warm[:, 0:1], 1.0)
+        nc.scalar.activation(warm[:, 1:2], warm[:, 0:1], ACT.Ln)
         nc.vector.memset(t2sw[:], 0)
 
         nc.sync.dma_start(idx[:], offs)
@@ -283,7 +286,7 @@ def tile_list_ad_bid_scores_kernel(tc, tab_words, tab_scales, tab2_words, tab2_s
         gate(7)
         magnitudes(10, 11)
         logs(4)
-        cast_w(1, "gs")
+        cast_w(1, "ss")
         gate(8)
         gate(9)
         quant_h(0)

@@ -18,6 +18,8 @@ MULT = mybir.AluOpType.mult
 ADD = mybir.AluOpType.add
 
 P = 128
+HALF = 512
+CHUNK = 256
 UNITS = [(A, P * j) for A in range(2) for j in range(4)] + [(A, P * j) for j in range(4, 8) for A in range(2)]
 
 
@@ -47,12 +49,12 @@ def tile_list_ad_bid_scores_kernel(tc, tab_words, tab_scales, tab2_words, tab2_s
         v2s = kt([P, S // 4], I32, "v2s")
         a4p = kt([P, H], I32, "a4p")
         a4sp = kt([P, 2 * H // 4], I32, "a4sp")
-        bq = [kt([P, 512], I32, "bq%d" % A) for A in range(2)]
+        bq = [kt([P, HALF], I32, "bq%d" % A) for A in range(2)]
         wq = [kt([P, N], I32, "wq%d" % A) for A in range(2)]
         ws = [kt([P, N], U8, "ws%d" % A) for A in range(2)]
-        hq = [kt([P, 2, 256], I32, "hq%d" % c) for c in range(4)]
-        hs = [kt([P, 2, 256], U8, "hs%d" % c) for c in range(4)]
-        hb = [kt([P, 2, 256, 4], BF16, "hb%d" % c) for c in range(4)]
+        hq = [kt([P, 2, CHUNK], I32, "hq%d" % c) for c in range(4)]
+        hs = [kt([P, 2, CHUNK], U8, "hs%d" % c) for c in range(4)]
+        hb = [kt([P, 2, CHUNK, 4], BF16, "hb%d" % c) for c in range(4)]
 
         tab0 = st(0, [P, T], I32, "tab0")
         a4raw = ht(8, [P, 2, H // 2], I32, "a4raw")
@@ -60,15 +62,19 @@ def tile_list_ad_bid_scores_kernel(tc, tab_words, tab_scales, tab2_words, tab2_s
         tab1 = ht(0, [P, T], I32, "tab1")
         t2sw = ht(18, [P, T // 4], I32, "t2sw")
         tab2 = ht(8, [P, T], I32, "tab2")
-        log_pair = [st(20 + i, [P, 2, 512], F32, "log%d" % i) for i in range(7)] + [ht(28, [P, 2, 512], F32, "log7")]
-        bbf = [st(4, [P, 2048], BF16, "bbf0"), ht(32, [P, 2048], BF16, "bbf1")]
+        log_pair = [st(20 + i, [P, 2, HALF], F32, "log%d" % i) for i in range(7)] + [ht(28, [P, 2, HALF], F32, "log7")]
+        bbf = [st(4, [P, 4 * HALF], BF16, "bbf0"), ht(32, [P, 4 * HALF], BF16, "bbf1")]
         wbf = [ht(34, [P, 4 * N], BF16, "wbf0"), kt([P, 4 * N], BF16, "wbf1")]
-        braw = [st(0, [P, 4, 512], F32, "braw0"), ht(0, [P, 4, 512], F32, "braw1")]
+        braw = [st(0, [P, 4, HALF], F32, "braw0"), ht(0, [P, 4, HALF], F32, "braw1")]
         wraw = [st(6, [P, 4, N], F32, "wraw0"), ht(19, [P, 4, N], F32, "wraw1")]
-        abs_pair = [ht(4 * (i - 4), [P, 2, 512], F32, "abs%d" % i) if i in (4, 5) else st((10, 11, 12, 10, 0, 0, 11, 12)[i], [P, 2, 512], F32, "abs%d" % i) for i in range(8)]
-        ysb = [ht(4, [P, 4, 256], F32, "ysb0"), st(11, [P, 4, 256], F32, "ysb1"), st(12, [P, 4, 256], F32, "ysb2"), kt([P, 4, 256], F32, "ysb3")]
-        v2 = [kt([P, 512], I32, "v2a"), ht(32, [P, 512], I32, "v2b")]
-        bs = [ht(18, [P, 512], U8, "bs0"), kt([P, 512], U8, "bs1")]
+        abs_slot = {0: 10, 1: 11, 2: 12, 3: 10, 6: 11, 7: 12}
+        abs_pair = [
+            st(abs_slot[i], [P, 2, HALF], F32, "abs%d" % i) if i in abs_slot else ht(4 * (i - 4), [P, 2, HALF], F32, "abs%d" % i)
+            for i in range(8)
+        ]
+        ysb = [ht(4, [P, 2, HALF], F32, "ysb0"), st(11, [P, 2, HALF], F32, "ysb1"), st(12, [P, 4, CHUNK], F32, "ysb2"), kt([P, 4, CHUNK], F32, "ysb3")]
+        v2 = [kt([P, HALF], I32, "v2a"), ht(32, [P, HALF], I32, "v2b")]
+        bs = [ht(18, [P, HALF], U8, "bs0"), kt([P, HALF], U8, "bs1")]
         g = [st(0, [P, T], F32, "g0"), ht(8, [P, T], F32, "g1"), st(4, [P, T], F32, "g2"), st(20, [P, T], F32, "g3")]
 
         nc.vector.memset(tsw[0:16, :], 0)
@@ -94,14 +100,41 @@ def tile_list_ad_bid_scores_kernel(tc, tab_words, tab_scales, tab2_words, tab2_s
         nc.sync.dma_start(out=tab1[:], in_=tab_words[1].rearrange("p t i -> p (t i)").bitcast(I32))
         nc.sync.dma_start(idx2[:], offs2)
 
-        def gather_words(dst, window, lst, j0, j1):
-            nc.vector.tensor_copy(dst[:, j0:j1].bitcast(U32), window[:].bitcast(U32).indirect(lst[:, j0 // 16 : j1 // 16]))
-
-        def gather_half(dst, window, lst, j0, j1):
-            nc.vector.tensor_copy(dst[:, j0 % 512 : j0 % 512 + j1 - j0].bitcast(U32), window[:].bitcast(U32).indirect(lst[:, j0 // 16 : j1 // 16]))
+        def gather_words(dst, window, lst, j0, j1, first):
+            nc.vector.tensor_copy(dst[:, j0 - first : j1 - first].bitcast(U32), window[:].bitcast(U32).indirect(lst[:, j0 // 16 : j1 // 16]))
 
         def gather_scales(dst, window, lst):
             nc.vector.tensor_copy(dst[:].bitcast(U8), window[:].bitcast(U8).indirect(lst[:]))
+
+        def load_b(A):
+            nc.sync.dma_start(out=braw[A][:], in_=b[:, HALF * A : HALF * (A + 1)].rearrange("(p j) r -> p j r", j=4))
+
+        def load_w(A):
+            wrows = w[HALF * A : HALF * (A + 1), :].rearrange("(m t e) n -> t m e n", t=4, e=4)
+            for t in range(4):
+                nc.sync.dma_start(out=wraw[A][:, t, :], in_=wrows[t])
+
+        def load_g(n):
+            nc.sync.dma_start(out=g[n][:], in_=gT[P * n : P * (n + 1), :])
+
+        def round_gpsimd(dst, src):
+            nc.gpsimd.tensor_scalar(dst, src, 1.0, 0.0, MULT, ADD)
+
+        def b_views(A):
+            src = braw[A][:].rearrange("p j (m t e) -> p t m j e", t=4, e=4)
+            dst = bbf[A][:].rearrange("p (t m e j) -> p t m j e", t=4, e=4, j=4)
+            return dst, src
+
+        def w_views(A):
+            src = wraw[A][:].rearrange("p t (u c i) -> p u c t i", u=4, i=4)
+            dst = wbf[A][:].rearrange("p (u c i t) -> p u c t i", u=4, i=4, t=4)
+            return dst, src
+
+        def quant_b(A):
+            nc.vector.quantize_mx(out=bq[A][:].bitcast(FP8X4), scales=bs[A][:], in_=bbf[A][:])
+
+        def quant_w(A):
+            nc.vector.quantize_mx(out=wq[A][:].bitcast(FP8X4), scales=ws[A][:], in_=wbf[A][:])
 
         gather_scales(gs, tsw, idx)
         for u in range(2):
@@ -112,8 +145,8 @@ def tile_list_ad_bid_scores_kernel(tc, tab_words, tab_scales, tab2_words, tab2_s
             a4sp[:].rearrange("p (x t m) -> p x m t", x=4, t=4),
             a4sraw[:].rearrange("p (x m t) -> p x m t", x=4, t=4),
         )
-        gather_words(v[0], tab0, idx, 0, S)
-        nc.sync.dma_start(out=braw[0][:], in_=b[:, 0:512].rearrange("(p j) r -> p j r", j=4))
+        gather_words(v[0], tab0, idx, 0, S, 0)
+        load_b(0)
         for Q in range(4):
             nc.sync.dma_start(out=t2sw[32 * Q : 32 * Q + 4, :], in_=tab2_scales[0, 4 * Q : 4 * Q + 4, :].bitcast(I32))
         nc.vector.tensor_copy(
@@ -121,83 +154,44 @@ def tile_list_ad_bid_scores_kernel(tc, tab_words, tab_scales, tab2_words, tab2_s
             a4raw[:].rearrange("p a (x m t e) -> p (a x) t m e", x=2, t=4, e=2),
         )
         nc.sync.dma_start(out=tab2[:], in_=tab2_words[0].rearrange("p t i -> p (t i)").bitcast(I32))
-        gather_words(v[1], tab1, idx, 0, 256)
-        gather_words(v[1], tab1, idx, 256, S)
-        nc.sync.dma_start(out=braw[1][:], in_=b[:, 512:1024].rearrange("(p j) r -> p j r", j=4))
-
-        def load_w(A):
-            wrows = w[512 * A : 512 * (A + 1), :].rearrange("(m t e) n -> t m e n", t=4, e=4)
-            for t in range(4):
-                nc.sync.dma_start(out=wraw[A][:, t, :], in_=wrows[t])
-
-        def load_g(n):
-            nc.sync.dma_start(out=g[n][:], in_=gT[P * n : P * (n + 1), :])
-
-        def cast(eng, dst, src):
-            if eng == "s":
-                nc.scalar.copy(dst, src)
-            else:
-                nc.vector.tensor_copy(dst, src)
-
-        def cast_b(A, engines):
-            src = braw[A][:].rearrange("p j (m t e) -> p t m j e", t=4, e=4)
-            dst = bbf[A][:].rearrange("p (t m e j) -> p t m j e", t=4, e=4, j=4)
-            for t in range(4):
-                if engines[t] == "g":
-                    nc.gpsimd.tensor_scalar(
-                        dst[:, t],
-                        src[:, t],
-                        1.0, 0.0, MULT, ADD,
-                    )
-                else:
-                    nc.vector.tensor_copy(dst[:, t], src[:, t])
-
-        def quant_b(A):
-            nc.vector.quantize_mx(out=bq[A][:].bitcast(FP8X4), scales=bs[A][:], in_=bbf[A][:])
-
-        def cast_w(A, engines):
-            src = wraw[A][:].rearrange("p t (u c i) -> p u c t i", u=4, i=4)
-            dst = wbf[A][:].rearrange("p (u c i t) -> p u c t i", u=4, i=4, t=4)
-            for half in range(2):
-                if engines[half] == "g":
-                    for u in range(2 * half, 2 * half + 2):
-                        nc.gpsimd.tensor_scalar(
-                            dst[:, u],
-                            src[:, u],
-                            1.0, 0.0, MULT, ADD,
-                        )
-                elif engines[half] == "s":
-                    cast(engines[half], dst[:, 2 * half : 2 * half + 2], src[:, 2 * half : 2 * half + 2])
-
-        def quant_w(A):
-            nc.vector.quantize_mx(out=wq[A][:].bitcast(FP8X4), scales=ws[A][:], in_=wbf[A][:])
+        gather_words(v[1], tab1, idx, 0, CHUNK, 0)
+        gather_words(v[1], tab1, idx, CHUNK, S, 0)
+        load_b(1)
 
         gather_scales(v2s, t2sw, idx2)
         load_w(0)
         load_w(1)
-        cast_b(0, "vggg")
+        b0_dst, b0_src = b_views(0)
+        nc.vector.tensor_copy(b0_dst[:, 0], b0_src[:, 0])
+        for t in range(1, 4):
+            round_gpsimd(b0_dst[:, t], b0_src[:, t])
         load_g(0)
         quant_b(0)
-        gather_half(v2[0], tab2, idx2, 0, 256)
-        gather_half(v2[0], tab2, idx2, 256, 512)
+        gather_words(v2[0], tab2, idx2, 0, CHUNK, 0)
+        gather_words(v2[0], tab2, idx2, CHUNK, HALF, 0)
 
-        banks = [psum.tile([P, 512], F32, name="bank%d" % i) for i in range(8)]
+        banks = [psum.tile([P, HALF], F32, name="bank%d" % i) for i in range(8)]
 
-        def magnitude(A, j0, ab, bank):
-            pp = bank[:].rearrange("p (t n) -> p t n", t=4)
-            for t in range(4):
-                for a in range(2):
-                    o = (2 * a + A) * 4 + t
-                    nc.tensor.matmul_mx(
-                        out=pp[:, t, :],
-                        lhsT=a4p[:, 64 * o : 64 * (o + 1)].bitcast(FP4X4),
-                        lhsT_scale=a4sp[:, 32 * o : 32 * (o + 1)].bitcast(U8),
-                        rhs=v[a][:, j0 : j0 + P].bitcast(FP8X4),
-                        rhs_scale=vs[a][:, j0 // 4 : (j0 + P) // 4].bitcast(U8),
-                        start=(a == 0),
-                        stop=(a == 1),
-                    )
-            nc.scalar.activation(ab.rearrange("p (n t) -> p n t", t=4), pp.rearrange("p t n -> p n t"), ACT.Abs)
+        def magnitudes(first, last):
+            for u in range(first, last):
+                A, j0 = UNITS[u]
+                pp = banks[u % 8][:].rearrange("p (t n) -> p t n", t=4)
+                for t in range(4):
+                    for a in range(2):
+                        o = (2 * a + A) * 4 + t
+                        nc.tensor.matmul_mx(
+                            out=pp[:, t, :],
+                            lhsT=a4p[:, 64 * o : 64 * (o + 1)].bitcast(FP4X4),
+                            lhsT_scale=a4sp[:, 32 * o : 32 * (o + 1)].bitcast(U8),
+                            rhs=v[a][:, j0 : j0 + P].bitcast(FP8X4),
+                            rhs_scale=vs[a][:, j0 // 4 : (j0 + P) // 4].bitcast(U8),
+                            start=(a == 0),
+                            stop=(a == 1),
+                        )
+                nc.scalar.activation(abs_pair[u // 2][:, u % 2, :].rearrange("p (n t) -> p n t", t=4), pp.rearrange("p t n -> p n t"), ACT.Abs)
+
+        def logs(pair):
+            nc.scalar.activation(log_pair[pair][:], abs_pair[pair][:], ACT.Ln, bias=1.0)
 
         def gate(u):
             A, j0 = UNITS[u]
@@ -207,12 +201,17 @@ def tile_list_ad_bid_scores_kernel(tc, tab_words, tab_scales, tab2_words, tab2_s
                     out=qq[:, t, :],
                     lhsT=bq[A][:, P * t : P * (t + 1)].bitcast(FP8X4),
                     lhsT_scale=bs[A][:, P * t : P * (t + 1)],
-                    rhs=v2[j0 // 512][:, j0 % 512 : j0 % 512 + P].bitcast(FP8X4),
+                    rhs=v2[j0 // HALF][:, j0 % HALF : j0 % HALF + P].bitcast(FP8X4),
                     rhs_scale=v2s[:, j0 // 4 : (j0 + P) // 4].bitcast(U8),
                     start=True,
                     stop=True,
                 )
-            nc.vector.tensor_tensor(hb[j0 // 256][:, A, j0 % 256 : j0 % 256 + P, :], log_pair[u // 2][:, u % 2, :].rearrange("p (n t) -> p n t", t=4), qq.rearrange("p t n -> p n t"), MULT)
+            nc.vector.tensor_tensor(
+                hb[j0 // CHUNK][:, A, j0 % CHUNK : j0 % CHUNK + P, :],
+                log_pair[u // 2][:, u % 2, :].rearrange("p (n t) -> p n t", t=4),
+                qq.rearrange("p t n -> p n t"),
+                MULT,
+            )
 
         def quant_h(c):
             nc.vector.quantize_mx(
@@ -221,72 +220,80 @@ def tile_list_ad_bid_scores_kernel(tc, tab_words, tab_scales, tab2_words, tab2_s
                 in_=hb[c][:].rearrange("p a n t -> p (a n t)"),
             )
 
-        def products(yy, n, j0, width):
+        def products(yy, n, c):
             for A in range(2):
                 nc.tensor.matmul_mx(
                     out=yy,
                     lhsT=wq[A][:, P * n : P * (n + 1)].bitcast(FP8X4),
                     lhsT_scale=ws[A][:, P * n : P * (n + 1)],
-                    rhs=hq[j0 // 256][:, A, :].bitcast(FP8X4),
-                    rhs_scale=hs[j0 // 256][:, A, :],
+                    rhs=hq[c][:, A, :].bitcast(FP8X4),
+                    rhs_scale=hs[c][:, A, :],
                     start=(A == 0),
                     stop=(A == 1),
                 )
 
-
-        def scores(j0):
+        def scores(c):
             for pair in range(2):
-                yy = banks[j0 // P + pair][:].rearrange("p (i n) -> p i n", i=2)
+                yy = banks[2 * c + pair][:].rearrange("p (i n) -> p i n", i=2)
                 for i in range(2):
-                    products(yy[:, i, :], 2 * pair + i, j0, 256)
-                nc.scalar.copy(ysb[j0 // 256][:, 2 * pair : 2 * pair + 2, :], yy)
+                    products(yy[:, i, :], 2 * pair + i, c)
+                nc.scalar.copy(ysb[c][:, 2 * pair : 2 * pair + 2, :], yy)
 
-        def bids(c, pairs, slot):
-            for pair in pairs:
-                osb = ht(28 + 2 * pair, [P, 2, 256], F32, "osb%d_%d" % (c, pair)) if c == 2 else st(slot + pair, [P, 2, 256], F32, "osb%d_%d" % (c, pair))
+        def early_scores(pair):
+            for i in range(2):
+                n = 2 * pair + i
+                for c in range(2):
+                    products(banks[n][:, CHUNK * c : CHUNK * (c + 1)], n, c)
+                nc.scalar.copy(ysb[pair][:, i, :], banks[n][:])
+
+        def early_bids(pair):
+            for i in range(2):
+                n = 2 * pair + i
+                osb = st(30 + n, [P, HALF], F32, "osb_early%d" % n)
+                nc.vector.tensor_tensor(osb[:], g[n][:].indirect(idx[:, 0 : HALF // 16]), ysb[pair][:, i, :], MULT)
+                nc.sync.dma_start(out=out[P * n : P * (n + 1), 0:HALF], in_=osb[:])
+
+        def bids(c):
+            cols = slice(CHUNK * c, CHUNK * (c + 1))
+            for pair in range(2):
+                name = "osb%d_%d" % (c, pair)
+                osb = ht(28 + 2 * pair, [P, 2, CHUNK], F32, name) if c == 2 else st(30 + 2 * c + pair, [P, 2, CHUNK], F32, name)
                 for i in range(2):
                     n = 2 * pair + i
                     nc.vector.tensor_tensor(osb[:, i, :], g[n][:].indirect(idx[:, 16 * c : 16 * (c + 1)]), ysb[c][:, n, :], MULT)
                     if c == 3:
-                        nc.sync.dma_start(out=out[P * n : P * (n + 1), 256 * c : 256 * (c + 1)], in_=osb[:, i, :])
-                if c < 3:
-                    nc.sync.dma_start(out=out[2 * P * pair : 2 * P * (pair + 1), 256 * c : 256 * (c + 1)].rearrange("(i p) j -> p i j", i=2), in_=osb[:])
-
-        def magnitudes(first, last):
-            for u in range(first, last):
-                A, j0 = UNITS[u]
-                magnitude(A, j0, abs_pair[u // 2][:, u % 2, :], banks[u % 8])
-
-        def logs(pair):
-            nc.scalar.activation(log_pair[pair][:], abs_pair[pair][:], ACT.Ln, bias=1.0)
+                        nc.sync.dma_start(out=out[P * n : P * (n + 1), cols], in_=osb[:, i, :])
+                if c == 2:
+                    nc.sync.dma_start(out=out[2 * P * pair : 2 * P * (pair + 1), cols].rearrange("(i p) j -> p i j", i=2), in_=osb[:])
 
         magnitudes(0, 3)
         logs(0)
         magnitudes(3, 5)
         logs(1)
-        cast_b(1, "gggg")
+        b1_dst, b1_src = b_views(1)
+        for t in range(4):
+            round_gpsimd(b1_dst[:, t], b1_src[:, t])
         magnitudes(5, 7)
         logs(2)
         magnitudes(7, 8)
         logs(3)
-        gate(0)
-        gate(1)
-        gate(2)
-        gate(3)
+        for u in range(0, 4):
+            gate(u)
         quant_b(1)
-        gather_half(v2[1], tab2, idx2, 512, S)
-        load_g(1)
-        load_g(2)
-        load_g(3)
+        gather_words(v2[1], tab2, idx2, HALF, S, HALF)
+        for n in range(1, 4):
+            load_g(n)
         magnitudes(8, 10)
-        cast_w(0, "gg")
-        gate(4)
-        gate(5)
-        gate(6)
-        gate(7)
+        w0_dst, w0_src = w_views(0)
+        for u in range(4):
+            round_gpsimd(w0_dst[:, u], w0_src[:, u])
+        for u in range(4, 8):
+            gate(u)
         magnitudes(10, 11)
         logs(4)
-        cast_w(1, "ss")
+        w1_dst, w1_src = w_views(1)
+        for u in (0, 2):
+            nc.scalar.copy(w1_dst[:, u : u + 2], w1_src[:, u : u + 2])
         gate(8)
         gate(9)
         quant_h(0)
@@ -295,23 +302,23 @@ def tile_list_ad_bid_scores_kernel(tc, tab_words, tab_scales, tab2_words, tab2_s
         quant_w(1)
         magnitudes(11, 13)
         logs(5)
-        scores(0)
+        early_scores(0)
         gate(10)
         gate(11)
         magnitudes(13, 15)
         logs(6)
-        scores(256)
+        early_scores(1)
         quant_h(2)
         gate(12)
         gate(13)
         magnitudes(15, 16)
         logs(7)
-        scores(512)
+        scores(2)
         gate(14)
         gate(15)
         quant_h(3)
-        scores(768)
-        bids(0, (0, 1), 30)
-        bids(1, (0, 1), 32)
-        bids(2, (0, 1), 34)
-        bids(3, (0, 1), 36)
+        scores(3)
+        early_bids(0)
+        early_bids(1)
+        bids(2)
+        bids(3)

@@ -27,15 +27,11 @@ def tile_list_ad_bid_scores_kernel(tc, tab_words, tab_scales, tab2_words, tab2_s
     nc = tc.nc
     with ExitStack() as ctx:
         keep = ctx.enter_context(tc.tile_pool(name="keep", bufs=1))
-        share = ctx.enter_context(tc.tile_pool(name="share", bufs=1))
         hand = ctx.enter_context(tc.tile_pool(name="hand", bufs=1))
         psum = ctx.enter_context(tc.psum_pool(name="psum", bufs=1))
 
         def kt(shape, dtype, name):
             return keep.tile(shape, dtype, name=name, align_bytes=64)
-
-        def st(slot, shape, dtype, name):
-            return share.tile(shape, dtype, name=name, tag="slot%d" % slot, bufs=1, align_bytes=64)
 
         def ht(kib, shape, dtype, name):
             return hand.tile(shape, dtype, name=name, align_bytes=64, offset=1024 * kib)
@@ -44,67 +40,48 @@ def tile_list_ad_bid_scores_kernel(tc, tab_words, tab_scales, tab2_words, tab2_s
         idx2 = keep.tile([P, S // 16], U16, name="idx2")
         tsw = kt([P, T // 4], I32, "tsw")
         gs = kt([P, S // 4], I32, "gs")
-        v = [kt([P, S], I32, "v%d" % a) for a in range(2)]
-        vs = [kt([P, S // 4], I32, "vs%d" % a) for a in range(2)]
-        v2s = kt([P, S // 4], I32, "v2s")
-        a4p = kt([P, H], I32, "a4p")
+        vs1 = kt([P, S // 4], I32, "vs1")
+        t2sw = kt([P, T // 4], I32, "t2sw")
+        a4sraw = kt([P, 2 * H // 4], I32, "a4sraw")
         a4sp = kt([P, 2 * H // 4], I32, "a4sp")
-        bq = [kt([P, HALF], I32, "bq%d" % A) for A in range(2)]
+        a4raw = kt([P, 2, H // 2], I32, "a4raw")
+        a4lo = [kt([P, 256], I32, "a4lo%d" % a) for a in range(2)]
+        a4hi = kt([P, 2, 256], I32, "a4hi")
+        v = [kt([P, S], I32, "v%d" % a) for a in range(2)]
+        tab2 = kt([P, T], I32, "tab2")
+        braw = [kt([P, 4, HALF], F32, "braw%d" % A) for A in range(2)]
+        bbf0 = [kt([P, 2 * HALF], BF16, "bbf0_%d" % i) for i in range(2)]
+        bbf1g = ht(8, [P, 2 * HALF], BF16, "bbf1g")
+        bs = [kt([P, HALF], U8, "bs%d" % A) for A in range(2)]
         wq = [kt([P, N], I32, "wq%d" % A) for A in range(2)]
         ws = [kt([P, N], U8, "ws%d" % A) for A in range(2)]
-        hq = [kt([P, 2, CHUNK], I32, "hq%d" % c) for c in range(4)]
         hs = [kt([P, 2, CHUNK], U8, "hs%d" % c) for c in range(4)]
         hb = [kt([P, 2, CHUNK, 4], BF16, "hb%d" % c) for c in range(4)]
 
-        tab0 = st(0, [P, T], I32, "tab0")
-        a4raw = ht(8, [P, 2, H // 2], I32, "a4raw")
-        a4sraw = kt([P, 2 * H // 4], I32, "a4sraw")
-        tab1 = ht(0, [P, T], I32, "tab1")
-        t2sw = ht(18, [P, T // 4], I32, "t2sw")
-        tab2 = ht(8, [P, T], I32, "tab2")
-        log_pair = [st(20 + i, [P, 2, HALF], F32, "log%d" % i) for i in range(7)] + [ht(28, [P, 2, HALF], F32, "log7")]
-        bbf = [st(4, [P, 4 * HALF], BF16, "bbf0"), ht(32, [P, 4 * HALF], BF16, "bbf1")]
-        wbf = [ht(34, [P, 4 * N], BF16, "wbf0"), kt([P, 4 * N], BF16, "wbf1")]
-        braw = [st(0, [P, 4, HALF], F32, "braw0"), ht(0, [P, 4, HALF], F32, "braw1")]
-        wraw = [st(6, [P, 4, N], F32, "wraw0"), ht(19, [P, 4, N], F32, "wraw1")]
-        abs_slot = {0: 10, 1: 11, 2: 12, 3: 10, 6: 11, 7: 12}
-        abs_pair = [
-            st(abs_slot[i], [P, 2, HALF], F32, "abs%d" % i) if i in abs_slot else ht(4 * (i - 4), [P, 2, HALF], F32, "abs%d" % i)
-            for i in range(8)
-        ]
-        ysb = [ht(4, [P, 2, HALF], F32, "ysb0"), st(11, [P, 2, HALF], F32, "ysb1"), st(12, [P, 4, CHUNK], F32, "ysb2"), kt([P, 4, CHUNK], F32, "ysb3")]
-        v2 = [kt([P, HALF], I32, "v2a"), ht(32, [P, HALF], I32, "v2b")]
-        bs = [ht(18, [P, HALF], U8, "bs0"), kt([P, HALF], U8, "bs1")]
-        g = [st(0, [P, T], F32, "g0"), ht(8, [P, T], F32, "g1"), st(4, [P, T], F32, "g2"), st(20, [P, T], F32, "g3")]
+        tab = [ht(0, [P, T], I32, "tab0"), kt([P, T], I32, "tab1")]
+        g = [ht(0, [P, T], F32, "g0")] + [kt([P, T], F32, "g%d" % n) for n in range(1, 4)]
+        v2s = kt([P, S // 4], I32, "v2s")
+        log_pair = [ht(10, [P, 2, HALF], F32, "log0")] + [kt([P, 2, HALF], F32, "log%d" % i) for i in range(1, 8)]
+        bq = [kt([P, HALF], I32, "bq0"), ht(10, [P, HALF], I32, "bq1")]
+        bbf1v = ht(12, [P, 2 * HALF], BF16, "bbf1v")
+        v2 = [kt([P, HALF], I32, "v2a"), kt([P, CHUNK], I32, "v2b"), ht(8, [P, CHUNK], I32, "v2c")]
+        wraw = [ht(17, [P, 4, N], F32, "wraw0"), kt([P, 4, N], F32, "wraw1")]
+        abs_at = [25, 29, 33, 25, 29, 33, 37, 41]
+        abs_pair = [ht(abs_at[i], [P, 2, HALF], F32, "abs%d" % i) for i in range(8)]
+        wbf = [ht(13, [P, 4 * N], BF16, "wbf0"), ht(25, [P, 4 * N], BF16, "wbf1")]
+        hq = [ht(17, [P, 2, CHUNK], I32, "hq0"), ht(19, [P, 2, CHUNK], I32, "hq1")] + [kt([P, 2, CHUNK], I32, "hq%d" % c) for c in (2, 3)]
+        ysb = [ht(29, [P, 2, HALF], F32, "ysb0"), ht(33, [P, 2, HALF], F32, "ysb1"), ht(41, [P, 4, CHUNK], F32, "ysb2"), kt([P, 4, CHUNK], F32, "ysb3")]
 
-        nc.vector.memset(tsw[0:16, :], 0)
-        nc.vector.memset(tsw[32:48, :], 0)
-        nc.vector.memset(tsw[64:128, :], 0)
-        nc.gpsimd.memset(a4sraw[:], 0)
+        nc.vector.memset(tsw[:], 0)
+        nc.vector.memset(a4sraw[:], 0)
+        nc.vector.memset(t2sw[:], 0)
+        nc.vector.memset(vs1[96:128, :], 0)
         warm = kt([P, 2], F32, "warm")
         nc.gpsimd.memset(warm[:, 0:1], 1.0)
         nc.scalar.activation(warm[:, 1:2], warm[:, 0:1], ACT.Ln)
-        nc.vector.memset(t2sw[:], 0)
 
-        nc.sync.dma_start(idx[:], offs)
-        rows = tab_scales.rearrange("a (u h r) n -> h (a u) r n", u=2, h=2)
-        for h in range(2):
-            nc.sync.dma_start(out=tsw[32 * h + 16 : 32 * h + 32, :], in_=rows[h].bitcast(I32))
-        for Q in range(4):
-            nc.sync.dma_start(
-                out=a4sraw[32 * Q : 32 * Q + 4, :].rearrange("p (a n) -> p a n", a=2),
-                in_=a4_scales[:, 4 * Q : 4 * Q + 4, :].rearrange("a r n -> r a n").bitcast(I32),
-            )
-        nc.sync.dma_start(out=tab0[:], in_=tab_words[0].rearrange("p t i -> p (t i)").bitcast(I32))
-        nc.sync.dma_start(out=a4raw[:], in_=a4_words.rearrange("a p n -> p a n").bitcast(I32))
-        nc.sync.dma_start(out=tab1[:], in_=tab_words[1].rearrange("p t i -> p (t i)").bitcast(I32))
-        nc.sync.dma_start(idx2[:], offs2)
-
-        def gather_words(dst, window, lst, j0, j1, first):
-            nc.vector.tensor_copy(dst[:, j0 - first : j1 - first].bitcast(U32), window[:].bitcast(U32).indirect(lst[:, j0 // 16 : j1 // 16]))
-
-        def gather_scales(dst, window, lst):
-            nc.vector.tensor_copy(dst[:].bitcast(U8), window[:].bitcast(U8).indirect(lst[:]))
+        def load_words(dst, words):
+            nc.sync.dma_start(out=dst[:], in_=words.rearrange("p t i -> p (t i)").bitcast(I32))
 
         def load_b(A):
             nc.sync.dma_start(out=braw[A][:], in_=b[:, HALF * A : HALF * (A + 1)].rearrange("(p j) r -> p j r", j=4))
@@ -114,79 +91,97 @@ def tile_list_ad_bid_scores_kernel(tc, tab_words, tab_scales, tab2_words, tab2_s
             for t in range(4):
                 nc.sync.dma_start(out=wraw[A][:, t, :], in_=wrows[t])
 
-        def load_g(n):
+        def gather_words(dst, window, lst, j0, j1, first):
+            nc.vector.tensor_copy(dst[:, j0 - first : j1 - first].bitcast(U32), window[:].bitcast(U32).indirect(lst[:, j0 // 16 : j1 // 16]))
+
+        def gather_scales(dst, window, lst):
+            nc.vector.tensor_copy(dst[:].bitcast(U8), window[:].bitcast(U8).indirect(lst[:]))
+
+        nc.sync.dma_start(idx[:], offs)
+        nc.sync.dma_start(idx2[:], offs2)
+        rows = tab_scales.rearrange("a (Q r) n -> r Q a n", r=4)
+        for r in range(4):
+            nc.sync.dma_start(out=tsw[r:P:16, :], in_=rows[r].bitcast(I32))
+        load_words(tab[0], tab_words[0])
+        for Q in range(4):
+            nc.sync.dma_start(
+                out=a4sraw[32 * Q : 32 * Q + 4, :].rearrange("p (a n) -> p a n", a=2),
+                in_=a4_scales[:, 4 * Q : 4 * Q + 4, :].rearrange("a r n -> r a n").bitcast(I32),
+            )
+        load_words(tab[1], tab_words[1])
+        nc.sync.dma_start(out=a4raw[:], in_=a4_words.rearrange("a p n -> p a n").bitcast(I32))
+        gather_scales(gs, tsw, idx)
+        nc.sync.dma_start(out=vs1[0:112, :], in_=gs[16:128, :])
+        vs = [gs, vs1]
+        for Q in range(4):
+            nc.sync.dma_start(out=t2sw[32 * Q : 32 * Q + 4, :], in_=tab2_scales[0, 4 * Q : 4 * Q + 4, :].bitcast(I32))
+        gather_words(v[0], tab[0], idx, 0, S, 0)
+        load_b(0)
+        load_words(tab2, tab2_words[0])
+        load_b(1)
+        load_w(0)
+        load_w(1)
+        for n in range(4):
             nc.sync.dma_start(out=g[n][:], in_=gT[P * n : P * (n + 1), :])
 
         def round_gpsimd(dst, src):
             nc.gpsimd.tensor_scalar(dst, src, 1.0, 0.0, MULT, ADD)
 
-        def b_views(A):
-            src = braw[A][:].rearrange("p j (m t e) -> p t m j e", t=4, e=4)
-            dst = bbf[A][:].rearrange("p (t m e j) -> p t m j e", t=4, e=4, j=4)
-            return dst, src
+        def b_src(A):
+            return braw[A][:].rearrange("p j (m t e) -> p t m j e", t=4, e=4)
+
+        def b_dst(tile):
+            return tile[:].rearrange("p (t m e j) -> p t m j e", m=32, e=4, j=4)
 
         def w_views(A):
             src = wraw[A][:].rearrange("p t (u c i) -> p u c t i", u=4, i=4)
             dst = wbf[A][:].rearrange("p (u c i t) -> p u c t i", u=4, i=4, t=4)
             return dst, src
 
-        def quant_b(A):
-            nc.vector.quantize_mx(out=bq[A][:].bitcast(FP8X4), scales=bs[A][:], in_=bbf[A][:])
+        def quantise(codes, scales, values):
+            nc.vector.quantize_mx(out=codes.bitcast(FP8X4), scales=scales, in_=values)
 
-        def quant_w(A):
-            nc.vector.quantize_mx(out=wq[A][:].bitcast(FP8X4), scales=ws[A][:], in_=wbf[A][:])
-
-        gather_scales(gs, tsw, idx)
-        for u in range(2):
-            for a in range(2):
-                first = 16 + 4 * (2 * a + u)
-                nc.scalar.dma_start(out=vs[a][64 * u : 64 * (u + 1), :], in_=gs[first : first + 64, :])
-        nc.vector.tensor_copy(
-            a4sp[:].rearrange("p (x t m) -> p x m t", x=4, t=4),
-            a4sraw[:].rearrange("p (x m t) -> p x m t", x=4, t=4),
+        nc.scalar.copy(
+            a4sp[:].bitcast(U32).rearrange("p (x t m) -> p x m t", x=4, t=4),
+            a4sraw[:].bitcast(U32).rearrange("p (x m t) -> p x m t", x=4, t=4),
         )
-        gather_words(v[0], tab0, idx, 0, S, 0)
-        load_b(0)
-        for Q in range(4):
-            nc.sync.dma_start(out=t2sw[32 * Q : 32 * Q + 4, :], in_=tab2_scales[0, 4 * Q : 4 * Q + 4, :].bitcast(I32))
-        nc.vector.tensor_copy(
-            a4p[:].rearrange("p (x t m e) -> p x t m e", x=4, t=4, e=2),
-            a4raw[:].rearrange("p a (x m t e) -> p (a x) t m e", x=2, t=4, e=2),
-        )
-        nc.sync.dma_start(out=tab2[:], in_=tab2_words[0].rearrange("p t i -> p (t i)").bitcast(I32))
-        gather_words(v[1], tab1, idx, 0, CHUNK, 0)
-        gather_words(v[1], tab1, idx, CHUNK, S, 0)
-        load_b(1)
+        a4src = a4raw[:].bitcast(U32).rearrange("p a (A m t e) -> p A a t m e", A=2, t=4, e=2)
+        for a in range(2):
+            nc.scalar.copy(a4lo[a][:].bitcast(U32).rearrange("p (t m e) -> p t m e", t=4, e=2), a4src[:, 0, a])
+        nc.scalar.copy(a4hi[:].bitcast(U32).rearrange("p a (t m e) -> p a t m e", t=4, e=2), a4src[:, 1])
 
+        gather_words(v[1], tab[1], idx, 0, CHUNK, 0)
+        gather_words(v[1], tab[1], idx, CHUNK, S, 0)
         gather_scales(v2s, t2sw, idx2)
-        load_w(0)
-        load_w(1)
-        b0_dst, b0_src = b_views(0)
-        nc.vector.tensor_copy(b0_dst[:, 0], b0_src[:, 0])
-        for t in range(1, 4):
-            round_gpsimd(b0_dst[:, t], b0_src[:, t])
-        load_g(0)
-        quant_b(0)
+        for i in range(2):
+            nc.vector.tensor_copy(b_dst(bbf0[i]), b_src(0)[:, 2 * i : 2 * i + 2])
         gather_words(v2[0], tab2, idx2, 0, CHUNK, 0)
+        for i in range(2):
+            quantise(bq[0][:, 256 * i : 256 * (i + 1)], bs[0][:, 256 * i : 256 * (i + 1)], bbf0[i][:])
         gather_words(v2[0], tab2, idx2, CHUNK, HALF, 0)
+        for t in range(2):
+            round_gpsimd(b_dst(bbf1g)[:, t], b_src(1)[:, t])
 
         banks = [psum.tile([P, HALF], F32, name="bank%d" % i) for i in range(8)]
+
+        score_bank = [(7, 2), (3, 4), (5, 6), (7, 2)]
 
         def magnitudes(first, last):
             for u in range(first, last):
                 A, j0 = UNITS[u]
-                pp = banks[u % 8][:].rearrange("p (t n) -> p t n", t=4)
-                for t in range(4):
-                    for a in range(2):
+                pp = banks[u % 7][:].rearrange("p (t n) -> p t n", t=4)
+                for a in range(2):
+                    words = a4hi[:, a, :] if A else a4lo[a][:]
+                    for t in range(4):
                         o = (2 * a + A) * 4 + t
                         nc.tensor.matmul_mx(
                             out=pp[:, t, :],
-                            lhsT=a4p[:, 64 * o : 64 * (o + 1)].bitcast(FP4X4),
+                            lhsT=words[:, 64 * t : 64 * (t + 1)].bitcast(FP4X4),
                             lhsT_scale=a4sp[:, 32 * o : 32 * (o + 1)].bitcast(U8),
                             rhs=v[a][:, j0 : j0 + P].bitcast(FP8X4),
                             rhs_scale=vs[a][:, j0 // 4 : (j0 + P) // 4].bitcast(U8),
-                            start=(a == 0),
-                            stop=(a == 1),
+                            start=(a == 0 and t == 0),
+                            stop=(a == 1 and t == 3),
                         )
                 nc.scalar.activation(abs_pair[u // 2][:, u % 2, :].rearrange("p (n t) -> p n t", t=4), pp.rearrange("p t n -> p n t"), ACT.Abs)
 
@@ -195,13 +190,13 @@ def tile_list_ad_bid_scores_kernel(tc, tab_words, tab_scales, tab2_words, tab2_s
 
         def gate(u):
             A, j0 = UNITS[u]
-            qq = banks[u % 8][:].rearrange("p (t n) -> p t n", t=4)
+            qq = banks[u % 7][:].rearrange("p (t n) -> p t n", t=4)
             for t in range(4):
                 nc.tensor.matmul_mx(
                     out=qq[:, t, :],
                     lhsT=bq[A][:, P * t : P * (t + 1)].bitcast(FP8X4),
                     lhsT_scale=bs[A][:, P * t : P * (t + 1)],
-                    rhs=v2[j0 // HALF][:, j0 % HALF : j0 % HALF + P].bitcast(FP8X4),
+                    rhs=(v2[0][:, j0 : j0 + P] if j0 < HALF else v2[j0 // CHUNK - 1][:, j0 % CHUNK : j0 % CHUNK + P]).bitcast(FP8X4),
                     rhs_scale=v2s[:, j0 // 4 : (j0 + P) // 4].bitcast(U8),
                     start=True,
                     stop=True,
@@ -213,12 +208,11 @@ def tile_list_ad_bid_scores_kernel(tc, tab_words, tab_scales, tab2_words, tab2_s
                 MULT,
             )
 
+        def quant_w(A):
+            quantise(wq[A][:], ws[A][:], wbf[A][:])
+
         def quant_h(c):
-            nc.vector.quantize_mx(
-                out=hq[c][:].rearrange("p a n -> p (a n)").bitcast(FP8X4),
-                scales=hs[c][:].rearrange("p a n -> p (a n)"),
-                in_=hb[c][:].rearrange("p a n t -> p (a n t)"),
-            )
+            quantise(hq[c][:].rearrange("p a n -> p (a n)"), hs[c][:].rearrange("p a n -> p (a n)"), hb[c][:].rearrange("p a n t -> p (a n t)"))
 
         def products(yy, n, c):
             for A in range(2):
@@ -234,62 +228,55 @@ def tile_list_ad_bid_scores_kernel(tc, tab_words, tab_scales, tab2_words, tab2_s
 
         def scores(c):
             for pair in range(2):
-                yy = banks[2 * c + pair][:].rearrange("p (i n) -> p i n", i=2)
+                yy = banks[score_bank[c][pair]][:].rearrange("p (i n) -> p i n", i=2)
                 for i in range(2):
                     products(yy[:, i, :], 2 * pair + i, c)
                 nc.scalar.copy(ysb[c][:, 2 * pair : 2 * pair + 2, :], yy)
 
-        def early_scores(pair):
-            for i in range(2):
-                n = 2 * pair + i
-                for c in range(2):
-                    products(banks[n][:, CHUNK * c : CHUNK * (c + 1)], n, c)
-                nc.scalar.copy(ysb[pair][:, i, :], banks[n][:])
+        def early_scores(n):
+            bank = banks[score_bank[n // 2][n % 2]]
+            for c in range(2):
+                products(bank[:, CHUNK * c : CHUNK * (c + 1)], n, c)
+            nc.scalar.copy(ysb[n // 2][:, n % 2, :], bank[:])
 
-        def early_bids(pair):
-            for i in range(2):
-                n = 2 * pair + i
-                osb = st(30 + n, [P, HALF], F32, "osb_early%d" % n)
-                nc.vector.tensor_tensor(osb[:], g[n][:].indirect(idx[:, 0 : HALF // 16]), ysb[pair][:, i, :], MULT)
-                nc.sync.dma_start(out=out[P * n : P * (n + 1), 0:HALF], in_=osb[:])
+        def early_bid(n):
+            osb = kt([P, HALF], F32, "osb_early%d" % n)
+            nc.vector.tensor_tensor(osb[:], g[n][:].indirect(idx[:, 0 : HALF // 16]), ysb[n // 2][:, n % 2, :], MULT)
+            nc.sync.dma_start(out=out[P * n : P * (n + 1), 0:HALF], in_=osb[:])
 
-        def bids(c):
+        osb2 = [kt([P, 2, CHUNK], F32, "osb2_%d" % pair) for pair in range(2)]
+        osb3 = [kt([P, CHUNK], F32, "osb3_%d" % n) for n in range(4)]
+
+        def bid(c, n):
             cols = slice(CHUNK * c, CHUNK * (c + 1))
-            for pair in range(2):
-                name = "osb%d_%d" % (c, pair)
-                osb = ht(28 + 2 * pair, [P, 2, CHUNK], F32, name) if c == 2 else st(30 + 2 * c + pair, [P, 2, CHUNK], F32, name)
-                for i in range(2):
-                    n = 2 * pair + i
-                    nc.vector.tensor_tensor(osb[:, i, :], g[n][:].indirect(idx[:, 16 * c : 16 * (c + 1)]), ysb[c][:, n, :], MULT)
-                    if c == 3:
-                        nc.sync.dma_start(out=out[P * n : P * (n + 1), cols], in_=osb[:, i, :])
-                if c == 2:
-                    nc.sync.dma_start(out=out[2 * P * pair : 2 * P * (pair + 1), cols].rearrange("(i p) j -> p i j", i=2), in_=osb[:])
+            dst = osb2[n // 2][:, n % 2, :] if c == 2 else osb3[n][:]
+            nc.vector.tensor_tensor(dst, g[n][:].indirect(idx[:, 16 * c : 16 * (c + 1)]), ysb[c][:, n, :], MULT)
+            if c == 3:
+                nc.sync.dma_start(out=out[P * n : P * (n + 1), cols], in_=dst)
+            elif n % 2:
+                nc.sync.dma_start(out=out[P * (n - 1) : P * (n + 1), cols].rearrange("(i p) j -> p i j", i=2), in_=osb2[n // 2][:])
 
         magnitudes(0, 3)
         logs(0)
         magnitudes(3, 5)
         logs(1)
-        b1_dst, b1_src = b_views(1)
-        for t in range(4):
-            round_gpsimd(b1_dst[:, t], b1_src[:, t])
         magnitudes(5, 7)
         logs(2)
-        magnitudes(7, 8)
-        logs(3)
         for u in range(0, 4):
             gate(u)
-        quant_b(1)
-        gather_words(v2[1], tab2, idx2, HALF, S, HALF)
-        for n in range(1, 4):
-            load_g(n)
-        magnitudes(8, 10)
+        magnitudes(7, 9)
+        logs(3)
+        gather_words(v2[1], tab2, idx2, HALF, HALF + CHUNK, HALF)
+        nc.vector.tensor_copy(b_dst(bbf1v), b_src(1)[:, 2:4])
+        quantise(bq[1][:, 0:256], bs[1][:, 0:256], bbf1g[:])
+        quantise(bq[1][:, 256:512], bs[1][:, 256:512], bbf1v[:])
+        gather_words(v2[2], tab2, idx2, HALF + CHUNK, S, HALF + CHUNK)
         w0_dst, w0_src = w_views(0)
         for u in range(4):
             round_gpsimd(w0_dst[:, u], w0_src[:, u])
+        magnitudes(9, 11)
         for u in range(4, 8):
             gate(u)
-        magnitudes(10, 11)
         logs(4)
         w1_dst, w1_src = w_views(1)
         for u in (0, 2):
@@ -297,28 +284,34 @@ def tile_list_ad_bid_scores_kernel(tc, tab_words, tab_scales, tab2_words, tab2_s
         gate(8)
         gate(9)
         quant_h(0)
-        quant_w(0)
         quant_h(1)
+        quant_w(0)
         quant_w(1)
         magnitudes(11, 13)
         logs(5)
         early_scores(0)
+        early_scores(1)
         gate(10)
         gate(11)
+        early_bid(0)
+        quant_h(2)
         magnitudes(13, 15)
         logs(6)
-        early_scores(1)
-        quant_h(2)
+        early_scores(2)
         gate(12)
         gate(13)
         magnitudes(15, 16)
+        early_scores(3)
         logs(7)
         scores(2)
         gate(14)
         gate(15)
+        bid(2, 0)
         quant_h(3)
         scores(3)
-        early_bids(0)
-        early_bids(1)
-        bids(2)
-        bids(3)
+        for n in range(1, 4):
+            early_bid(n)
+        for n in range(1, 4):
+            bid(2, n)
+        for n in range(4):
+            bid(3, n)

@@ -44,14 +44,14 @@ def tile_list_ad_bid_scores_kernel(tc, tab_words, tab_scales, tab2_words, tab2_s
         t2sw = kt([P, T // 4], I32, "t2sw")
         a4sraw = kt([P, 2 * H // 4], I32, "a4sraw")
         a4sp = kt([P, 2 * H // 4], I32, "a4sp")
-        a4raw = kt([P, 2, H // 2], I32, "a4raw")
+        a4raw = [kt([P, 2, H // 4], I32, "a4raw%d" % A) for A in range(2)]
         a4lo = [kt([P, 256], I32, "a4lo%d" % a) for a in range(2)]
         a4hi = kt([P, 2, 256], I32, "a4hi")
         v = [kt([P, S], I32, "v%d" % a) for a in range(2)]
         tab2 = kt([P, T], I32, "tab2")
         braw = [kt([P, 4, HALF], F32, "braw%d" % A) for A in range(2)]
         bbf0 = [kt([P, 2 * HALF], BF16, "bbf0_%d" % i) for i in range(2)]
-        bbf1g = ht(8, [P, 2 * HALF], BF16, "bbf1g")
+        bbf1g = ht(45, [P, 3 * HALF], BF16, "bbf1g")
         bs = [kt([P, HALF], U8, "bs%d" % A) for A in range(2)]
         wq = [kt([P, N], I32, "wq%d" % A) for A in range(2)]
         ws = [kt([P, N], U8, "ws%d" % A) for A in range(2)]
@@ -63,12 +63,12 @@ def tile_list_ad_bid_scores_kernel(tc, tab_words, tab_scales, tab2_words, tab2_s
         v2s = kt([P, S // 4], I32, "v2s")
         log_pair = [ht(10, [P, 2, HALF], F32, "log0")] + [kt([P, 2, HALF], F32, "log%d" % i) for i in range(1, 8)]
         bq = [kt([P, HALF], I32, "bq0"), ht(10, [P, HALF], I32, "bq1")]
-        bbf1v = ht(12, [P, 2 * HALF], BF16, "bbf1v")
-        v2 = [kt([P, HALF], I32, "v2a"), kt([P, CHUNK], I32, "v2b"), ht(8, [P, CHUNK], I32, "v2c")]
+        bbf1s = ht(48, [P, HALF], BF16, "bbf1s")
+        v2 = [kt([P, HALF], I32, "v2a"), kt([P, CHUNK], I32, "v2b"), ht(45, [P, CHUNK], I32, "v2c")]
         wraw = [ht(17, [P, 4, N], F32, "wraw0"), kt([P, 4, N], F32, "wraw1")]
-        abs_at = [25, 29, 33, 25, 29, 33, 37, 41]
+        abs_at = [25, 48, 33, 25, 29, 33, 37, 41]
         abs_pair = [ht(abs_at[i], [P, 2, HALF], F32, "abs%d" % i) for i in range(8)]
-        wbf = [ht(13, [P, 4 * N], BF16, "wbf0"), ht(25, [P, 4 * N], BF16, "wbf1")]
+        wbf = [ht(48, [P, 4 * N], BF16, "wbf0"), ht(25, [P, 4 * N], BF16, "wbf1")]
         hq = [ht(17, [P, 2, CHUNK], I32, "hq0"), ht(19, [P, 2, CHUNK], I32, "hq1")] + [kt([P, 2, CHUNK], I32, "hq%d" % c) for c in (2, 3)]
         ysb = [ht(29, [P, 2, HALF], F32, "ysb0"), ht(33, [P, 2, HALF], F32, "ysb1"), ht(41, [P, 4, CHUNK], F32, "ysb2"), kt([P, 4, CHUNK], F32, "ysb3")]
 
@@ -109,7 +109,9 @@ def tile_list_ad_bid_scores_kernel(tc, tab_words, tab_scales, tab2_words, tab2_s
                 in_=a4_scales[:, 4 * Q : 4 * Q + 4, :].rearrange("a r n -> r a n").bitcast(I32),
             )
         load_words(tab[1], tab_words[1])
-        nc.sync.dma_start(out=a4raw[:], in_=a4_words.rearrange("a p n -> p a n").bitcast(I32))
+        a4halves = a4_words.rearrange("a p (A n) -> A p a n", A=2)
+        for A in range(2):
+            nc.sync.dma_start(out=a4raw[A][:], in_=a4halves[A].bitcast(I32))
         gather_scales(gs, tsw, idx)
         nc.sync.dma_start(out=vs1[0:112, :], in_=gs[16:128, :])
         vs = [gs, vs1]
@@ -145,10 +147,10 @@ def tile_list_ad_bid_scores_kernel(tc, tab_words, tab_scales, tab2_words, tab2_s
             a4sp[:].bitcast(U32).rearrange("p (x t m) -> p x m t", x=4, t=4),
             a4sraw[:].bitcast(U32).rearrange("p (x m t) -> p x m t", x=4, t=4),
         )
-        a4src = a4raw[:].bitcast(U32).rearrange("p a (A m t e) -> p A a t m e", A=2, t=4, e=2)
+        a4src = [a4raw[A][:].bitcast(U32).rearrange("p a (m t e) -> p a t m e", t=4, e=2) for A in range(2)]
         for a in range(2):
-            nc.scalar.copy(a4lo[a][:].bitcast(U32).rearrange("p (t m e) -> p t m e", t=4, e=2), a4src[:, 0, a])
-        nc.scalar.copy(a4hi[:].bitcast(U32).rearrange("p a (t m e) -> p a t m e", t=4, e=2), a4src[:, 1])
+            nc.scalar.copy(a4lo[a][:].bitcast(U32).rearrange("p (t m e) -> p t m e", t=4, e=2), a4src[0][:, a])
+        nc.gpsimd.tensor_copy(a4hi[:].bitcast(U32).rearrange("p a (t m e) -> p a t m e", t=4, e=2), a4src[1])
 
         gather_words(v[1], tab[1], idx, 0, CHUNK, 0)
         gather_words(v[1], tab[1], idx, CHUNK, S, 0)
@@ -159,7 +161,7 @@ def tile_list_ad_bid_scores_kernel(tc, tab_words, tab_scales, tab2_words, tab2_s
         for i in range(2):
             quantise(bq[0][:, 256 * i : 256 * (i + 1)], bs[0][:, 256 * i : 256 * (i + 1)], bbf0[i][:])
         gather_words(v2[0], tab2, idx2, CHUNK, HALF, 0)
-        for t in range(2):
+        for t in range(3):
             round_gpsimd(b_dst(bbf1g)[:, t], b_src(1)[:, t])
 
         banks = [psum.tile([P, HALF], F32, name="bank%d" % i) for i in range(8)]
@@ -262,14 +264,14 @@ def tile_list_ad_bid_scores_kernel(tc, tab_words, tab_scales, tab2_words, tab2_s
         logs(1)
         magnitudes(5, 7)
         logs(2)
+        nc.scalar.copy(b_dst(bbf1s)[:, 0], b_src(1)[:, 3])
         for u in range(0, 4):
             gate(u)
         magnitudes(7, 9)
         logs(3)
         gather_words(v2[1], tab2, idx2, HALF, HALF + CHUNK, HALF)
-        nc.vector.tensor_copy(b_dst(bbf1v), b_src(1)[:, 2:4])
-        quantise(bq[1][:, 0:256], bs[1][:, 0:256], bbf1g[:])
-        quantise(bq[1][:, 256:512], bs[1][:, 256:512], bbf1v[:])
+        quantise(bq[1][:, 0:384], bs[1][:, 0:384], bbf1g[:])
+        quantise(bq[1][:, 384:512], bs[1][:, 384:512], bbf1s[:])
         gather_words(v2[2], tab2, idx2, HALF + CHUNK, S, HALF + CHUNK)
         w0_dst, w0_src = w_views(0)
         for u in range(4):
@@ -279,16 +281,17 @@ def tile_list_ad_bid_scores_kernel(tc, tab_words, tab_scales, tab2_words, tab2_s
             gate(u)
         logs(4)
         w1_dst, w1_src = w_views(1)
-        for u in (0, 2):
-            nc.scalar.copy(w1_dst[:, u : u + 2], w1_src[:, u : u + 2])
+        nc.scalar.copy(w1_dst[:, 0:2], w1_src[:, 0:2])
+        magnitudes(11, 12)
+        nc.scalar.copy(w1_dst[:, 2:4], w1_src[:, 2:4])
+        logs(5)
         gate(8)
         gate(9)
         quant_h(0)
         quant_h(1)
         quant_w(0)
         quant_w(1)
-        magnitudes(11, 13)
-        logs(5)
+        magnitudes(12, 13)
         early_scores(0)
         early_scores(1)
         gate(10)
@@ -297,20 +300,21 @@ def tile_list_ad_bid_scores_kernel(tc, tab_words, tab_scales, tab2_words, tab2_s
         quant_h(2)
         magnitudes(13, 15)
         logs(6)
-        early_scores(2)
         gate(12)
         gate(13)
         magnitudes(15, 16)
-        early_scores(3)
+        early_scores(2)
         logs(7)
+        early_bid(1)
+        early_bid(2)
         scores(2)
+        early_scores(3)
         gate(14)
         gate(15)
         bid(2, 0)
         quant_h(3)
         scores(3)
-        for n in range(1, 4):
-            early_bid(n)
+        early_bid(3)
         for n in range(1, 4):
             bid(2, n)
         for n in range(4):

@@ -20,7 +20,7 @@ ADD = mybir.AluOpType.add
 P = 128
 HALF = 512
 CHUNK = 256
-UNITS = [(A, P * j) for A in range(2) for j in range(4)] + [(A, P * j) for j in range(4, 8) for A in range(2)]
+UNITS = [(A, P * j) for A in range(2) for j in range(5)] + [(A, P * j) for j in range(5, 8) for A in range(2)]
 
 
 def tile_list_ad_bid_scores_kernel(tc, tab_words, tab_scales, tab2_words, tab2_scales, offs, offs2, a4_words, a4_scales, b, w, gT, out):
@@ -61,7 +61,7 @@ def tile_list_ad_bid_scores_kernel(tc, tab_words, tab_scales, tab2_words, tab2_s
         tab = [ht(0, [P, T], I32, "tab0"), kt([P, T], I32, "tab1")]
         g = [ht(0, [P, T], F32, "g0")] + [kt([P, T], F32, "g%d" % n) for n in range(1, 4)]
         v2s = kt([P, S // 4], I32, "v2s")
-        log_pair = [ht(10, [P, 2, HALF], F32, "log0")] + [kt([P, 2, HALF], F32, "log%d" % i) for i in range(1, 8)]
+        log_pair = [ht(10, [P, 2, HALF], F32, "log1") if i == 1 else kt([P, 2, HALF], F32, "log%d" % i) for i in range(8)]
         bq = [kt([P, HALF], I32, "bq0"), ht(10, [P, HALF], I32, "bq1")]
         bbf1s = ht(48, [P, HALF], BF16, "bbf1s")
         v2 = [kt([P, HALF], I32, "v2a"), kt([P, CHUNK], I32, "v2b"), ht(45, [P, CHUNK], I32, "v2c")]
@@ -265,11 +265,13 @@ def tile_list_ad_bid_scores_kernel(tc, tab_words, tab_scales, tab2_words, tab2_s
         magnitudes(5, 7)
         logs(2)
         nc.scalar.copy(b_dst(bbf1s)[:, 0], b_src(1)[:, 3])
-        for u in range(0, 4):
+        gate(0)
+        gate(1)
+        gather_words(v2[1], tab2, idx2, HALF, HALF + CHUNK, HALF)
+        for u in range(2, 5):
             gate(u)
         magnitudes(7, 9)
         logs(3)
-        gather_words(v2[1], tab2, idx2, HALF, HALF + CHUNK, HALF)
         quantise(bq[1][:, 0:384], bs[1][:, 0:384], bbf1g[:])
         quantise(bq[1][:, 384:512], bs[1][:, 384:512], bbf1s[:])
         gather_words(v2[2], tab2, idx2, HALF + CHUNK, S, HALF + CHUNK)
@@ -277,7 +279,7 @@ def tile_list_ad_bid_scores_kernel(tc, tab_words, tab_scales, tab2_words, tab2_s
         for u in range(4):
             round_gpsimd(w0_dst[:, u], w0_src[:, u])
         magnitudes(9, 11)
-        for u in range(4, 8):
+        for u in range(5, 8):
             gate(u)
         logs(4)
         w1_dst, w1_src = w_views(1)

@@ -20,6 +20,8 @@ ADD = mybir.AluOpType.add
 P = 128
 HALF = 512
 CHUNK = 256
+UNIT_BANKS = 7
+GPSIMD_SLICES = 3
 UNITS = [(A, P * j) for A in range(2) for j in range(5)] + [(A, P * j) for j in range(5, 8) for A in range(2)]
 
 
@@ -51,7 +53,7 @@ def tile_list_ad_bid_scores_kernel(tc, tab_words, tab_scales, tab2_words, tab2_s
         tab2 = kt([P, T], I32, "tab2")
         braw = [kt([P, 4, HALF], F32, "braw%d" % A) for A in range(2)]
         bbf0 = [kt([P, 2 * HALF], BF16, "bbf0_%d" % i) for i in range(2)]
-        bbf1g = ht(45, [P, 3 * HALF], BF16, "bbf1g")
+        bbf1g = ht(45, [P, GPSIMD_SLICES * HALF], BF16, "bbf1g")
         bs = [kt([P, HALF], U8, "bs%d" % A) for A in range(2)]
         wq = [kt([P, N], I32, "wq%d" % A) for A in range(2)]
         ws = [kt([P, N], U8, "ws%d" % A) for A in range(2)]
@@ -161,7 +163,7 @@ def tile_list_ad_bid_scores_kernel(tc, tab_words, tab_scales, tab2_words, tab2_s
         for i in range(2):
             quantise(bq[0][:, 256 * i : 256 * (i + 1)], bs[0][:, 256 * i : 256 * (i + 1)], bbf0[i][:])
         gather_words(v2[0], tab2, idx2, CHUNK, HALF, 0)
-        for t in range(3):
+        for t in range(GPSIMD_SLICES):
             round_gpsimd(b_dst(bbf1g)[:, t], b_src(1)[:, t])
 
         banks = [psum.tile([P, HALF], F32, name="bank%d" % i) for i in range(8)]
@@ -171,7 +173,7 @@ def tile_list_ad_bid_scores_kernel(tc, tab_words, tab_scales, tab2_words, tab2_s
         def magnitudes(first, last):
             for u in range(first, last):
                 A, j0 = UNITS[u]
-                pp = banks[u % 7][:].rearrange("p (t n) -> p t n", t=4)
+                pp = banks[u % UNIT_BANKS][:].rearrange("p (t n) -> p t n", t=4)
                 for a in range(2):
                     words = a4hi[:, a, :] if A else a4lo[a][:]
                     for t in range(4):
@@ -192,13 +194,14 @@ def tile_list_ad_bid_scores_kernel(tc, tab_words, tab_scales, tab2_words, tab2_s
 
         def gate(u):
             A, j0 = UNITS[u]
-            qq = banks[u % 7][:].rearrange("p (t n) -> p t n", t=4)
+            qq = banks[u % UNIT_BANKS][:].rearrange("p (t n) -> p t n", t=4)
+            words = v2[0][:, j0 : j0 + P] if j0 < HALF else v2[j0 // CHUNK - 1][:, j0 % CHUNK : j0 % CHUNK + P]
             for t in range(4):
                 nc.tensor.matmul_mx(
                     out=qq[:, t, :],
                     lhsT=bq[A][:, P * t : P * (t + 1)].bitcast(FP8X4),
                     lhsT_scale=bs[A][:, P * t : P * (t + 1)],
-                    rhs=(v2[0][:, j0 : j0 + P] if j0 < HALF else v2[j0 // CHUNK - 1][:, j0 % CHUNK : j0 % CHUNK + P]).bitcast(FP8X4),
+                    rhs=words.bitcast(FP8X4),
                     rhs_scale=v2s[:, j0 // 4 : (j0 + P) // 4].bitcast(U8),
                     start=True,
                     stop=True,
@@ -216,29 +219,30 @@ def tile_list_ad_bid_scores_kernel(tc, tab_words, tab_scales, tab2_words, tab2_s
         def quant_h(c):
             quantise(hq[c][:].rearrange("p a n -> p (a n)"), hs[c][:].rearrange("p a n -> p (a n)"), hb[c][:].rearrange("p a n t -> p (a n t)"))
 
-        def products(yy, n, c):
-            for A in range(2):
-                nc.tensor.matmul_mx(
-                    out=yy,
-                    lhsT=wq[A][:, P * n : P * (n + 1)].bitcast(FP8X4),
-                    lhsT_scale=ws[A][:, P * n : P * (n + 1)],
-                    rhs=hq[c][:, A, :].bitcast(FP8X4),
-                    rhs_scale=hs[c][:, A, :],
-                    start=(A == 0),
-                    stop=(A == 1),
-                )
+        def product(yy, n, c, A, start, stop):
+            nc.tensor.matmul_mx(
+                out=yy,
+                lhsT=wq[A][:, P * n : P * (n + 1)].bitcast(FP8X4),
+                lhsT_scale=ws[A][:, P * n : P * (n + 1)],
+                rhs=hq[c][:, A, :].bitcast(FP8X4),
+                rhs_scale=hs[c][:, A, :],
+                start=start,
+                stop=stop,
+            )
 
         def scores(c):
             for pair in range(2):
                 yy = banks[score_bank[c][pair]][:].rearrange("p (i n) -> p i n", i=2)
                 for i in range(2):
-                    products(yy[:, i, :], 2 * pair + i, c)
+                    for A in range(2):
+                        product(yy[:, i, :], 2 * pair + i, c, A, A == 0, A == 1)
                 nc.scalar.copy(ysb[c][:, 2 * pair : 2 * pair + 2, :], yy)
 
         def early_scores(n):
             bank = banks[score_bank[n // 2][n % 2]]
-            for c in range(2):
-                products(bank[:, CHUNK * c : CHUNK * (c + 1)], n, c)
+            for A in range(2):
+                for c in range(2):
+                    product(bank[:, CHUNK * c : CHUNK * (c + 1)], n, c, A, A == 0 and c == 0, A == 1 and c == 1)
             nc.scalar.copy(ysb[n // 2][:, n % 2, :], bank[:])
 
         def early_bid(n):
@@ -264,7 +268,7 @@ def tile_list_ad_bid_scores_kernel(tc, tab_words, tab_scales, tab2_words, tab2_s
         logs(1)
         magnitudes(5, 7)
         logs(2)
-        nc.scalar.copy(b_dst(bbf1s)[:, 0], b_src(1)[:, 3])
+        nc.scalar.copy(b_dst(bbf1s)[:, 0], b_src(1)[:, GPSIMD_SLICES])
         gate(0)
         gate(1)
         gather_words(v2[1], tab2, idx2, HALF, HALF + CHUNK, HALF)
@@ -272,8 +276,9 @@ def tile_list_ad_bid_scores_kernel(tc, tab_words, tab_scales, tab2_words, tab2_s
             gate(u)
         magnitudes(7, 9)
         logs(3)
-        quantise(bq[1][:, 0:384], bs[1][:, 0:384], bbf1g[:])
-        quantise(bq[1][:, 384:512], bs[1][:, 384:512], bbf1s[:])
+        split = P * GPSIMD_SLICES
+        quantise(bq[1][:, 0:split], bs[1][:, 0:split], bbf1g[:])
+        quantise(bq[1][:, split:HALF], bs[1][:, split:HALF], bbf1s[:])
         gather_words(v2[2], tab2, idx2, HALF + CHUNK, S, HALF + CHUNK)
         w0_dst, w0_src = w_views(0)
         for u in range(4):
@@ -293,14 +298,14 @@ def tile_list_ad_bid_scores_kernel(tc, tab_words, tab_scales, tab2_words, tab2_s
         quant_h(1)
         quant_w(0)
         quant_w(1)
-        magnitudes(12, 13)
+        magnitudes(12, 14)
         early_scores(0)
         early_scores(1)
         gate(10)
         gate(11)
         early_bid(0)
         quant_h(2)
-        magnitudes(13, 15)
+        magnitudes(14, 15)
         logs(6)
         gate(12)
         gate(13)

from contextlib import ExitStack

import concourse.mybir as mybir

K, C, H, N, T, S = 1024, 512, 1024, 512, 2048, 1024
FLOPS = 2 * S * (K * H + C * H + H * N)

F32 = mybir.dt.float32
BF16 = mybir.dt.bfloat16
I32 = mybir.dt.int32
U32 = mybir.dt.uint32
U16 = mybir.dt.uint16
U8 = mybir.dt.uint8
FP8X4 = mybir.dt.float8_e4m3fn_x4
FP4X4 = mybir.dt.float4_e2m1fn_x4
ACT = mybir.ActivationFunctionType
MULT = mybir.AluOpType.mult
ADD = mybir.AluOpType.add

P = 128
HALF = 512
CHUNK = 256
UNIT_BANKS = 7
GPSIMD_SLICES = 3
UNITS = [(A, P * j) for A in range(2) for j in range(5)] + [(A, P * j) for j in range(5, 8) for A in range(2)]


def tile_list_ad_bid_scores_kernel(tc, tab_words, tab_scales, tab2_words, tab2_scales, offs, offs2, a4_words, a4_scales, b, w, gT, out):
    nc = tc.nc
    with ExitStack() as ctx:
        keep = ctx.enter_context(tc.tile_pool(name="keep", bufs=1))
        hand = ctx.enter_context(tc.tile_pool(name="hand", bufs=1))
        psum = ctx.enter_context(tc.psum_pool(name="psum", bufs=1))

        def kt(shape, dtype, name):
            return keep.tile(shape, dtype, name=name, align_bytes=64)

        def ht(kib, shape, dtype, name):
            return hand.tile(shape, dtype, name=name, align_bytes=64, offset=1024 * kib)

        idx = keep.tile([P, S // 16], U16, name="idx")
        idx2 = keep.tile([P, S // 16], U16, name="idx2")
        tsw = kt([P, T // 4], I32, "tsw")
        gs = kt([P, S // 4], I32, "gs")
        vs1 = kt([P, S // 4], I32, "vs1")
        t2sw = kt([P, T // 4], I32, "t2sw")
        a4sraw = kt([P, 2 * H // 4], I32, "a4sraw")
        a4sp = kt([P, 2 * H // 4], I32, "a4sp")
        a4raw = [kt([P, 2, H // 4], I32, "a4raw%d" % A) for A in range(2)]
        a4lo = [kt([P, 256], I32, "a4lo%d" % a) for a in range(2)]
        a4hi = kt([P, 2, 256], I32, "a4hi")
        v = [kt([P, S], I32, "v%d" % a) for a in range(2)]
        tab2 = kt([P, T], I32, "tab2")
        braw = [kt([P, 4, HALF], F32, "braw%d" % A) for A in range(2)]
        bbf0 = [kt([P, 2 * HALF], BF16, "bbf0_%d" % i) for i in range(2)]
        bbf1g = ht(45, [P, GPSIMD_SLICES * HALF], BF16, "bbf1g")
        bs = [kt([P, HALF], U8, "bs%d" % A) for A in range(2)]
        wq = [kt([P, N], I32, "wq%d" % A) for A in range(2)]
        ws = [kt([P, N], U8, "ws%d" % A) for A in range(2)]
        hs = [kt([P, 2, CHUNK], U8, "hs%d" % c) for c in range(4)]
        hb = [kt([P, 2, CHUNK, 4], BF16, "hb%d" % c) for c in range(4)]

        tab = [ht(0, [P, T], I32, "tab0"), kt([P, T], I32, "tab1")]
        g = [ht(0, [P, T], F32, "g0")] + [kt([P, T], F32, "g%d" % n) for n in range(1, 4)]
        v2s = kt([P, S // 4], I32, "v2s")
        log_pair = [ht(10, [P, 2, HALF], F32, "log1") if i == 1 else kt([P, 2, HALF], F32, "log%d" % i) for i in range(8)]
        bq = [kt([P, HALF], I32, "bq0"), ht(10, [P, HALF], I32, "bq1")]
        bbf1s = ht(48, [P, HALF], BF16, "bbf1s")
        v2 = [kt([P, HALF], I32, "v2a"), kt([P, CHUNK], I32, "v2b"), ht(45, [P, CHUNK], I32, "v2c")]
        wraw = [ht(17, [P, 4, N], F32, "wraw0"), kt([P, 4, N], F32, "wraw1")]
        abs_at = [25, 48, 33, 25, 29, 33, 37, 41]
        abs_pair = [ht(abs_at[i], [P, 2, HALF], F32, "abs%d" % i) for i in range(8)]
        wbf = [ht(48, [P, 4 * N], BF16, "wbf0"), ht(25, [P, 4 * N], BF16, "wbf1")]
        hq = [ht(17, [P, 2, CHUNK], I32, "hq0"), ht(19, [P, 2, CHUNK], I32, "hq1")] + [kt([P, 2, CHUNK], I32, "hq%d" % c) for c in (2, 3)]
        ysb = [ht(29, [P, 2, HALF], F32, "ysb0"), ht(33, [P, 2, HALF], F32, "ysb1"), ht(41, [P, 4, CHUNK], F32, "ysb2"), kt([P, 4, CHUNK], F32, "ysb3")]

        nc.vector.memset(tsw[:], 0)
        nc.vector.memset(a4sraw[:], 0)
        nc.vector.memset(t2sw[:], 0)
        nc.vector.memset(vs1[96:128, :], 0)
        warm = kt([P, 2], F32, "warm")
        nc.gpsimd.memset(warm[:, 0:1], 1.0)
        nc.scalar.activation(warm[:, 1:2], warm[:, 0:1], ACT.Ln)

        def load_words(dst, words):
            nc.sync.dma_start(out=dst[:], in_=words.rearrange("p t i -> p (t i)").bitcast(I32))

        def load_b(A):
            nc.sync.dma_start(out=braw[A][:], in_=b[:, HALF * A : HALF * (A + 1)].rearrange("(p j) r -> p j r", j=4))

        def load_w(A):
            wrows = w[HALF * A : HALF * (A + 1), :].rearrange("(m t e) n -> t m e n", t=4, e=4)
            for t in range(4):
                nc.sync.dma_start(out=wraw[A][:, t, :], in_=wrows[t])

        def gather_words(dst, window, lst, j0, j1, first):
            nc.vector.tensor_copy(dst[:, j0 - first : j1 - first].bitcast(U32), window[:].bitcast(U32).indirect(lst[:, j0 // 16 : j1 // 16]))

        def gather_scales(dst, window, lst):
            nc.vector.tensor_copy(dst[:].bitcast(U8), window[:].bitcast(U8).indirect(lst[:]))

        nc.sync.dma_start(idx[:], offs)
        nc.sync.dma_start(idx2[:], offs2)
        rows = tab_scales.rearrange("a (Q r) n -> r Q a n", r=4)
        for r in range(4):
            nc.sync.dma_start(out=tsw[r:P:16, :], in_=rows[r].bitcast(I32))
        load_words(tab[0], tab_words[0])
        for Q in range(4):
            nc.sync.dma_start(
                out=a4sraw[32 * Q : 32 * Q + 4, :].rearrange("p (a n) -> p a n", a=2),
                in_=a4_scales[:, 4 * Q : 4 * Q + 4, :].rearrange("a r n -> r a n").bitcast(I32),
            )
        load_words(tab[1], tab_words[1])
        a4halves = a4_words.rearrange("a p (A n) -> A p a n", A=2)
        for A in range(2):
            nc.sync.dma_start(out=a4raw[A][:], in_=a4halves[A].bitcast(I32))
        gather_scales(gs, tsw, idx)
        nc.sync.dma_start(out=vs1[0:112, :], in_=gs[16:128, :])
        vs = [gs, vs1]
        for Q in range(4):
            nc.sync.dma_start(out=t2sw[32 * Q : 32 * Q + 4, :], in_=tab2_scales[0, 4 * Q : 4 * Q + 4, :].bitcast(I32))
        gather_words(v[0], tab[0], idx, 0, S, 0)
        load_b(0)
        load_words(tab2, tab2_words[0])
        load_b(1)
        load_w(0)
        load_w(1)
        for n in range(4):
            nc.sync.dma_start(out=g[n][:], in_=gT[P * n : P * (n + 1), :])

        def round_gpsimd(dst, src):
            nc.gpsimd.tensor_scalar(dst, src, 1.0, 0.0, MULT, ADD)

        def b_src(A):
            return braw[A][:].rearrange("p j (m t e) -> p t m j e", t=4, e=4)

        def b_dst(tile):
            return tile[:].rearrange("p (t m e j) -> p t m j e", m=32, e=4, j=4)

        def w_views(A):
            src = wraw[A][:].rearrange("p t (u c i) -> p u c t i", u=4, i=4)
            dst = wbf[A][:].rearrange("p (u c i t) -> p u c t i", u=4, i=4, t=4)
            return dst, src

        def quantise(codes, scales, values):
            nc.vector.quantize_mx(out=codes.bitcast(FP8X4), scales=scales, in_=values)

        nc.scalar.copy(
            a4sp[:].bitcast(U32).rearrange("p (x t m) -> p x m t", x=4, t=4),
            a4sraw[:].bitcast(U32).rearrange("p (x m t) -> p x m t", x=4, t=4),
        )
        a4src = [a4raw[A][:].bitcast(U32).rearrange("p a (m t e) -> p a t m e", t=4, e=2) for A in range(2)]
        for a in range(2):
            nc.scalar.copy(a4lo[a][:].bitcast(U32).rearrange("p (t m e) -> p t m e", t=4, e=2), a4src[0][:, a])
        nc.gpsimd.tensor_copy(a4hi[:].bitcast(U32).rearrange("p a (t m e) -> p a t m e", t=4, e=2), a4src[1])

        gather_words(v[1], tab[1], idx, 0, CHUNK, 0)
        gather_words(v[1], tab[1], idx, CHUNK, S, 0)
        gather_scales(v2s, t2sw, idx2)
        for i in range(2):
            nc.vector.tensor_copy(b_dst(bbf0[i]), b_src(0)[:, 2 * i : 2 * i + 2])
        gather_words(v2[0], tab2, idx2, 0, CHUNK, 0)
        for i in range(2):
            quantise(bq[0][:, 256 * i : 256 * (i + 1)], bs[0][:, 256 * i : 256 * (i + 1)], bbf0[i][:])
        gather_words(v2[0], tab2, idx2, CHUNK, HALF, 0)
        for t in range(GPSIMD_SLICES):
            round_gpsimd(b_dst(bbf1g)[:, t], b_src(1)[:, t])

        banks = [psum.tile([P, HALF], F32, name="bank%d" % i) for i in range(8)]

        score_bank = [(7, 2), (3, 4), (5, 6), (7, 2)]

        def magnitudes(first, last):
            for u in range(first, last):
                A, j0 = UNITS[u]
                pp = banks[u % UNIT_BANKS][:].rearrange("p (t n) -> p t n", t=4)
                for a in range(2):
                    words = a4hi[:, a, :] if A else a4lo[a][:]
                    for t in range(4):
                        o = (2 * a + A) * 4 + t
                        nc.tensor.matmul_mx(
                            out=pp[:, t, :],
                            lhsT=words[:, 64 * t : 64 * (t + 1)].bitcast(FP4X4),
                            lhsT_scale=a4sp[:, 32 * o : 32 * (o + 1)].bitcast(U8),
                            rhs=v[a][:, j0 : j0 + P].bitcast(FP8X4),
                            rhs_scale=vs[a][:, j0 // 4 : (j0 + P) // 4].bitcast(U8),
                            start=(a == 0 and t == 0),
                            stop=(a == 1 and t == 3),
                        )
                nc.scalar.activation(abs_pair[u // 2][:, u % 2, :].rearrange("p (n t) -> p n t", t=4), pp.rearrange("p t n -> p n t"), ACT.Abs)

        def logs(pair):
            nc.scalar.activation(log_pair[pair][:], abs_pair[pair][:], ACT.Ln, bias=1.0)

        def gate(u):
            A, j0 = UNITS[u]
            qq = banks[u % UNIT_BANKS][:].rearrange("p (t n) -> p t n", t=4)
            words = v2[0][:, j0 : j0 + P] if j0 < HALF else v2[j0 // CHUNK - 1][:, j0 % CHUNK : j0 % CHUNK + P]
            for t in range(4):
                nc.tensor.matmul_mx(
                    out=qq[:, t, :],
                    lhsT=bq[A][:, P * t : P * (t + 1)].bitcast(FP8X4),
                    lhsT_scale=bs[A][:, P * t : P * (t + 1)],
                    rhs=words.bitcast(FP8X4),
                    rhs_scale=v2s[:, j0 // 4 : (j0 + P) // 4].bitcast(U8),
                    start=True,
                    stop=True,
                )
            nc.vector.tensor_tensor(
                hb[j0 // CHUNK][:, A, j0 % CHUNK : j0 % CHUNK + P, :],
                log_pair[u // 2][:, u % 2, :].rearrange("p (n t) -> p n t", t=4),
                qq.rearrange("p t n -> p n t"),
                MULT,
            )

        def quant_w(A):
            quantise(wq[A][:], ws[A][:], wbf[A][:])

        def quant_h(c):
            quantise(hq[c][:].rearrange("p a n -> p (a n)"), hs[c][:].rearrange("p a n -> p (a n)"), hb[c][:].rearrange("p a n t -> p (a n t)"))

        def product(yy, n, c, A, start, stop):
            nc.tensor.matmul_mx(
                out=yy,
                lhsT=wq[A][:, P * n : P * (n + 1)].bitcast(FP8X4),
                lhsT_scale=ws[A][:, P * n : P * (n + 1)],
                rhs=hq[c][:, A, :].bitcast(FP8X4),
                rhs_scale=hs[c][:, A, :],
                start=start,
                stop=stop,
            )

        def scores(c):
            for pair in range(2):
                yy = banks[score_bank[c][pair]][:].rearrange("p (i n) -> p i n", i=2)
                for i in range(2):
                    for A in range(2):
                        product(yy[:, i, :], 2 * pair + i, c, A, A == 0, A == 1)
                nc.scalar.copy(ysb[c][:, 2 * pair : 2 * pair + 2, :], yy)

        def early_scores(n):
            bank = banks[score_bank[n // 2][n % 2]]
            for A in range(2):
                for c in range(2):
                    product(bank[:, CHUNK * c : CHUNK * (c + 1)], n, c, A, A == 0 and c == 0, A == 1 and c == 1)
            nc.scalar.copy(ysb[n // 2][:, n % 2, :], bank[:])

        def early_bid(n):
            osb = kt([P, HALF], F32, "osb_early%d" % n)
            nc.vector.tensor_tensor(osb[:], g[n][:].indirect(idx[:, 0 : HALF // 16]), ysb[n // 2][:, n % 2, :], MULT)
            nc.sync.dma_start(out=out[P * n : P * (n + 1), 0:HALF], in_=osb[:])

        osb2 = [kt([P, 2, CHUNK], F32, "osb2_%d" % pair) for pair in range(2)]
        osb3 = [kt([P, CHUNK], F32, "osb3_%d" % n) for n in range(4)]

        def bid(c, n):
            cols = slice(CHUNK * c, CHUNK * (c + 1))
            dst = osb2[n // 2][:, n % 2, :] if c == 2 else osb3[n][:]
            nc.vector.tensor_tensor(dst, g[n][:].indirect(idx[:, 16 * c : 16 * (c + 1)]), ysb[c][:, n, :], MULT)
            if c == 3:
                nc.sync.dma_start(out=out[P * n : P * (n + 1), cols], in_=dst)
            elif n % 2:
                nc.sync.dma_start(out=out[P * (n - 1) : P * (n + 1), cols].rearrange("(i p) j -> p i j", i=2), in_=osb2[n // 2][:])

        magnitudes(0, 3)
        logs(0)
        magnitudes(3, 5)
        logs(1)
        magnitudes(5, 7)
        logs(2)
        nc.scalar.copy(b_dst(bbf1s)[:, 0], b_src(1)[:, GPSIMD_SLICES])
        gate(0)
        gate(1)
        gather_words(v2[1], tab2, idx2, HALF, HALF + CHUNK, HALF)
        for u in range(2, 5):
            gate(u)
        magnitudes(7, 9)
        logs(3)
        split = P * GPSIMD_SLICES
        quantise(bq[1][:, 0:split], bs[1][:, 0:split], bbf1g[:])
        quantise(bq[1][:, split:HALF], bs[1][:, split:HALF], bbf1s[:])
        gather_words(v2[2], tab2, idx2, HALF + CHUNK, S, HALF + CHUNK)
        w0_dst, w0_src = w_views(0)
        for u in range(4):
            round_gpsimd(w0_dst[:, u], w0_src[:, u])
        magnitudes(9, 11)
        for u in range(5, 8):
            gate(u)
        logs(4)
        w1_dst, w1_src = w_views(1)
        nc.scalar.copy(w1_dst[:, 0:2], w1_src[:, 0:2])
        magnitudes(11, 12)
        nc.scalar.copy(w1_dst[:, 2:4], w1_src[:, 2:4])
        logs(5)
        gate(8)
        gate(9)
        quant_h(0)
        quant_h(1)
        quant_w(0)
        quant_w(1)
        magnitudes(12, 14)
        early_scores(0)
        early_scores(1)
        gate(10)
        gate(11)
        early_bid(0)
        quant_h(2)
        magnitudes(14, 15)
        logs(6)
        gate(12)
        gate(13)
        magnitudes(15, 16)
        early_scores(2)
        logs(7)
        early_bid(1)
        early_bid(2)
        scores(2)
        early_scores(3)
        gate(14)
        gate(15)
        bid(2, 0)
        quant_h(3)
        scores(3)
        early_bid(3)
        for n in range(1, 4):
            bid(2, n)
        for n in range(4):
            bid(3, n)
